import numpy as np
import ml_dtypes


def mxq(x, axis, fmt="e4m3"):
    dtype, down = {"e4m3": (ml_dtypes.float8_e4m3fn, 7), "e5m2": (ml_dtypes.float8_e5m2, 14)}[fmt]
    v = np.moveaxis(np.asarray(x, np.float32).astype(ml_dtypes.bfloat16).astype(np.float64), axis, -1)
    blocks = v.reshape(v.shape[:-1] + (-1, 32))
    amax = np.abs(blocks).max(-1, keepdims=True)
    byte = np.maximum(np.where(amax > 0, np.frexp(amax)[1] - 1 + 127, 0) - down, 1)
    scale = np.exp2(byte - 127.0)
    codes = (blocks / scale).astype(np.float32).astype(dtype).astype(np.float64)
    return np.moveaxis((codes * scale).reshape(v.shape), -1, axis)


WIDE = False


def mx_kscale(k):
    if not WIDE:
        return np.ones(k)
    levels = np.array([24, -24, 12, -12, 0])
    if k % 512:
        return np.exp2(np.random.permutation(np.resize(levels, k // 32))).repeat(32)
    a = np.empty((k // 512, 16))
    for p in range(k // 512):
        a[p, :8] = np.random.permutation(np.resize(levels, 8))
        for g in range(8):
            far = levels[np.abs(levels - a[p, g]) >= 10]
            a[p, g + 8] = far[np.random.randint(len(far))]
    return np.exp2(a.ravel()).repeat(32)


def f64(x):
    return np.asarray(x).astype(np.float64)


def striped(idx):
    return np.tile(idx.reshape(-1, 16).T, (8, 1)).astype(np.uint16)


def unstriped(offs):
    return offs[:16].T.reshape(-1).astype(np.int64)


E2M1 = np.array([0.0, 0.5, 1.0, 1.5, 2.0, 3.0, 4.0, 6.0, -0.0, -0.5, -1.0, -1.5, -2.0, -3.0, -4.0, -6.0])


def pack_weight(w, fmt):
    k, n = w.shape
    w = f64(np.asarray(w, np.float32).astype(ml_dtypes.bfloat16)).reshape(k // 32, 32, n)
    amax = np.abs(w).max(1)
    if fmt == "e4m3":
        byte = np.frexp(amax)[1] - 1 + 127 - 7
    else:
        mant, ex = np.frexp(amax / 6.0)
        byte = np.where(mant > 0.5, ex, ex - 1) + 127
    byte = np.clip(np.where(amax > 0, byte, 1), 1, 254)
    scaled = (w * np.exp2(127.0 - byte)[:, None, :]).reshape(k, n).astype(np.float32)
    by_word = np.ascontiguousarray(scaled.reshape(k // 512, 128, 4, n).transpose(0, 1, 3, 2))
    if fmt == "e4m3":
        words = by_word.astype(ml_dtypes.float8_e4m3fn).view(np.uint8)
    else:
        c = by_word.astype(ml_dtypes.float4_e2m1fn).view(np.uint8) & 0xF
        words = (c[..., 0::2] | (c[..., 1::2] << 4)).reshape(k // 512, 128, 2 * n)
    return np.ascontiguousarray(words), np.ascontiguousarray(byte.astype(np.uint8).reshape(k // 512, 16, n))


def unpack_weight(words, scales, fmt):
    g, _, n = scales.shape
    words = np.ascontiguousarray(words).reshape(g, 128, n, -1)
    if fmt == "e4m3":
        vals = words.view(ml_dtypes.float8_e4m3fn).astype(np.float64)
    else:
        nib = np.empty((g, 128, n, 4), np.uint8)
        nib[..., 0::2] = words & 0xF
        nib[..., 1::2] = words >> 4
        vals = E2M1[nib]
    vals = vals * np.repeat(np.exp2(scales.astype(np.float64) - 127.0), 8, axis=1)[..., None]
    return vals.transpose(0, 1, 3, 2).reshape(g * 512, n)


def pack_table4(v):
    words, scales = pack_weight(v, "e2m1")
    g, t = words.shape[0] // 2, v.shape[1]
    return np.ascontiguousarray(words.reshape(g, 2, 128, t, 2).transpose(0, 2, 3, 1, 4).reshape(g, 128, t, 4)), scales


def unpack_table4(words, scales):
    g, _, t, _ = words.shape
    return unpack_weight(words.reshape(g, 128, t, 2, 2).transpose(0, 3, 1, 2, 4).reshape(2 * g, 128, 2 * t), scales, "e2m1")


def sigm(f):
    return 1.0 / (1.0 + np.exp(-np.maximum(f, -700.0)))


K, L, R, N, T, J = 1024, 512, 512, 512, 4096, 1024


def setup_inputs():
    n = np.random.standard_normal
    s = mx_kscale(K)[:, None]
    s2 = mx_kscale(L)[:, None]
    u = mx_kscale(R)[:, None]
    p_tab = pack_table4(n((K, T)) * s)
    p_tab2 = pack_weight(n((L, T)) * s2, "e4m3")
    p_wer = pack_weight(n((K, R)) / np.sqrt(K) / s * u.T, "e2m1")
    p_wei = pack_weight(n((K, R)) / np.sqrt(K) / s * u.T, "e2m1")
    return {
        "tab_words": p_tab[0],
        "tab_scales": p_tab[1],
        "tab2_words": p_tab2[0],
        "tab2_scales": p_tab2[1],
        "wer_words": p_wer[0],
        "wer_scales": p_wer[1],
        "wei_words": p_wei[0],
        "wei_scales": p_wei[1],
        "wrr": (n((L, R)) / np.sqrt(L) / s2).astype(np.float32),
        "wri": (n((L, R)) / np.sqrt(L) / s2).astype(np.float32),
        "nr": (n((R, N)) / np.sqrt(R) / u).astype(np.float32),
        "ni": (n((R, N)) / np.sqrt(R) / u).astype(np.float32),
        "offs": striped(np.random.permutation(T)[:J]),
        "offs2": striped(np.random.permutation(T)[:J]),
    }


def reference(tab_words, tab_scales, tab2_words, tab2_scales, wer_words, wer_scales, wei_words, wei_scales, wrr, wri, nr, ni, offs, offs2):
    idx = unstriped(offs)
    idx2 = unstriped(offs2)
    tab_ = unpack_table4(tab_words, tab_scales)[:, idx]
    tab2_ = unpack_weight(tab2_words, tab2_scales, "e4m3")[:, idx2]
    wer_ = unpack_weight(wer_words, wer_scales, "e2m1")
    aer = wer_.T @ tab_
    wei_ = unpack_weight(wei_words, wei_scales, "e2m1")
    aei = wei_.T @ tab_
    wrr_ = mxq(f64(wrr), 0, "e4m3")
    arr = wrr_.T @ tab2_
    wri_ = mxq(f64(wri), 0, "e4m3")
    ari = wri_.T @ tab2_
    hr = aer * arr - aei * ari
    hi = aer * ari + aei * arr
    hr_ = mxq(hr, 0, "e4m3")
    hi_ = mxq(hi, 0, "e4m3")
    nr_ = mxq(f64(nr), 0, "e4m3")
    ni_ = mxq(f64(ni), 0, "e4m3")
    y = nr_.T @ hr_ + ni_.T @ hi_
    return sigm(y)

@@ -1,0 +1,266 @@
+from contextlib import ExitStack
+
+import concourse.mybir as mybir
+
+K, L, R, N, T, J = 1024, 512, 512, 512, 4096, 1024
+FLOPS = 2 * J * (2 * K * R + 2 * L * R + 2 * R * N)
+
+F32 = mybir.dt.float32
+BF16 = mybir.dt.bfloat16
+I32 = mybir.dt.int32
+U32 = mybir.dt.uint32
+U16 = mybir.dt.uint16
+U8 = mybir.dt.uint8
+FP8X4 = mybir.dt.float8_e4m3fn_x4
+FP4X4 = mybir.dt.float4_e2m1fn_x4
+MULT = mybir.AluOpType.mult
+ADD = mybir.AluOpType.add
+SIGMOID = mybir.ActivationFunctionType.Sigmoid
+
+P = 128
+CH = 128
+NCH = J // CH
+HALF = 512
+TAB_ROW, TAB2_ROW = 112, 48
+TAB_S, W_S, PLANE_BYTES = 0, 2 * J, 2 * J + 4 * R
+TAB2_K = 4
+
+
+def tile_list_ckg_sig_kernel(
+    tc, tab_words, tab_scales, tab2_words, tab2_scales, wer_words, wer_scales, wei_words, wei_scales,
+    wrr, wri, nr, ni, offs, offs2, out
+):
+    nc = tc.nc
+    with ExitStack() as ctx:
+        keep = ctx.enter_context(tc.tile_pool(name="keep", bufs=1))
+        ring = ctx.enter_context(tc.tile_pool(name="ring", bufs=3))
+        ps_ab = ctx.enter_context(tc.psum_pool(name="ps_ab", bufs=2))
+        ps_cd = ctx.enter_context(tc.psum_pool(name="ps_cd", bufs=4))
+        ps_y = ctx.enter_context(tc.psum_pool(name="ps_y", bufs=2))
+
+        idx = keep.tile([P, J // 16], U16, name="idx")
+        idx2 = keep.tile([P, J // 16], U16, name="idx2")
+        tab_sw = keep.tile([P, 2, T // 4], I32, name="tab_sw", align_bytes=64)
+        tab2_sw = keep.tile([P, T // 4], I32, name="tab2_sw", tag="then_wri", align_bytes=64)
+        w_sraw = keep.tile([P, 2, 2, R // 4], I32, name="w_sraw", tag="then_tab2", align_bytes=64)
+        tab_w = keep.tile([P, T], I32, name="tab_w", align_bytes=64)
+        wer_raw = keep.tile([P, 2, R // 2], I32, name="wer_raw", align_bytes=64)
+        wei_raw = keep.tile([P, 2, R // 2], I32, name="wei_raw", align_bytes=64)
+        wrr_raw = keep.tile([P, 4, R], F32, name="wrr_raw", align_bytes=64)
+        planes = keep.tile([P, PLANE_BYTES // 4], I32, name="planes", align_bytes=64)
+        plane2 = keep.tile([P, J // 4], I32, name="plane2", align_bytes=64)
+
+        nc.sync.dma_start(idx[:], offs)
+        nc.sync.dma_start(tab_sw[TAB_ROW:P], tab_scales.bitcast(I32).rearrange("a q c -> q a c"))
+        nc.sync.dma_start(w_sraw[TAB_ROW:P, 0], wer_scales.bitcast(I32).rearrange("a q c -> q a c"))
+        nc.sync.dma_start(w_sraw[TAB_ROW:P, 1], wei_scales.bitcast(I32).rearrange("a q c -> q a c"))
+        nc.sync.dma_start(idx2[:], offs2)
+        nc.sync.dma_start(tab2_sw[TAB2_ROW : TAB2_ROW + 16, :], tab2_scales.bitcast(I32)[0])
+        nc.sync.dma_start(wer_raw[:], wer_words.bitcast(I32).rearrange("a p c -> p a c"))
+        nc.sync.dma_start(wei_raw[:], wei_words.bitcast(I32).rearrange("a p c -> p a c"))
+        nc.sync.dma_start(tab_w[:], tab_words[0].rearrange("p t b -> p (t b)").bitcast(I32))
+        nc.sync.dma_start(wrr_raw[:], wrr.rearrange("(p j) c -> p j c", j=4))
+
+        nc.vector.memset(tab_sw[0:TAB_ROW], 0)
+        nc.vector.memset(w_sraw[96:TAB_ROW], 0)
+        nc.gpsimd.memset(planes[:], 0)
+        nc.gpsimd.memset(tab2_sw[0:TAB2_ROW, :], 0)
+        nc.gpsimd.memset(tab2_sw[64:P, :], 0)
+        nc.gpsimd.memset(plane2[:], 0)
+
+        tab_sg = keep.tile([P, 2, J], U8, name="tab_sg", align_bytes=64)
+        for a in range(2):
+            nc.vector.tensor_copy(tab_sg[:, a, :], tab_sw[:, a, :].bitcast(U8).indirect(idx[:]))
+
+        joined = keep.tile([P, PLANE_BYTES // 4], I32, name="joined", align_bytes=64)
+        nc.vector.tensor_copy(joined[96:P, 0 : W_S // 4], tab_sg[96:P].rearrange("p a j -> p (a j)").bitcast(I32))
+        nc.vector.tensor_copy(
+            joined[96:P, W_S // 4 :].rearrange("p (s t g e) -> p s t g e", s=4, t=4, e=2),
+            w_sraw[96:P].rearrange("p w a (g t e) -> p (w a) t g e", t=4, e=2),
+        )
+        for r in range(4):
+            nc.sync.dma_start(planes[r:P:32, :], joined[TAB_ROW + r : P : 4, :])
+        planes8 = planes[:].bitcast(U8)
+        plane28 = plane2[TAB2_K:P, :].bitcast(U8)
+
+        tab_g = [
+            keep.tile([P, HALF], U32, name="tab_g0", tag="then_tab2_sg", align_bytes=64),
+            keep.tile([P, HALF], U32, name="tab_g1", align_bytes=64),
+        ]
+        tab_p = keep.tile([P, 2, 2 * J], U8, name="tab_p", align_bytes=64)
+        tab2_g = keep.tile([P, J], U32, name="tab2_g", align_bytes=64)
+        w_p = keep.tile([P, 2, 2, R // 2], I32, name="w_p", align_bytes=64)
+
+        def gather_tab(h):
+            nc.vector.tensor_copy(tab_g[h][:], tab_w[:].bitcast(U32).indirect(idx[:, h * 32 : (h + 1) * 32]))
+
+        def part_tab(h):
+            cols = slice(h * HALF, (h + 1) * HALF)
+            nc.vector.tensor_copy(
+                tab_p[:].bitcast(U16)[:, :, cols],
+                tab_g[h][:].bitcast(U16).rearrange("p (j a) -> p a j", a=2),
+            )
+
+        def gather_tab2(h):
+            cols = slice(h * HALF, (h + 1) * HALF)
+            nc.vector.tensor_copy(tab2_g[:, cols], tab2_w[:].bitcast(U32).indirect(idx2[:, h * 32 : (h + 1) * 32]))
+
+        def order_columns(w, raw):
+            nc.vector.tensor_copy(
+                w_p[:, w].rearrange("p a (t g e) -> p a t g e", t=4, e=4),
+                raw[:].rearrange("p a (g t e) -> p a t g e", t=4, e=4),
+            )
+
+        order_columns(0, wer_raw)
+        order_columns(1, wei_raw)
+        tab2_w = keep.tile([P, T], I32, name="tab2_w", tag="then_tab2", align_bytes=64)
+        nc.sync.dma_start(tab2_w[:], tab2_words[0].rearrange("p t b -> p (t b)").bitcast(I32))
+        gather_tab(0)
+        part_tab(0)
+        tab2_sg = keep.tile([P, J], U8, name="tab2_sg", tag="then_tab2_sg", align_bytes=64)
+        nc.vector.tensor_copy(tab2_sg[:], tab2_sw[:].bitcast(U8).indirect(idx2[:]))
+        for r in range(4):
+            nc.sync.dma_start(plane2[TAB2_K + r : P : 32, :], tab2_sg[TAB2_ROW + r : 64 : 4, :].bitcast(I32))
+        gather_tab(1)
+
+        def cast_rel(raw, name, on_scalar, tag):
+            grouped = keep.tile([P, 4, P, 4], BF16, name=name, tag=tag, align_bytes=64)
+            for t in range(4):
+                dst = grouped[:, t].rearrange("p (g i) j -> p g i j", i=8)
+                src = raw[:].rearrange("p j (g t i) -> p t g i j", t=4, i=8)[:, t]
+                if t < on_scalar:
+                    nc.scalar.copy(dst, src)
+                else:
+                    nc.gpsimd.tensor_scalar(dst, src, 1.0, 0.0, MULT, ADD)
+            return grouped
+
+        def quant(grouped, name):
+            codes = keep.tile([P, 512], U32, name=name + "_c", align_bytes=64)
+            scales = keep.tile([P, 512], U8, name=name + "_s", align_bytes=64)
+            nc.vector.quantize_mx(out=codes[:].bitcast(FP8X4), scales=scales[:], in_=grouped)
+            return codes, scales
+
+        wrr_g = cast_rel(wrr_raw, "wrr_g", 4, "then_n")
+        part_tab(1)
+        wrr_q = quant(wrr_g[:].rearrange("p t m j -> p (t m j)"), "wrr")
+
+        wri_raw = keep.tile([P, 4, R], F32, name="wri_raw", tag="then_wri", align_bytes=64)
+        nc.sync.dma_start(wri_raw[:], wri.rearrange("(p j) c -> p j c", j=4))
+        n_raw = keep.tile([P, 2, 4, N], F32, name="n_raw", tag="then_n", align_bytes=64)
+        for w, src in enumerate((nr, ni)):
+            for t in range(4):
+                nc.sync.dma_start(n_raw[:, w, t, :], src.rearrange("(g t i) n -> t g i n", t=4, i=8)[t])
+
+        ab = {}
+        xs = {}
+        ys = {}
+        hs = {}
+
+        def entity(c):
+            ab[c] = ring.tile([P, 2, CH, 4], F32, name="ab")
+            for w in range(2):
+                bank = ps_ab.tile([P, 4, CH], F32, name="bank_ab")
+                for t in range(4):
+                    for a in range(2):
+                        nc.tensor.matmul_mx(
+                            out=bank[:, t, :],
+                            lhsT=w_p[:, w, a, 64 * t : 64 * (t + 1)].bitcast(U8).bitcast(FP4X4),
+                            lhsT_scale=planes8[:, W_S + R * (2 * w + a) + P * t : W_S + R * (2 * w + a) + P * (t + 1)],
+                            rhs=tab_p[:, a, 2 * CH * c : 2 * CH * (c + 1)].bitcast(FP4X4),
+                            rhs_scale=planes8[:, J * a + CH * c : J * a + CH * (c + 1)],
+                            start=(a == 0),
+                            stop=(a == 1),
+                        )
+                nc.scalar.copy(ab[c][:, w], bank[:].rearrange("p t j -> p j t"))
+
+        def relation(c, wq):
+            codes, scales = wq
+            bank = ps_cd.tile([P, 4, CH], F32, name="bank_cd")
+            for t in range(4):
+                nc.tensor.matmul_mx(
+                    out=bank[:, t, :],
+                    lhsT=codes[:, P * t : P * (t + 1)].bitcast(FP8X4),
+                    lhsT_scale=scales[:, P * t : P * (t + 1)],
+                    rhs=tab2_g[:, CH * c : CH * (c + 1)].bitcast(FP8X4),
+                    rhs_scale=plane28[:, CH * c : CH * (c + 1)],
+                    start=True,
+                    stop=True,
+                )
+            return bank[:].rearrange("p t j -> p j t")
+
+        def times_arr(c):
+            arr = relation(c, wrr_q)
+            if c in (2, 4, 5):
+                x = keep.tile([P, 2, CH, 4], F32, name="x%d" % c, tag="then_x%d" % c, align_bytes=64)
+            else:
+                x = ring.tile([P, 2, CH, 4], F32, name="x")
+            nc.vector.tensor_tensor(x[:, 0], ab[c][:, 0], arr, MULT)
+            nc.vector.tensor_tensor(x[:, 1], ab[c][:, 1], arr, MULT)
+            xs[c] = x
+
+        def times_ari(c, wri_q):
+            ari = relation(c, wri_q)
+            y = ring.tile([P, 2, CH, 4], F32, name="y")
+            nc.vector.scalar_tensor_tensor(y[:, 0], ab[c][:, 1], -1.0, ari, MULT, MULT)
+            nc.vector.tensor_tensor(y[:, 1], ab[c][:, 0], ari, MULT)
+            ys[c] = y
+
+        def add(c):
+            h = ring.tile([P, 2 * CH * 4], BF16, name="h", bufs=5, align_bytes=64)
+            eng = nc.vector if c == NCH - 1 else nc.gpsimd
+            eng.tensor_tensor(
+                h[:], xs[c][:].rearrange("p w j t -> p (w j t)"), ys[c][:].rearrange("p w j t -> p (w j t)"), ADD
+            )
+            hs[c] = h
+
+        def score(c, n_q):
+            codes = ring.tile([P, 2 * CH], U32, name="h_c", align_bytes=64)
+            scales = ring.tile([P, 2 * CH], U8, name="h_s", align_bytes=64)
+            nc.vector.quantize_mx(out=codes[:].bitcast(FP8X4), scales=scales[:], in_=hs[c][:])
+            bank = ps_y.tile([P, 4, CH], F32, name="bank_y")
+            for m in range(4):
+                for w in range(2):
+                    nc.tensor.matmul_mx(
+                        out=bank[:, m, :],
+                        lhsT=n_q[w][0][:, P * m : P * (m + 1)].bitcast(FP8X4),
+                        lhsT_scale=n_q[w][1][:, P * m : P * (m + 1)],
+                        rhs=codes[:, CH * w : CH * (w + 1)].bitcast(FP8X4),
+                        rhs_scale=scales[:, CH * w : CH * (w + 1)],
+                        start=(w == 0),
+                        stop=(w == 1),
+                    )
+            res = ring.tile([P, 4, CH], F32, name="res")
+            nc.scalar.activation(res[:], bank[:], SIGMOID)
+            nc.sync.dma_start(out[:, CH * c : CH * (c + 1)].rearrange("(m p) j -> p m j", p=P), res[:])
+
+        def cast_cand(w):
+            grouped = keep.tile([P, N, 4], BF16, name="n_g%d" % w, tag="then_x%d" % (4 + w), align_bytes=64)
+            for n0 in range(0, N, 256):
+                nc.scalar.copy(grouped[:, n0 : n0 + 256], n_raw[:, w, :, n0 : n0 + 256].rearrange("p t n -> p n t"))
+            return grouped[:].rearrange("p n t -> p (n t)")
+
+        entity(0)
+        entity(1)
+        entity(2)
+        gather_tab2(0)
+        gather_tab2(1)
+        times_arr(0)
+        wri_g = cast_rel(wri_raw, "wri_g", 2, "then_x2")
+        times_arr(1)
+        wri_q = quant(wri_g[:].rearrange("p t m j -> p (t m j)"), "wri")
+        n_q = []
+        for c in range(NCH):
+            times_ari(c, wri_q)
+            add(c)
+            if c < 2:
+                n_g = cast_cand(c)
+            if c + 3 < NCH:
+                entity(c + 3)
+            if c + 2 < NCH:
+                times_arr(c + 2)
+            if c < 2:
+                n_q.append(quant(n_g, "n%d" % c))
+            if c >= 2:
+                score(c - 2, n_q)
+        score(NCH - 2, n_q)
+        score(NCH - 1, n_q)

@@ -155,6 +155,7 @@ def tile_list_ckg_sig_kernel(
         xs = {}
         ys = {}
         hs = {}
+        hq = {}
 
         def entity(c):
             ab[c] = ring.tile([P, 2, CH, 4], F32, name="ab")
@@ -206,17 +207,21 @@ def tile_list_ckg_sig_kernel(
             ys[c] = y
 
         def add(c):
-            h = ring.tile([P, 2 * CH * 4], BF16, name="h", bufs=5, align_bytes=64)
-            eng = nc.vector if c == NCH - 1 else nc.gpsimd
+            h = ring.tile([P, 2 * CH * 4], BF16, name="h", bufs=2, align_bytes=64)
+            eng = nc.vector if c >= NCH - 2 else nc.gpsimd
             eng.tensor_tensor(
                 h[:], xs[c][:].rearrange("p w j t -> p (w j t)"), ys[c][:].rearrange("p w j t -> p (w j t)"), ADD
             )
             hs[c] = h
 
-        def score(c, n_q):
-            codes = ring.tile([P, 2 * CH], U32, name="h_c", align_bytes=64)
-            scales = ring.tile([P, 2 * CH], U8, name="h_s", align_bytes=64)
+        def quant_h(c):
+            codes = keep.tile([P, 2 * CH], U32, name="h_c%d" % c, align_bytes=64)
+            scales = keep.tile([P, 2 * CH], U8, name="h_s%d" % c, align_bytes=64)
             nc.vector.quantize_mx(out=codes[:].bitcast(FP8X4), scales=scales[:], in_=hs[c][:])
+            hq[c] = (codes, scales)
+
+        def score(c, n_q):
+            codes, scales = hq[c]
             bank = ps_y.tile([P, 4, CH], F32, name="bank_y")
             for m in range(4):
                 for w in range(2):
@@ -248,19 +253,28 @@ def tile_list_ckg_sig_kernel(
         wri_g = cast_rel(wri_raw, "wri_g", 2, "then_x2")
         times_arr(1)
         wri_q = quant(wri_g[:].rearrange("p t m j -> p (t m j)"), "wri")
+        n_g = []
         n_q = []
         for c in range(NCH):
             times_ari(c, wri_q)
-            add(c)
-            if c < 2:
-                n_g = cast_cand(c)
+            if c == NCH - 1:
+                add(c - 1)
+            if c >= 2:
+                quant_h(c - 2)
+            if c in (2, 3):
+                n_q.append(quant(n_g[c - 2], "n%d" % (c - 2)))
+            if c != NCH - 2:
+                add(c)
             if c + 3 < NCH:
                 entity(c + 3)
+            if c < 2:
+                n_g.append(cast_cand(c))
             if c + 2 < NCH:
                 times_arr(c + 2)
-            if c < 2:
-                n_q.append(quant(n_g, "n%d" % c))
-            if c >= 2:
+            if c == 3:
+                score(0, n_q)
+            if c >= 3:
                 score(c - 2, n_q)
-        score(NCH - 2, n_q)
-        score(NCH - 1, n_q)
+        for c in range(NCH - 2, NCH):
+            quant_h(c)
+            score(c, n_q)

@@ -22,7 +22,7 @@ CH = 128
 NCH = J // CH
 HALF = 512
 TAB_ROW, TAB2_ROW = 112, 48
-TAB_S, W_S, PLANE_BYTES = 0, 2 * J, 2 * J + 4 * R
+TAB_S, W_S, PLANE_BYTES = (0, 2 * HALF + 4 * R), 2 * HALF, 2 * J + 4 * R
 TAB2_K = 4
 
 
@@ -68,26 +68,30 @@ def tile_list_ckg_sig_kernel(
         nc.gpsimd.memset(tab2_sw[64:P, :], 0)
         nc.gpsimd.memset(plane2[:], 0)
 
-        tab_sg = keep.tile([P, 2, J], U8, name="tab_sg", align_bytes=64)
-        for a in range(2):
-            nc.vector.tensor_copy(tab_sg[:, a, :], tab_sw[:, a, :].bitcast(U8).indirect(idx[:]))
+        def gather_tab_scales(h, tile):
+            for a in range(2):
+                nc.vector.tensor_copy(
+                    tile[:, a, :], tab_sw[:, a, :].bitcast(U8).indirect(idx[:, h * 32 : (h + 1) * 32])
+                )
 
-        joined = keep.tile([P, PLANE_BYTES // 4], I32, name="joined", align_bytes=64)
-        nc.vector.tensor_copy(joined[96:P, 0 : W_S // 4], tab_sg[96:P].rearrange("p a j -> p (a j)").bitcast(I32))
+        tab_sg0 = keep.tile([P, 2, HALF], U8, name="tab_sg0", align_bytes=64)
+        gather_tab_scales(0, tab_sg0)
+        joined = keep.tile([P, TAB_S[1] // 4], I32, name="joined", align_bytes=64)
+        nc.vector.tensor_copy(joined[96:P, 0 : W_S // 4], tab_sg0[96:P].rearrange("p a j -> p (a j)").bitcast(I32))
         nc.vector.tensor_copy(
             joined[96:P, W_S // 4 :].rearrange("p (s t g e) -> p s t g e", s=4, t=4, e=2),
             w_sraw[96:P].rearrange("p w a (g t e) -> p (w a) t g e", t=4, e=2),
         )
         for r in range(4):
-            nc.sync.dma_start(planes[r:P:32, :], joined[TAB_ROW + r : P : 4, :])
+            nc.sync.dma_start(planes[r:P:32, 0 : TAB_S[1] // 4], joined[TAB_ROW + r : P : 4, :])
         planes8 = planes[:].bitcast(U8)
         plane28 = plane2[TAB2_K:P, :].bitcast(U8)
 
         tab_g = [
-            keep.tile([P, HALF], U32, name="tab_g0", tag="then_tab2_sg", align_bytes=64),
+            keep.tile([P, HALF], U32, name="tab_g0", tag="then_tab_sg1", align_bytes=64),
             keep.tile([P, HALF], U32, name="tab_g1", align_bytes=64),
         ]
-        tab_p = keep.tile([P, 2, 2 * J], U8, name="tab_p", align_bytes=64)
+        tab_p = [keep.tile([P, 2, 2 * HALF], U8, name="tab_p%d" % h, align_bytes=64) for h in range(2)]
         tab2_g = keep.tile([P, J], U32, name="tab2_g", align_bytes=64)
         w_p = keep.tile([P, 2, 2, R // 2], I32, name="w_p", align_bytes=64)
 
@@ -95,9 +99,8 @@ def tile_list_ckg_sig_kernel(
             nc.vector.tensor_copy(tab_g[h][:], tab_w[:].bitcast(U32).indirect(idx[:, h * 32 : (h + 1) * 32]))
 
         def part_tab(h):
-            cols = slice(h * HALF, (h + 1) * HALF)
             nc.vector.tensor_copy(
-                tab_p[:].bitcast(U16)[:, :, cols],
+                tab_p[h][:].bitcast(U16),
                 tab_g[h][:].bitcast(U16).rearrange("p (j a) -> p a j", a=2),
             )
 
@@ -115,12 +118,21 @@ def tile_list_ckg_sig_kernel(
         order_columns(1, wei_raw)
         tab2_w = keep.tile([P, T], I32, name="tab2_w", tag="then_tab2", align_bytes=64)
         nc.sync.dma_start(tab2_w[:], tab2_words[0].rearrange("p t b -> p (t b)").bitcast(I32))
-        gather_tab(0)
-        part_tab(0)
-        tab2_sg = keep.tile([P, J], U8, name="tab2_sg", tag="then_tab2_sg", align_bytes=64)
+        tab2_sg = keep.tile([P, J], U8, name="tab2_sg", align_bytes=64)
         nc.vector.tensor_copy(tab2_sg[:], tab2_sw[:].bitcast(U8).indirect(idx2[:]))
         for r in range(4):
             nc.sync.dma_start(plane2[TAB2_K + r : P : 32, :], tab2_sg[TAB2_ROW + r : 64 : 4, :].bitcast(I32))
+        gather_tab(0)
+        part_tab(0)
+        wri_raw = keep.tile([P, 4, R], F32, name="wri_raw", tag="then_wri", align_bytes=64)
+        nc.sync.dma_start(wri_raw[:], wri.rearrange("(p j) c -> p j c", j=4))
+        tab_sg1 = keep.tile([P, 2, HALF], U8, name="tab_sg1", tag="then_tab_sg1", align_bytes=64)
+        gather_tab_scales(1, tab_sg1)
+        for r in range(4):
+            nc.sync.dma_start(
+                planes[r:P:32, TAB_S[1] // 4 :],
+                tab_sg1[TAB_ROW + r : P : 4].rearrange("p a j -> p (a j)").bitcast(I32),
+            )
         gather_tab(1)
 
         def cast_rel(raw, name, on_scalar, tag):
@@ -144,8 +156,6 @@ def tile_list_ckg_sig_kernel(
         part_tab(1)
         wrr_q = quant(wrr_g[:].rearrange("p t m j -> p (t m j)"), "wrr")
 
-        wri_raw = keep.tile([P, 4, R], F32, name="wri_raw", tag="then_wri", align_bytes=64)
-        nc.sync.dma_start(wri_raw[:], wri.rearrange("(p j) c -> p j c", j=4))
         n_raw = keep.tile([P, 2, 4, N], F32, name="n_raw", tag="then_n", align_bytes=64)
         for w, src in enumerate((nr, ni)):
             for t in range(4):
@@ -158,6 +168,7 @@ def tile_list_ckg_sig_kernel(
         hq = {}
 
         def entity(c):
+            s0 = TAB_S[c // 4] + CH * (c % 4)
             ab[c] = ring.tile([P, 2, CH, 4], F32, name="ab")
             for w in range(2):
                 bank = ps_ab.tile([P, 4, CH], F32, name="bank_ab")
@@ -167,8 +178,8 @@ def tile_list_ckg_sig_kernel(
                             out=bank[:, t, :],
                             lhsT=w_p[:, w, a, 64 * t : 64 * (t + 1)].bitcast(U8).bitcast(FP4X4),
                             lhsT_scale=planes8[:, W_S + R * (2 * w + a) + P * t : W_S + R * (2 * w + a) + P * (t + 1)],
-                            rhs=tab_p[:, a, 2 * CH * c : 2 * CH * (c + 1)].bitcast(FP4X4),
-                            rhs_scale=planes8[:, J * a + CH * c : J * a + CH * (c + 1)],
+                            rhs=tab_p[c // 4][:, a, 2 * CH * (c % 4) : 2 * CH * (c % 4 + 1)].bitcast(FP4X4),
+                            rhs_scale=planes8[:, s0 + HALF * a : s0 + HALF * a + CH],
                             start=(a == 0),
                             stop=(a == 1),
                         )
@@ -240,8 +251,8 @@ def tile_list_ckg_sig_kernel(
 
         def cast_cand(w):
             grouped = keep.tile([P, N, 4], BF16, name="n_g%d" % w, tag="then_x%d" % (4 + w), align_bytes=64)
-            for n0 in range(0, N, 256):
-                nc.scalar.copy(grouped[:, n0 : n0 + 256], n_raw[:, w, :, n0 : n0 + 256].rearrange("p t n -> p n t"))
+            for n0 in range(0, N, P):
+                nc.scalar.copy(grouped[:, n0 : n0 + P], n_raw[:, w, :, n0 : n0 + P].rearrange("p t n -> p n t"))
             return grouped[:].rearrange("p n t -> p (n t)")
 
         entity(0)

@@ -21,8 +21,8 @@ P = 128
 CH = 128
 NCH = J // CH
 HALF = 512
-TAB_ROW, TAB2_ROW = 112, 48
-TAB_S, W_S, PLANE_BYTES = (0, 2 * HALF + 4 * R), 2 * HALF, 2 * J + 4 * R
+TAB_ROW, TAB2_ROW = 96, 48
+W_S, PASS_BYTES = J, J + 2 * R
 TAB2_K = 4
 
 
@@ -40,55 +40,48 @@ def tile_list_ckg_sig_kernel(
 
         idx = keep.tile([P, J // 16], U16, name="idx")
         idx2 = keep.tile([P, J // 16], U16, name="idx2")
-        tab_sw = keep.tile([P, 2, T // 4], I32, name="tab_sw", align_bytes=64)
-        tab2_sw = keep.tile([P, T // 4], I32, name="tab2_sw", tag="then_wri", align_bytes=64)
-        w_sraw = keep.tile([P, 2, 2, R // 4], I32, name="w_sraw", tag="then_tab2", align_bytes=64)
+        tab_sw = keep.tile([P, T // 4], I32, name="tab_sw", align_bytes=64)
+        tab2_sw = keep.tile([P, T // 4], I32, name="tab2_sw", tag="then_wrr", align_bytes=64)
+        w_sraw = keep.tile([P, 2, R // 4], I32, name="w_sraw", tag="then_tab2", align_bytes=64)
         tab_w = keep.tile([P, T], I32, name="tab_w", align_bytes=64)
         wer_raw = keep.tile([P, 2, R // 2], I32, name="wer_raw", align_bytes=64)
         wei_raw = keep.tile([P, 2, R // 2], I32, name="wei_raw", align_bytes=64)
-        wrr_raw = keep.tile([P, 4, R], F32, name="wrr_raw", align_bytes=64)
-        planes = keep.tile([P, PLANE_BYTES // 4], I32, name="planes", align_bytes=64)
+        planes = keep.tile([P, 2, PASS_BYTES // 4], I32, name="planes", align_bytes=64)
         plane2 = keep.tile([P, J // 4], I32, name="plane2", align_bytes=64)
 
         nc.sync.dma_start(idx[:], offs)
-        nc.sync.dma_start(tab_sw[TAB_ROW:P], tab_scales.bitcast(I32).rearrange("a q c -> q a c"))
-        nc.sync.dma_start(w_sraw[TAB_ROW:P, 0], wer_scales.bitcast(I32).rearrange("a q c -> q a c"))
-        nc.sync.dma_start(w_sraw[TAB_ROW:P, 1], wei_scales.bitcast(I32).rearrange("a q c -> q a c"))
+        nc.sync.dma_start(tab_sw[TAB_ROW:P], tab_scales.bitcast(I32).rearrange("a q c -> (a q) c"))
+        nc.sync.dma_start(w_sraw[TAB_ROW:P, 0], wer_scales.bitcast(I32).rearrange("a q c -> (a q) c"))
+        nc.sync.dma_start(w_sraw[TAB_ROW:P, 1], wei_scales.bitcast(I32).rearrange("a q c -> (a q) c"))
         nc.sync.dma_start(idx2[:], offs2)
         nc.sync.dma_start(tab2_sw[TAB2_ROW : TAB2_ROW + 16, :], tab2_scales.bitcast(I32)[0])
         nc.sync.dma_start(wer_raw[:], wer_words.bitcast(I32).rearrange("a p c -> p a c"))
         nc.sync.dma_start(wei_raw[:], wei_words.bitcast(I32).rearrange("a p c -> p a c"))
         nc.sync.dma_start(tab_w[:], tab_words[0].rearrange("p t b -> p (t b)").bitcast(I32))
-        nc.sync.dma_start(wrr_raw[:], wrr.rearrange("(p j) c -> p j c", j=4))
 
         nc.vector.memset(tab_sw[0:TAB_ROW], 0)
-        nc.vector.memset(w_sraw[96:TAB_ROW], 0)
         nc.gpsimd.memset(planes[:], 0)
         nc.gpsimd.memset(tab2_sw[0:TAB2_ROW, :], 0)
         nc.gpsimd.memset(tab2_sw[64:P, :], 0)
         nc.gpsimd.memset(plane2[:], 0)
 
-        def gather_tab_scales(h, tile):
-            for a in range(2):
-                nc.vector.tensor_copy(
-                    tile[:, a, :], tab_sw[:, a, :].bitcast(U8).indirect(idx[:, h * 32 : (h + 1) * 32])
-                )
-
-        tab_sg0 = keep.tile([P, 2, HALF], U8, name="tab_sg0", align_bytes=64)
-        gather_tab_scales(0, tab_sg0)
-        joined = keep.tile([P, TAB_S[1] // 4], I32, name="joined", align_bytes=64)
-        nc.vector.tensor_copy(joined[96:P, 0 : W_S // 4], tab_sg0[96:P].rearrange("p a j -> p (a j)").bitcast(I32))
+        tab_sg = keep.tile([P, J], U8, name="tab_sg", align_bytes=64)
+        nc.vector.tensor_copy(tab_sg[:], tab_sw[:].bitcast(U8).indirect(idx[:]))
+        joined = keep.tile([P, PASS_BYTES // 4], I32, name="joined", align_bytes=64)
+        nc.vector.tensor_copy(joined[TAB_ROW:P, 0 : W_S // 4], tab_sg[TAB_ROW:P].bitcast(I32))
         nc.vector.tensor_copy(
-            joined[96:P, W_S // 4 :].rearrange("p (s t g e) -> p s t g e", s=4, t=4, e=2),
-            w_sraw[96:P].rearrange("p w a (g t e) -> p (w a) t g e", t=4, e=2),
+            joined[TAB_ROW:P, W_S // 4 :].rearrange("p (w t g e) -> p w t g e", w=2, t=4, e=2),
+            w_sraw[TAB_ROW:P].rearrange("p w (g t e) -> p w t g e", t=4, e=2),
         )
-        for r in range(4):
-            nc.sync.dma_start(planes[r:P:32, 0 : TAB_S[1] // 4], joined[TAB_ROW + r : P : 4, :])
+        for a in range(2):
+            for r in range(4):
+                row = TAB_ROW + 16 * a
+                nc.sync.dma_start(planes[r:P:32, a, :], joined[row + r : row + 16 : 4, :])
         planes8 = planes[:].bitcast(U8)
         plane28 = plane2[TAB2_K:P, :].bitcast(U8)
 
         tab_g = [
-            keep.tile([P, HALF], U32, name="tab_g0", tag="then_tab_sg1", align_bytes=64),
+            keep.tile([P, HALF], U32, name="tab_g0", tag="then_wri", align_bytes=64),
             keep.tile([P, HALF], U32, name="tab_g1", align_bytes=64),
         ]
         tab_p = [keep.tile([P, 2, 2 * HALF], U8, name="tab_p%d" % h, align_bytes=64) for h in range(2)]
@@ -122,26 +115,23 @@ def tile_list_ckg_sig_kernel(
         nc.vector.tensor_copy(tab2_sg[:], tab2_sw[:].bitcast(U8).indirect(idx2[:]))
         for r in range(4):
             nc.sync.dma_start(plane2[TAB2_K + r : P : 32, :], tab2_sg[TAB2_ROW + r : 64 : 4, :].bitcast(I32))
+        wrr_raw = keep.tile([P, 4, R], F32, name="wrr_raw", tag="then_wrr", align_bytes=64)
+        nc.sync.dma_start(wrr_raw[:], wrr.rearrange("(p j) c -> p j c", j=4))
         gather_tab(0)
         part_tab(0)
         wri_raw = keep.tile([P, 4, R], F32, name="wri_raw", tag="then_wri", align_bytes=64)
         nc.sync.dma_start(wri_raw[:], wri.rearrange("(p j) c -> p j c", j=4))
-        tab_sg1 = keep.tile([P, 2, HALF], U8, name="tab_sg1", tag="then_tab_sg1", align_bytes=64)
-        gather_tab_scales(1, tab_sg1)
-        for r in range(4):
-            nc.sync.dma_start(
-                planes[r:P:32, TAB_S[1] // 4 :],
-                tab_sg1[TAB_ROW + r : P : 4].rearrange("p a j -> p (a j)").bitcast(I32),
-            )
         gather_tab(1)
 
-        def cast_rel(raw, name, on_scalar, tag):
+        def cast_rel(raw, name, engines, tag):
             grouped = keep.tile([P, 4, P, 4], BF16, name=name, tag=tag, align_bytes=64)
             for t in range(4):
                 dst = grouped[:, t].rearrange("p (g i) j -> p g i j", i=8)
                 src = raw[:].rearrange("p j (g t i) -> p t g i j", t=4, i=8)[:, t]
-                if t < on_scalar:
+                if engines[t] == "scalar":
                     nc.scalar.copy(dst, src)
+                elif engines[t] == "vector":
+                    nc.vector.tensor_copy(dst, src)
                 else:
                     nc.gpsimd.tensor_scalar(dst, src, 1.0, 0.0, MULT, ADD)
             return grouped
@@ -152,14 +142,7 @@ def tile_list_ckg_sig_kernel(
             nc.vector.quantize_mx(out=codes[:].bitcast(FP8X4), scales=scales[:], in_=grouped)
             return codes, scales
 
-        wrr_g = cast_rel(wrr_raw, "wrr_g", 4, "then_n")
         part_tab(1)
-        wrr_q = quant(wrr_g[:].rearrange("p t m j -> p (t m j)"), "wrr")
-
-        n_raw = keep.tile([P, 2, 4, N], F32, name="n_raw", tag="then_n", align_bytes=64)
-        for w, src in enumerate((nr, ni)):
-            for t in range(4):
-                nc.sync.dma_start(n_raw[:, w, t, :], src.rearrange("(g t i) n -> t g i n", t=4, i=8)[t])
 
         ab = {}
         xs = {}
@@ -168,8 +151,10 @@ def tile_list_ckg_sig_kernel(
         hq = {}
 
         def entity(c):
-            s0 = TAB_S[c // 4] + CH * (c % 4)
-            ab[c] = ring.tile([P, 2, CH, 4], F32, name="ab")
+            if c % 4 == 3:
+                ab[c] = keep.tile([P, 2, CH, 4], F32, name="ab%d" % c, tag="then_ab", align_bytes=64)
+            else:
+                ab[c] = ring.tile([P, 2, CH, 4], F32, name="ab")
             for w in range(2):
                 bank = ps_ab.tile([P, 4, CH], F32, name="bank_ab")
                 for t in range(4):
@@ -177,9 +162,9 @@ def tile_list_ckg_sig_kernel(
                         nc.tensor.matmul_mx(
                             out=bank[:, t, :],
                             lhsT=w_p[:, w, a, 64 * t : 64 * (t + 1)].bitcast(U8).bitcast(FP4X4),
-                            lhsT_scale=planes8[:, W_S + R * (2 * w + a) + P * t : W_S + R * (2 * w + a) + P * (t + 1)],
+                            lhsT_scale=planes8[:, a, W_S + R * w + P * t : W_S + R * w + P * (t + 1)],
                             rhs=tab_p[c // 4][:, a, 2 * CH * (c % 4) : 2 * CH * (c % 4 + 1)].bitcast(FP4X4),
-                            rhs_scale=planes8[:, s0 + HALF * a : s0 + HALF * a + CH],
+                            rhs_scale=planes8[:, a, CH * c : CH * (c + 1)],
                             start=(a == 0),
                             stop=(a == 1),
                         )
@@ -202,10 +187,10 @@ def tile_list_ckg_sig_kernel(
 
         def times_arr(c):
             arr = relation(c, wrr_q)
-            if c in (2, 4, 5):
+            if c in (2, 5, 6):
                 x = keep.tile([P, 2, CH, 4], F32, name="x%d" % c, tag="then_x%d" % c, align_bytes=64)
             else:
-                x = ring.tile([P, 2, CH, 4], F32, name="x")
+                x = ring.tile([P, 2, CH, 4], F32, name="x", bufs=4)
             nc.vector.tensor_tensor(x[:, 0], ab[c][:, 0], arr, MULT)
             nc.vector.tensor_tensor(x[:, 1], ab[c][:, 1], arr, MULT)
             xs[c] = x
@@ -233,24 +218,29 @@ def tile_list_ckg_sig_kernel(
 
         def score(c, n_q):
             codes, scales = hq[c]
-            bank = ps_y.tile([P, 4, CH], F32, name="bank_y")
-            for m in range(4):
-                for w in range(2):
-                    nc.tensor.matmul_mx(
-                        out=bank[:, m, :],
-                        lhsT=n_q[w][0][:, P * m : P * (m + 1)].bitcast(FP8X4),
-                        lhsT_scale=n_q[w][1][:, P * m : P * (m + 1)],
-                        rhs=codes[:, CH * w : CH * (w + 1)].bitcast(FP8X4),
-                        rhs_scale=scales[:, CH * w : CH * (w + 1)],
-                        start=(w == 0),
-                        stop=(w == 1),
-                    )
-            res = ring.tile([P, 4, CH], F32, name="res")
-            nc.scalar.activation(res[:], bank[:], SIGMOID)
-            nc.sync.dma_start(out[:, CH * c : CH * (c + 1)].rearrange("(m p) j -> p m j", p=P), res[:])
+            parts = 2 if c == NCH - 1 else 1
+            step = 4 // parts
+            for m0 in range(0, 4, step):
+                pool = ps_cd if parts == 2 else ps_y
+                bank = pool.tile([P, step, CH], F32, name="bank_cd" if parts == 2 else "bank_y")
+                for m in range(m0, m0 + step):
+                    for w in range(2):
+                        nc.tensor.matmul_mx(
+                            out=bank[:, m - m0, :],
+                            lhsT=n_q[w][0][:, P * m : P * (m + 1)].bitcast(FP8X4),
+                            lhsT_scale=n_q[w][1][:, P * m : P * (m + 1)],
+                            rhs=codes[:, CH * w : CH * (w + 1)].bitcast(FP8X4),
+                            rhs_scale=scales[:, CH * w : CH * (w + 1)],
+                            start=(w == 0),
+                            stop=(w == 1),
+                        )
+                res = ring.tile([P, step, CH], F32, name="res")
+                nc.scalar.activation(res[:], bank[:], SIGMOID)
+                rows = out[P * m0 : P * (m0 + step), CH * c : CH * (c + 1)]
+                nc.sync.dma_start(rows.rearrange("(m p) j -> p m j", p=P), res[:])
 
         def cast_cand(w):
-            grouped = keep.tile([P, N, 4], BF16, name="n_g%d" % w, tag="then_x%d" % (4 + w), align_bytes=64)
+            grouped = keep.tile([P, N, 4], BF16, name="n_g%d" % w, tag="then_x%d" % (5 + w), align_bytes=64)
             for n0 in range(0, N, P):
                 nc.scalar.copy(grouped[:, n0 : n0 + P], n_raw[:, w, :, n0 : n0 + P].rearrange("p t n -> p n t"))
             return grouped[:].rearrange("p n t -> p (n t)")
@@ -260,32 +250,52 @@ def tile_list_ckg_sig_kernel(
         entity(2)
         gather_tab2(0)
         gather_tab2(1)
+        n_raw = keep.tile([P, 2, 4, N], F32, name="n_raw", tag="then_tab2", align_bytes=64)
+        for w, src in enumerate((nr, ni)):
+            for t in range(4):
+                nc.sync.dma_start(n_raw[:, w, t, :], src.rearrange("(g t i) n -> t g i n", t=4, i=8)[t])
+        wrr_g = cast_rel(wrr_raw, "wrr_g", ("vector", "vector", "vector", "scalar"), "then_ab")
+        wrr_q = quant(wrr_g[:].rearrange("p t m j -> p (t m j)"), "wrr")
         times_arr(0)
-        wri_g = cast_rel(wri_raw, "wri_g", 2, "then_x2")
+        entity(3)
+        wri_g = cast_rel(wri_raw, "wri_g", ("scalar", "scalar", "gpsimd", "gpsimd"), "then_x2")
         times_arr(1)
         wri_q = quant(wri_g[:].rearrange("p t m j -> p (t m j)"), "wri")
-        n_g = []
+        times_arr(2)
+        times_ari(0, wri_q)
+        add(0)
+        entity(4)
+        n_g = [cast_cand(0)]
+        times_arr(3)
+        times_ari(1, wri_q)
+        add(1)
+        entity(5)
+        n_g.append(cast_cand(1))
+        times_arr(4)
         n_q = []
-        for c in range(NCH):
+        for c in range(2, 6):
             times_ari(c, wri_q)
-            if c == NCH - 1:
-                add(c - 1)
-            if c >= 2:
-                quant_h(c - 2)
-            if c in (2, 3):
+            quant_h(c - 2)
+            if c < 4:
                 n_q.append(quant(n_g[c - 2], "n%d" % (c - 2)))
-            if c != NCH - 2:
-                add(c)
+            add(c)
+            if c + 4 < NCH:
+                entity(c + 4)
             if c + 3 < NCH:
-                entity(c + 3)
-            if c < 2:
-                n_g.append(cast_cand(c))
-            if c + 2 < NCH:
-                times_arr(c + 2)
+                times_arr(c + 3)
             if c == 3:
                 score(0, n_q)
             if c >= 3:
                 score(c - 2, n_q)
-        for c in range(NCH - 2, NCH):
-            quant_h(c)
-            score(c, n_q)
+        times_ari(6, wri_q)
+        times_ari(7, wri_q)
+        quant_h(4)
+        score(4, n_q)
+        add(6)
+        quant_h(5)
+        score(5, n_q)
+        quant_h(6)
+        score(6, n_q)
+        add(7)
+        quant_h(7)
+        score(7, n_q)

@@ -41,10 +41,10 @@ def tile_list_ckg_sig_kernel(
         idx = keep.tile([P, J // 16], U16, name="idx")
         idx2 = keep.tile([P, J // 16], U16, name="idx2")
         tab_sw = keep.tile([P, T // 4], I32, name="tab_sw", align_bytes=64)
-        tab2_sw = keep.tile([P, T // 4], I32, name="tab2_sw", tag="then_wrr", align_bytes=64)
+        tab2_sw = keep.tile([P, T // 4], I32, name="tab2_sw", align_bytes=64)
         w_sraw = keep.tile([P, 2, R // 4], I32, name="w_sraw", tag="then_tab2", align_bytes=64)
         tab_w = keep.tile([P, T], I32, name="tab_w", align_bytes=64)
-        wer_raw = keep.tile([P, 2, R // 2], I32, name="wer_raw", align_bytes=64)
+        wer_raw = keep.tile([P, 2, R // 2], I32, name="wer_raw", tag="then_wrr", align_bytes=64)
         wei_raw = keep.tile([P, 2, R // 2], I32, name="wei_raw", align_bytes=64)
         planes = keep.tile([P, 2, PASS_BYTES // 4], I32, name="planes", align_bytes=64)
         plane2 = keep.tile([P, J // 4], I32, name="plane2", align_bytes=64)
@@ -73,10 +73,13 @@ def tile_list_ckg_sig_kernel(
             joined[TAB_ROW:P, W_S // 4 :].rearrange("p (w t g e) -> p w t g e", w=2, t=4, e=2),
             w_sraw[TAB_ROW:P].rearrange("p w (g t e) -> p w t g e", t=4, e=2),
         )
+        tab2_w = keep.tile([P, T], I32, name="tab2_w", tag="then_tab2", align_bytes=64)
         for a in range(2):
             for r in range(4):
                 row = TAB_ROW + 16 * a
                 nc.sync.dma_start(planes[r:P:32, a, :], joined[row + r : row + 16 : 4, :])
+            if a == 0:
+                nc.sync.dma_start(tab2_w[:], tab2_words[0].rearrange("p t b -> p (t b)").bitcast(I32))
         planes8 = planes[:].bitcast(U8)
         plane28 = plane2[TAB2_K:P, :].bitcast(U8)
 
@@ -108,15 +111,13 @@ def tile_list_ckg_sig_kernel(
             )
 
         order_columns(0, wer_raw)
+        wrr_raw = keep.tile([P, 4, R], F32, name="wrr_raw", tag="then_wrr", align_bytes=64)
+        nc.sync.dma_start(wrr_raw[:], wrr.rearrange("(p j) c -> p j c", j=4))
         order_columns(1, wei_raw)
-        tab2_w = keep.tile([P, T], I32, name="tab2_w", tag="then_tab2", align_bytes=64)
-        nc.sync.dma_start(tab2_w[:], tab2_words[0].rearrange("p t b -> p (t b)").bitcast(I32))
         tab2_sg = keep.tile([P, J], U8, name="tab2_sg", align_bytes=64)
         nc.vector.tensor_copy(tab2_sg[:], tab2_sw[:].bitcast(U8).indirect(idx2[:]))
         for r in range(4):
             nc.sync.dma_start(plane2[TAB2_K + r : P : 32, :], tab2_sg[TAB2_ROW + r : 64 : 4, :].bitcast(I32))
-        wrr_raw = keep.tile([P, 4, R], F32, name="wrr_raw", tag="then_wrr", align_bytes=64)
-        nc.sync.dma_start(wrr_raw[:], wrr.rearrange("(p j) c -> p j c", j=4))
         gather_tab(0)
         part_tab(0)
         wri_raw = keep.tile([P, 4, R], F32, name="wri_raw", tag="then_wri", align_bytes=64)
@@ -151,10 +152,8 @@ def tile_list_ckg_sig_kernel(
         hq = {}
 
         def entity(c):
-            if c % 4 == 3:
-                ab[c] = keep.tile([P, 2, CH, 4], F32, name="ab%d" % c, tag="then_ab", align_bytes=64)
-            else:
-                ab[c] = ring.tile([P, 2, CH, 4], F32, name="ab")
+            tag = ("ab0", "then_wrr", "ab2", "then_ab")[c % 4]
+            ab[c] = keep.tile([P, 2, CH, 4], F32, name="ab%d" % c, tag=tag, align_bytes=64)
             for w in range(2):
                 bank = ps_ab.tile([P, 4, CH], F32, name="bank_ab")
                 for t in range(4):
@@ -203,7 +202,10 @@ def tile_list_ckg_sig_kernel(
             ys[c] = y
 
         def add(c):
-            h = ring.tile([P, 2 * CH * 4], BF16, name="h", bufs=2, align_bytes=64)
+            if c >= NCH - 2:
+                h = keep.tile([P, 2 * CH * 4], BF16, name="h%d" % c, tag="h_last", align_bytes=64)
+            else:
+                h = ring.tile([P, 2 * CH * 4], BF16, name="h", bufs=2, align_bytes=64)
             eng = nc.vector if c >= NCH - 2 else nc.gpsimd
             eng.tensor_tensor(
                 h[:], xs[c][:].rearrange("p w j t -> p (w j t)"), ys[c][:].rearrange("p w j t -> p (w j t)"), ADD
@@ -234,7 +236,7 @@ def tile_list_ckg_sig_kernel(
                             start=(w == 0),
                             stop=(w == 1),
                         )
-                res = ring.tile([P, step, CH], F32, name="res")
+                res = ring.tile([P, step, CH], F32, name="res", bufs=5)
                 nc.scalar.activation(res[:], bank[:], SIGMOID)
                 rows = out[P * m0 : P * (m0 + step), CH * c : CH * (c + 1)]
                 nc.sync.dma_start(rows.rearrange("(m p) j -> p m j", p=P), res[:])
@@ -246,8 +248,6 @@ def tile_list_ckg_sig_kernel(
             return grouped[:].rearrange("p n t -> p (n t)")
 
         entity(0)
-        entity(1)
-        entity(2)
         gather_tab2(0)
         gather_tab2(1)
         n_raw = keep.tile([P, 2, 4, N], F32, name="n_raw", tag="then_tab2", align_bytes=64)
@@ -256,10 +256,12 @@ def tile_list_ckg_sig_kernel(
                 nc.sync.dma_start(n_raw[:, w, t, :], src.rearrange("(g t i) n -> t g i n", t=4, i=8)[t])
         wrr_g = cast_rel(wrr_raw, "wrr_g", ("vector", "vector", "vector", "scalar"), "then_ab")
         wrr_q = quant(wrr_g[:].rearrange("p t m j -> p (t m j)"), "wrr")
+        entity(1)
         times_arr(0)
-        entity(3)
+        entity(2)
         wri_g = cast_rel(wri_raw, "wri_g", ("scalar", "scalar", "gpsimd", "gpsimd"), "then_x2")
         times_arr(1)
+        entity(3)
         wri_q = quant(wri_g[:].rearrange("p t m j -> p (t m j)"), "wri")
         times_arr(2)
         times_ari(0, wri_q)

@@ -21,9 +21,14 @@ P = 128
 CH = 128
 NCH = J // CH
 HALF = 512
-TAB_ROW, TAB2_ROW = 96, 48
+TAB_ROW, TAB2_ROW = 96, 112
 W_S, PASS_BYTES = J, J + 2 * R
 TAB2_K = 4
+BANKS = {"ab": (0, 3), "cd": (3, 3), "y": (6, 2)}
+H_KIB = (78, 68, 78, 67, 77, 66, 76)
+N_KIB = (84, 88)
+AB_KIB = (92, 96, 100, 28, 0, 8, 104, 108)
+X_KIB = {4: 69, 5: 79}
 
 
 def tile_list_ckg_sig_kernel(
@@ -34,75 +39,89 @@ def tile_list_ckg_sig_kernel(
     with ExitStack() as ctx:
         keep = ctx.enter_context(tc.tile_pool(name="keep", bufs=1))
         ring = ctx.enter_context(tc.tile_pool(name="ring", bufs=3))
-        ps_ab = ctx.enter_context(tc.psum_pool(name="ps_ab", bufs=2))
-        ps_cd = ctx.enter_context(tc.psum_pool(name="ps_cd", bufs=4))
-        ps_y = ctx.enter_context(tc.psum_pool(name="ps_y", bufs=2))
+        lay = ctx.enter_context(tc.tile_pool(name="lay", bufs=1))
+        psum = ctx.enter_context(tc.psum_pool(name="psum", bufs=1))
+
+        def laid(shape, dtype, name, kib):
+            return lay.tile(shape, dtype, name=name, align_bytes=64, offset=int(1024 * kib))
+
+        turns = {"ab": 0, "cd": 0, "y": 0}
+
+        def next_bank(kind, shape):
+            first, count = BANKS[kind]
+            turn = turns[kind]
+            turns.update({kind: turn + 1})
+            return psum.tile(shape, F32, name="%s%d" % (kind, turn), offset=2048 * (first + turn % count))
 
         idx = keep.tile([P, J // 16], U16, name="idx")
         idx2 = keep.tile([P, J // 16], U16, name="idx2")
         tab_sw = keep.tile([P, T // 4], I32, name="tab_sw", align_bytes=64)
-        tab2_sw = keep.tile([P, T // 4], I32, name="tab2_sw", align_bytes=64)
-        w_sraw = keep.tile([P, 2, R // 4], I32, name="w_sraw", tag="then_tab2", align_bytes=64)
-        tab_w = keep.tile([P, T], I32, name="tab_w", align_bytes=64)
-        wer_raw = keep.tile([P, 2, R // 2], I32, name="wer_raw", tag="then_wrr", align_bytes=64)
+        tab2_sw = laid([P, T // 4], I32, "tab2_sw", 24)
+        tab_w = laid([P, T], I32, "tab_w", 0)
+        wer_raw = keep.tile([P, 2, R // 2], I32, name="wer_raw", align_bytes=64)
         wei_raw = keep.tile([P, 2, R // 2], I32, name="wei_raw", align_bytes=64)
         planes = keep.tile([P, 2, PASS_BYTES // 4], I32, name="planes", align_bytes=64)
         plane2 = keep.tile([P, J // 4], I32, name="plane2", align_bytes=64)
+        joined = keep.tile([P, PASS_BYTES // 4], I32, name="joined", align_bytes=64)
+        w_sraw = keep.tile([P, 2, R // 4], I32, name="w_sraw", align_bytes=64)
+        w_p = keep.tile([P, 2, 2, R // 2], I32, name="w_p", align_bytes=64)
 
         nc.sync.dma_start(idx[:], offs)
         nc.sync.dma_start(tab_sw[TAB_ROW:P], tab_scales.bitcast(I32).rearrange("a q c -> (a q) c"))
-        nc.sync.dma_start(w_sraw[TAB_ROW:P, 0], wer_scales.bitcast(I32).rearrange("a q c -> (a q) c"))
-        nc.sync.dma_start(w_sraw[TAB_ROW:P, 1], wei_scales.bitcast(I32).rearrange("a q c -> (a q) c"))
+        for w, src in enumerate((wer_scales, wei_scales)):
+            nc.sync.dma_start(w_sraw[TAB_ROW:P, w], src.bitcast(I32).rearrange("a q c -> (a q) c"))
         nc.sync.dma_start(idx2[:], offs2)
         nc.sync.dma_start(tab2_sw[TAB2_ROW : TAB2_ROW + 16, :], tab2_scales.bitcast(I32)[0])
+        nc.sync.dma_start(tab_w[:], tab_words[0].rearrange("p t b -> p (t b)").bitcast(I32))
         nc.sync.dma_start(wer_raw[:], wer_words.bitcast(I32).rearrange("a p c -> p a c"))
         nc.sync.dma_start(wei_raw[:], wei_words.bitcast(I32).rearrange("a p c -> p a c"))
-        nc.sync.dma_start(tab_w[:], tab_words[0].rearrange("p t b -> p (t b)").bitcast(I32))
 
         nc.vector.memset(tab_sw[0:TAB_ROW], 0)
         nc.gpsimd.memset(planes[:], 0)
-        nc.gpsimd.memset(tab2_sw[0:TAB2_ROW, :], 0)
-        nc.gpsimd.memset(tab2_sw[64:P, :], 0)
+        nc.gpsimd.memset(tab2_sw[0:TAB2_ROW], 0)
         nc.gpsimd.memset(plane2[:], 0)
 
-        tab_sg = keep.tile([P, J], U8, name="tab_sg", align_bytes=64)
+        tab_sg = laid([P, J], U8, "tab_sg", 39.5)
         nc.vector.tensor_copy(tab_sg[:], tab_sw[:].bitcast(U8).indirect(idx[:]))
-        joined = keep.tile([P, PASS_BYTES // 4], I32, name="joined", align_bytes=64)
-        nc.vector.tensor_copy(joined[TAB_ROW:P, 0 : W_S // 4], tab_sg[TAB_ROW:P].bitcast(I32))
         nc.vector.tensor_copy(
             joined[TAB_ROW:P, W_S // 4 :].rearrange("p (w t g e) -> p w t g e", w=2, t=4, e=2),
             w_sraw[TAB_ROW:P].rearrange("p w (g t e) -> p w t g e", t=4, e=2),
         )
-        tab2_w = keep.tile([P, T], I32, name="tab2_w", tag="then_tab2", align_bytes=64)
+        nc.vector.tensor_copy(joined[TAB_ROW:P, 0 : W_S // 4], tab_sg[TAB_ROW:P].bitcast(I32))
+        tab2_w = laid([P, T], I32, "tab2_w", 40)
+        wrr_raw = laid([P, 4, R], F32, "wrr_raw", 32)
         for a in range(2):
             for r in range(4):
                 row = TAB_ROW + 16 * a
                 nc.sync.dma_start(planes[r:P:32, a, :], joined[row + r : row + 16 : 4, :])
             if a == 0:
-                nc.sync.dma_start(tab2_w[:], tab2_words[0].rearrange("p t b -> p (t b)").bitcast(I32))
+                nc.sync.dma_start(wrr_raw[:], wrr.rearrange("(p j) c -> p j c", j=4))
+        nc.sync.dma_start(tab2_w[:], tab2_words[0].rearrange("p t b -> p (t b)").bitcast(I32))
         planes8 = planes[:].bitcast(U8)
         plane28 = plane2[TAB2_K:P, :].bitcast(U8)
 
         tab_g = [
-            keep.tile([P, HALF], U32, name="tab_g0", tag="then_wri", align_bytes=64),
+            keep.tile([P, HALF], U32, name="tab_g0", align_bytes=64),
             keep.tile([P, HALF], U32, name="tab_g1", align_bytes=64),
         ]
-        tab_p = [keep.tile([P, 2, 2 * HALF], U8, name="tab_p%d" % h, align_bytes=64) for h in range(2)]
-        tab2_g = keep.tile([P, J], U32, name="tab2_g", align_bytes=64)
-        w_p = keep.tile([P, 2, 2, R // 2], I32, name="w_p", align_bytes=64)
+        tab_p = {}
+        tab2_g = [keep.tile([P, HALF], U32, name="tab2_g%d" % h, align_bytes=64) for h in range(2)]
 
         def gather_tab(h):
             nc.vector.tensor_copy(tab_g[h][:], tab_w[:].bitcast(U32).indirect(idx[:, h * 32 : (h + 1) * 32]))
 
-        def part_tab(h):
+        def part_tab(first, count, kib):
+            parted = laid([P, 2, 2 * CH * count], U8, "tab_p%d" % first, kib)
+            cols = slice(CH * (first % 4), CH * (first % 4 + count))
             nc.vector.tensor_copy(
-                tab_p[h][:].bitcast(U16),
-                tab_g[h][:].bitcast(U16).rearrange("p (j a) -> p a j", a=2),
+                parted[:].bitcast(U16),
+                tab_g[first // 4][:, cols].bitcast(U16).rearrange("p (j a) -> p a j", a=2),
             )
+            for c in range(count):
+                tab_p[first + c] = parted[:, :, 2 * CH * c : 2 * CH * (c + 1)]
 
         def gather_tab2(h):
-            cols = slice(h * HALF, (h + 1) * HALF)
-            nc.vector.tensor_copy(tab2_g[:, cols], tab2_w[:].bitcast(U32).indirect(idx2[:, h * 32 : (h + 1) * 32]))
+            nc.vector.tensor_copy(tab2_g[h][:], tab2_w[:].bitcast(U32).indirect(idx2[:, h * 32 : (h + 1) * 32]))
 
         def order_columns(w, raw):
             nc.vector.tensor_copy(
@@ -110,22 +129,23 @@ def tile_list_ckg_sig_kernel(
                 raw[:].rearrange("p a (g t e) -> p a t g e", t=4, e=4),
             )
 
-        order_columns(0, wer_raw)
-        wrr_raw = keep.tile([P, 4, R], F32, name="wrr_raw", tag="then_wrr", align_bytes=64)
-        nc.sync.dma_start(wrr_raw[:], wrr.rearrange("(p j) c -> p j c", j=4))
-        order_columns(1, wei_raw)
         tab2_sg = keep.tile([P, J], U8, name="tab2_sg", align_bytes=64)
         nc.vector.tensor_copy(tab2_sg[:], tab2_sw[:].bitcast(U8).indirect(idx2[:]))
         for r in range(4):
-            nc.sync.dma_start(plane2[TAB2_K + r : P : 32, :], tab2_sg[TAB2_ROW + r : 64 : 4, :].bitcast(I32))
-        gather_tab(0)
-        part_tab(0)
-        wri_raw = keep.tile([P, 4, R], F32, name="wri_raw", tag="then_wri", align_bytes=64)
+            nc.sync.dma_start(plane2[TAB2_K + r : P : 32, :], tab2_sg[TAB2_ROW + r : P : 4, :].bitcast(I32))
+        wri_raw = laid([P, 4, R], F32, "wri_raw", 24)
         nc.sync.dma_start(wri_raw[:], wri.rearrange("(p j) c -> p j c", j=4))
+        gather_tab(0)
+        part_tab(0, 4, 60)
+        order_columns(0, wer_raw)
+        order_columns(1, wei_raw)
         gather_tab(1)
+        n_raw = [laid([P, 4, N], F32, "n_raw%d" % w, 8 * w) for w in range(2)]
+        for w, src in enumerate((nr, ni)):
+            for t in range(4):
+                nc.sync.dma_start(n_raw[w][:, t, :], src.rearrange("(g t i) n -> t g i n", t=4, i=8)[t])
 
-        def cast_rel(raw, name, engines, tag):
-            grouped = keep.tile([P, 4, P, 4], BF16, name=name, tag=tag, align_bytes=64)
+        def cast_rel(raw, grouped, engines):
             for t in range(4):
                 dst = grouped[:, t].rearrange("p (g i) j -> p g i j", i=8)
                 src = raw[:].rearrange("p j (g t i) -> p t g i j", t=4, i=8)[:, t]
@@ -135,169 +155,179 @@ def tile_list_ckg_sig_kernel(
                     nc.vector.tensor_copy(dst, src)
                 else:
                     nc.gpsimd.tensor_scalar(dst, src, 1.0, 0.0, MULT, ADD)
-            return grouped
+            return grouped[:].rearrange("p t m j -> p (t m j)")
 
-        def quant(grouped, name):
-            codes = keep.tile([P, 512], U32, name=name + "_c", align_bytes=64)
-            scales = keep.tile([P, 512], U8, name=name + "_s", align_bytes=64)
+        def quant(grouped, name, kib=None):
+            words = grouped.shape[1] // 4
+            if kib is None:
+                codes = keep.tile([P, words], U32, name=name + "_c", align_bytes=64)
+            else:
+                codes = laid([P, words], U32, name + "_c", kib)
+            scales = keep.tile([P, words], U8, name=name + "_s", align_bytes=64)
             nc.vector.quantize_mx(out=codes[:].bitcast(FP8X4), scales=scales[:], in_=grouped)
             return codes, scales
 
-        part_tab(1)
-
         ab = {}
         xs = {}
+        cd = {}
+        wr_q = {}
         ys = {}
         hs = {}
         hq = {}
 
-        def entity(c):
-            tag = ("ab0", "then_wrr", "ab2", "then_ab")[c % 4]
-            ab[c] = keep.tile([P, 2, CH, 4], F32, name="ab%d" % c, tag=tag, align_bytes=64)
-            for w in range(2):
-                bank = ps_ab.tile([P, 4, CH], F32, name="bank_ab")
-                for t in range(4):
-                    for a in range(2):
-                        nc.tensor.matmul_mx(
-                            out=bank[:, t, :],
-                            lhsT=w_p[:, w, a, 64 * t : 64 * (t + 1)].bitcast(U8).bitcast(FP4X4),
-                            lhsT_scale=planes8[:, a, W_S + R * w + P * t : W_S + R * w + P * (t + 1)],
-                            rhs=tab_p[c // 4][:, a, 2 * CH * (c % 4) : 2 * CH * (c % 4 + 1)].bitcast(FP4X4),
-                            rhs_scale=planes8[:, a, CH * c : CH * (c + 1)],
-                            start=(a == 0),
-                            stop=(a == 1),
-                        )
-                nc.scalar.copy(ab[c][:, w], bank[:].rearrange("p t j -> p j t"))
-
-        def relation(c, wq):
-            codes, scales = wq
-            bank = ps_cd.tile([P, 4, CH], F32, name="bank_cd")
+        def first_stage(bank, table, table_s, weight, weight_s, width, dtype, passes):
             for t in range(4):
-                nc.tensor.matmul_mx(
-                    out=bank[:, t, :],
-                    lhsT=codes[:, P * t : P * (t + 1)].bitcast(FP8X4),
-                    lhsT_scale=scales[:, P * t : P * (t + 1)],
-                    rhs=tab2_g[:, CH * c : CH * (c + 1)].bitcast(FP8X4),
-                    rhs_scale=plane28[:, CH * c : CH * (c + 1)],
-                    start=True,
-                    stop=True,
+                for a in range(passes):
+                    nc.tensor.matmul_mx(
+                        out=bank[:, CH * t : CH * (t + 1)],
+                        lhsT=weight(a)[:, width * t : width * (t + 1)].bitcast(dtype),
+                        lhsT_scale=weight_s(a)[:, P * t : P * (t + 1)],
+                        rhs=table(a).bitcast(dtype),
+                        rhs_scale=table_s(a),
+                        start=(a == 0),
+                        stop=(a == passes - 1),
+                    )
+            return bank[:].rearrange("p (t j) -> p j t", t=4)
+
+        def entity(c):
+            ab[c] = laid([P, 2, CH, 4], F32, "ab%d" % c, AB_KIB[c])
+            for w in range(2):
+                bank = next_bank("ab", [P, R])
+                sums = first_stage(
+                    bank,
+                    lambda a: tab_p[c][:, a, :],
+                    lambda a: planes8[:, a, CH * c : CH * (c + 1)],
+                    lambda a: w_p[:, w, a, :].bitcast(U8),
+                    lambda a: planes8[:, a, W_S + R * w : W_S + R * (w + 1)],
+                    2 * P, FP4X4, 2,
                 )
-            return bank[:].rearrange("p t j -> p j t")
+                nc.scalar.copy(ab[c][:, w], sums)
+
+        def relation(part, c):
+            wq = wr_q[part]
+            bank = next_bank("ab" if (part, c) == ("r", 0) else "cd", [P, R])
+            cd[part, c] = first_stage(
+                bank,
+                lambda a: tab2_g[c // 4][:, CH * (c % 4) : CH * (c % 4 + 1)],
+                lambda a: plane28[:, CH * c : CH * (c + 1)],
+                lambda a: wq[0][:],
+                lambda a: wq[1][:],
+                P, FP8X4, 1,
+            )
 
         def times_arr(c):
-            arr = relation(c, wrr_q)
-            if c in (2, 5, 6):
-                x = keep.tile([P, 2, CH, 4], F32, name="x%d" % c, tag="then_x%d" % c, align_bytes=64)
+            arr = cd["r", c]
+            if c in X_KIB:
+                x = laid([P, 2, CH, 4], F32, "x%d" % c, X_KIB[c])
             else:
-                x = ring.tile([P, 2, CH, 4], F32, name="x", bufs=4)
-            nc.vector.tensor_tensor(x[:, 0], ab[c][:, 0], arr, MULT)
-            nc.vector.tensor_tensor(x[:, 1], ab[c][:, 1], arr, MULT)
+                x = ring.tile([P, 2, CH, 4], F32, name="x", align_bytes=64)
+            nc.vector.tensor_tensor(x[:], ab[c][:], arr.unsqueeze(1).to_broadcast([P, 2, CH, 4]), MULT)
             xs[c] = x
 
-        def times_ari(c, wri_q):
-            ari = relation(c, wri_q)
-            y = ring.tile([P, 2, CH, 4], F32, name="y")
+        def times_ari(c):
+            ari = cd["i", c]
+            y = ring.tile([P, 2, CH, 4], F32, name="y", align_bytes=64)
             nc.vector.scalar_tensor_tensor(y[:, 0], ab[c][:, 1], -1.0, ari, MULT, MULT)
             nc.vector.tensor_tensor(y[:, 1], ab[c][:, 0], ari, MULT)
             ys[c] = y
 
         def add(c):
-            if c >= NCH - 2:
-                h = keep.tile([P, 2 * CH * 4], BF16, name="h%d" % c, tag="h_last", align_bytes=64)
-            else:
-                h = ring.tile([P, 2 * CH * 4], BF16, name="h", bufs=2, align_bytes=64)
-            eng = nc.vector if c >= NCH - 2 else nc.gpsimd
-            eng.tensor_tensor(
-                h[:], xs[c][:].rearrange("p w j t -> p (w j t)"), ys[c][:].rearrange("p w j t -> p (w j t)"), ADD
+            hs[c] = laid([P, 2 * CH * 4], BF16, "h%d" % c, H_KIB[c])
+            nc.gpsimd.tensor_tensor(
+                hs[c][:], xs[c][:].rearrange("p w j t -> p (w j t)"), ys[c][:].rearrange("p w j t -> p (w j t)"), ADD
             )
-            hs[c] = h
 
         def quant_h(c):
-            codes = keep.tile([P, 2 * CH], U32, name="h_c%d" % c, align_bytes=64)
-            scales = keep.tile([P, 2 * CH], U8, name="h_s%d" % c, align_bytes=64)
-            nc.vector.quantize_mx(out=codes[:].bitcast(FP8X4), scales=scales[:], in_=hs[c][:])
-            hq[c] = (codes, scales)
+            hq[c] = quant(hs[c][:], "h%d" % c, N_KIB[c - 1] if c in (1, 2) else None)
 
-        def score(c, n_q):
+        def score(c):
             codes, scales = hq[c]
-            parts = 2 if c == NCH - 1 else 1
-            step = 4 // parts
-            for m0 in range(0, 4, step):
-                pool = ps_cd if parts == 2 else ps_y
-                bank = pool.tile([P, step, CH], F32, name="bank_cd" if parts == 2 else "bank_y")
-                for m in range(m0, m0 + step):
-                    for w in range(2):
-                        nc.tensor.matmul_mx(
-                            out=bank[:, m - m0, :],
-                            lhsT=n_q[w][0][:, P * m : P * (m + 1)].bitcast(FP8X4),
-                            lhsT_scale=n_q[w][1][:, P * m : P * (m + 1)],
-                            rhs=codes[:, CH * w : CH * (w + 1)].bitcast(FP8X4),
-                            rhs_scale=scales[:, CH * w : CH * (w + 1)],
-                            start=(w == 0),
-                            stop=(w == 1),
-                        )
-                res = ring.tile([P, step, CH], F32, name="res", bufs=5)
-                nc.scalar.activation(res[:], bank[:], SIGMOID)
-                rows = out[P * m0 : P * (m0 + step), CH * c : CH * (c + 1)]
-                nc.sync.dma_start(rows.rearrange("(m p) j -> p m j", p=P), res[:])
+            bank = next_bank("y", [P, 4, CH])
+            for m in range(4):
+                for w in range(2):
+                    cols = slice(CH * w, CH * (w + 1))
+                    score_pass(bank[:, m, :], m, w, codes[:, cols], scales[:, cols], w == 0, w == 1)
+            finish(bank, c, 0, 4)
+
+        def score_pass(dst, m, w, codes, scales, start, stop):
+            nc.tensor.matmul_mx(
+                out=dst,
+                lhsT=n_q[w][0][:, P * m : P * (m + 1)].bitcast(FP8X4),
+                lhsT_scale=n_q[w][1][:, P * m : P * (m + 1)],
+                rhs=codes.bitcast(FP8X4),
+                rhs_scale=scales,
+                start=start,
+                stop=stop,
+            )
+
+        def finish(bank, c, m0, count):
+            res = ring.tile([P, count, CH], F32, name="res", bufs=5)
+            nc.scalar.activation(res[:], bank[:], SIGMOID)
+            rows = out[P * m0 : P * (m0 + count), CH * c : CH * (c + 1)]
+            nc.sync.dma_start(rows.rearrange("(m p) j -> p m j", p=P), res[:])
+
+        def last_chunk(c):
+            halves = []
+            for w in range(2):
+                h = laid([P, CH * 4], BF16, "h_last%d" % w, H_KIB[c - 2 + w])
+                nc.vector.tensor_tensor(
+                    h[:], xs[c][:, w].rearrange("p j t -> p (j t)"), ys[c][:, w].rearrange("p j t -> p (j t)"), ADD
+                )
+                halves.append(h)
+                if w == 0:
+                    quant_h(c - 1)
+                    score(c - 1)
+            banks = [next_bank("cd", [P, 2, CH]) for half in range(2)]
+            for w in range(2):
+                codes, scales = quant(halves[w][:], "h_last%d" % w)
+                for m in range(4):
+                    first, last = (w, m % 2) == (0, 0), (w, m % 2) == (1, 1)
+                    score_pass(banks[m // 2][:, m % 2, :], m, w, codes[:], scales[:], first, last)
+            for half in range(2):
+                finish(banks[half], c, 2 * half, 2)
 
         def cast_cand(w):
-            grouped = keep.tile([P, N, 4], BF16, name="n_g%d" % w, tag="then_x%d" % (5 + w), align_bytes=64)
+            grouped = laid([P, N, 4], BF16, "n_g%d" % w, N_KIB[w])
             for n0 in range(0, N, P):
-                nc.scalar.copy(grouped[:, n0 : n0 + P], n_raw[:, w, :, n0 : n0 + P].rearrange("p t n -> p n t"))
+                nc.scalar.copy(grouped[:, n0 : n0 + P], n_raw[w][:, :, n0 : n0 + P].rearrange("p t n -> p n t"))
             return grouped[:].rearrange("p n t -> p (n t)")
 
-        entity(0)
+        for c in range(2):
+            entity(c)
+        wrr_g = laid([P, 4, P, 4], BF16, "wrr_g", 56)
+        wr_q["r"] = quant(cast_rel(wrr_raw, wrr_g, ("vector",) * 4), "wrr")
         gather_tab2(0)
+        relation("r", 0)
         gather_tab2(1)
-        n_raw = keep.tile([P, 2, 4, N], F32, name="n_raw", tag="then_tab2", align_bytes=64)
-        for w, src in enumerate((nr, ni)):
-            for t in range(4):
-                nc.sync.dma_start(n_raw[:, w, t, :], src.rearrange("(g t i) n -> t g i n", t=4, i=8)[t])
-        wrr_g = cast_rel(wrr_raw, "wrr_g", ("vector", "vector", "vector", "scalar"), "then_ab")
-        wrr_q = quant(wrr_g[:].rearrange("p t m j -> p (t m j)"), "wrr")
-        entity(1)
-        times_arr(0)
         entity(2)
-        wri_g = cast_rel(wri_raw, "wri_g", ("scalar", "scalar", "gpsimd", "gpsimd"), "then_x2")
-        times_arr(1)
+        wri_g = cast_rel(wri_raw, laid([P, 4, P, 4], BF16, "wri_g", 32), ("scalar", "scalar", "gpsimd", "gpsimd"))
+        times_arr(0)
+        wr_q["i"] = quant(wri_g, "wri")
+        relation("i", 0)
+        relation("r", 1)
+        relation("i", 1)
+        part_tab(4, 4, 32)
         entity(3)
-        wri_q = quant(wri_g[:].rearrange("p t m j -> p (t m j)"), "wri")
-        times_arr(2)
-        times_ari(0, wri_q)
-        add(0)
-        entity(4)
-        n_g = [cast_cand(0)]
-        times_arr(3)
-        times_ari(1, wri_q)
-        add(1)
-        entity(5)
-        n_g.append(cast_cand(1))
-        times_arr(4)
+        n_g = []
         n_q = []
-        for c in range(2, 6):
-            times_ari(c, wri_q)
-            quant_h(c - 2)
-            if c < 4:
-                n_q.append(quant(n_g[c - 2], "n%d" % (c - 2)))
-            add(c)
+        for c in range(NCH):
+            if c > 0:
+                times_arr(c)
+                if c + 1 < NCH:
+                    relation("i", c + 1)
+            times_ari(c)
+            if c + 2 < NCH:
+                relation("r", c + 2)
+            if c in (3, 4):
+                n_q.append(quant(n_g[c - 3], "n%d" % (c - 3)))
+            for d in range(max(c - 2, 0), c - 1):
+                quant_h(d)
+            if c + 1 < NCH:
+                add(c)
+            if c < 2:
+                n_g.append(cast_cand(c))
             if c + 4 < NCH:
                 entity(c + 4)
-            if c + 3 < NCH:
-                times_arr(c + 3)
-            if c == 3:
-                score(0, n_q)
-            if c >= 3:
-                score(c - 2, n_q)
-        times_ari(6, wri_q)
-        times_ari(7, wri_q)
-        quant_h(4)
-        score(4, n_q)
-        add(6)
-        quant_h(5)
-        score(5, n_q)
-        quant_h(6)
-        score(6, n_q)
-        add(7)
-        quant_h(7)
-        score(7, n_q)
+            for d in {4: (0, 1, 2), 5: (3,), 6: (4,), 7: (5,)}.get(c, ()):
+                score(d)
+        last_chunk(NCH - 1)

@@ -1,6 +1,7 @@
 from contextlib import ExitStack
 
 import concourse.mybir as mybir
+from concourse.masks import make_identity
 
 K, L, R, N, T, J = 1024, 512, 512, 512, 4096, 1024
 FLOPS = 2 * J * (2 * K * R + 2 * L * R + 2 * R * N)
@@ -25,10 +26,13 @@ TAB_ROW, TAB2_ROW = 96, 112
 W_S, PASS_BYTES = J, J + 2 * R
 TAB2_K = 4
 BANKS = {"ab": (0, 3), "cd": (3, 3), "y": (6, 2)}
-H_KIB = (78, 68, 78, 67, 77, 66, 76)
-N_KIB = (84, 88)
+TURNED = (3, 6)
+GROUPS = ((0, 1), (2,), (3, 4), (5,), (6,))
+KIB = {
+    "h0": 64, "h1": 68, "y4": 66, "h2": 70, "h3": 74, "y7": 72, "h4": 76, "h_last1": 76,
+    "n_g0": 84, "h0_c": 84, "n_g1": 88, "h1_c": 88, "y2": 112, "h0_s": 112, "y5": 116, "h2_c": 116,
+}
 AB_KIB = (92, 96, 100, 28, 0, 8, 104, 108)
-X_KIB = {4: 69, 5: 79}
 
 
 def tile_list_ckg_sig_kernel(
@@ -80,6 +84,8 @@ def tile_list_ckg_sig_kernel(
         nc.gpsimd.memset(planes[:], 0)
         nc.gpsimd.memset(tab2_sw[0:TAB2_ROW], 0)
         nc.gpsimd.memset(plane2[:], 0)
+        ident = keep.tile([P, P], F32, name="ident", align_bytes=64)
+        make_identity(nc, ident[:])
 
         tab_sg = laid([P, J], U8, "tab_sg", 39.5)
         nc.vector.tensor_copy(tab_sg[:], tab_sw[:].bitcast(U8).indirect(idx[:]))
@@ -157,13 +163,15 @@ def tile_list_ckg_sig_kernel(
                     nc.gpsimd.tensor_scalar(dst, src, 1.0, 0.0, MULT, ADD)
             return grouped[:].rearrange("p t m j -> p (t m j)")
 
-        def quant(grouped, name, kib=None):
+        def placed(shape, dtype, name):
+            if name in KIB:
+                return laid(shape, dtype, name, KIB[name])
+            return keep.tile(shape, dtype, name=name, align_bytes=64)
+
+        def quant(grouped, name):
             words = grouped.shape[1] // 4
-            if kib is None:
-                codes = keep.tile([P, words], U32, name=name + "_c", align_bytes=64)
-            else:
-                codes = laid([P, words], U32, name + "_c", kib)
-            scales = keep.tile([P, words], U8, name=name + "_s", align_bytes=64)
+            codes = placed([P, words], U32, name + "_c")
+            scales = placed([P, words], U8, name + "_s")
             nc.vector.quantize_mx(out=codes[:].bitcast(FP8X4), scales=scales[:], in_=grouped)
             return codes, scales
 
@@ -175,7 +183,19 @@ def tile_list_ckg_sig_kernel(
         hs = {}
         hq = {}
 
-        def first_stage(bank, table, table_s, weight, weight_s, width, dtype, passes):
+        def first_stage(bank, c, table, table_s, weight, weight_s, width, dtype, passes):
+            if c in TURNED:
+                for a in range(passes):
+                    nc.tensor.matmul_mx(
+                        out=bank[:],
+                        lhsT=table(a).bitcast(dtype),
+                        lhsT_scale=table_s(a),
+                        rhs=weight(a).bitcast(dtype),
+                        rhs_scale=weight_s(a),
+                        start=(a == 0),
+                        stop=(a == passes - 1),
+                    )
+                return bank[:].rearrange("p (j t) -> p j t", t=4)
             for t in range(4):
                 for a in range(passes):
                     nc.tensor.matmul_mx(
@@ -194,7 +214,7 @@ def tile_list_ckg_sig_kernel(
             for w in range(2):
                 bank = next_bank("ab", [P, R])
                 sums = first_stage(
-                    bank,
+                    bank, c,
                     lambda a: tab_p[c][:, a, :],
                     lambda a: planes8[:, a, CH * c : CH * (c + 1)],
                     lambda a: w_p[:, w, a, :].bitcast(U8),
@@ -207,7 +227,7 @@ def tile_list_ckg_sig_kernel(
             wq = wr_q[part]
             bank = next_bank("ab" if (part, c) == ("r", 0) else "cd", [P, R])
             cd[part, c] = first_stage(
-                bank,
+                bank, c,
                 lambda a: tab2_g[c // 4][:, CH * (c % 4) : CH * (c % 4 + 1)],
                 lambda a: plane28[:, CH * c : CH * (c + 1)],
                 lambda a: wq[0][:],
@@ -217,37 +237,50 @@ def tile_list_ckg_sig_kernel(
 
         def times_arr(c):
             arr = cd["r", c]
-            if c in X_KIB:
-                x = laid([P, 2, CH, 4], F32, "x%d" % c, X_KIB[c])
-            else:
-                x = ring.tile([P, 2, CH, 4], F32, name="x", align_bytes=64)
+            x = ring.tile([P, 2, CH, 4], F32, name="x", bufs=4, align_bytes=64)
             nc.vector.tensor_tensor(x[:], ab[c][:], arr.unsqueeze(1).to_broadcast([P, 2, CH, 4]), MULT)
             xs[c] = x
 
         def times_ari(c):
             ari = cd["i", c]
-            y = ring.tile([P, 2, CH, 4], F32, name="y", align_bytes=64)
+            y = placed([P, 2, CH, 4], F32, "y%d" % c)
             nc.vector.scalar_tensor_tensor(y[:, 0], ab[c][:, 1], -1.0, ari, MULT, MULT)
             nc.vector.tensor_tensor(y[:, 1], ab[c][:, 0], ari, MULT)
             ys[c] = y
 
         def add(c):
-            hs[c] = laid([P, 2 * CH * 4], BF16, "h%d" % c, H_KIB[c])
-            nc.gpsimd.tensor_tensor(
-                hs[c][:], xs[c][:].rearrange("p w j t -> p (w j t)"), ys[c][:].rearrange("p w j t -> p (w j t)"), ADD
-            )
-
-        def quant_h(c):
-            hq[c] = quant(hs[c][:], "h%d" % c, N_KIB[c - 1] if c in (1, 2) else None)
-
-        def score(c):
-            codes, scales = hq[c]
-            bank = next_bank("y", [P, 4, CH])
-            for m in range(4):
+            group = [c in members for members in GROUPS].index(True)
+            if group not in hs:
+                hs[group] = placed([P, 2, CH * len(GROUPS[group]) * 4], BF16, "h%d" % group)
+            place = GROUPS[group].index(c)
+            h = hs[group][:, :, 4 * CH * place : 4 * CH * (place + 1)]
+            x = xs[c][:].rearrange("p w j t -> p w (j t)")
+            y = ys[c][:].rearrange("p w j t -> p w (j t)")
+            if c not in TURNED:
+                nc.gpsimd.tensor_tensor(h, x, y, ADD)
+            else:
                 for w in range(2):
-                    cols = slice(CH * w, CH * (w + 1))
-                    score_pass(bank[:, m, :], m, w, codes[:, cols], scales[:, cols], w == 0, w == 1)
-            finish(bank, c, 0, 4)
+                    bank = next_bank("ab", [P, 4, CH])
+                    for t in range(4):
+                        cols = slice(P * t, P * (t + 1))
+                        nc.tensor.matmul(bank[:, t, :], y[:, w, cols], ident[:], start=True, stop=False, is_transpose=True)
+                        nc.tensor.matmul(bank[:, t, :], x[:, w, cols], ident[:], start=False, stop=True, is_transpose=True)
+                    nc.scalar.copy(h[:, w].rearrange("p (j t) -> p j t", t=4), bank[:].rearrange("p t j -> p j t"))
+
+        def quant_h(group):
+            hq[group] = quant(hs[group][:].rearrange("p w e -> p (w e)"), "h%d" % group)
+
+        def score(group):
+            codes, scales = hq[group]
+            width = CH * len(GROUPS[group])
+            step = R // width
+            for m0 in range(0, 4, step):
+                bank = next_bank("y", [P, step, width])
+                for m in range(m0, m0 + step):
+                    for w in range(2):
+                        cols = slice(width * w, width * (w + 1))
+                        score_pass(bank[:, m - m0, :], m, w, codes[:, cols], scales[:, cols], w == 0, w == 1)
+                finish(bank, CH * GROUPS[group][0], width, m0, step)
 
         def score_pass(dst, m, w, codes, scales, start, stop):
             nc.tensor.matmul_mx(
@@ -260,23 +293,23 @@ def tile_list_ckg_sig_kernel(
                 stop=stop,
             )
 
-        def finish(bank, c, m0, count):
-            res = ring.tile([P, count, CH], F32, name="res", bufs=5)
+        def finish(bank, first, width, m0, count):
+            res = ring.tile([P, count, width], F32, name="res", bufs=5)
             nc.scalar.activation(res[:], bank[:], SIGMOID)
-            rows = out[P * m0 : P * (m0 + count), CH * c : CH * (c + 1)]
+            rows = out[P * m0 : P * (m0 + count), first : first + width]
             nc.sync.dma_start(rows.rearrange("(m p) j -> p m j", p=P), res[:])
 
         def last_chunk(c):
             halves = []
             for w in range(2):
-                h = laid([P, CH * 4], BF16, "h_last%d" % w, H_KIB[c - 2 + w])
+                h = placed([P, CH * 4], BF16, "h_last%d" % w)
                 nc.vector.tensor_tensor(
                     h[:], xs[c][:, w].rearrange("p j t -> p (j t)"), ys[c][:, w].rearrange("p j t -> p (j t)"), ADD
                 )
                 halves.append(h)
                 if w == 0:
-                    quant_h(c - 1)
-                    score(c - 1)
+                    quant_h(len(GROUPS) - 1)
+                    score(len(GROUPS) - 1)
             banks = [next_bank("cd", [P, 2, CH]) for half in range(2)]
             for w in range(2):
                 codes, scales = quant(halves[w][:], "h_last%d" % w)
@@ -284,10 +317,10 @@ def tile_list_ckg_sig_kernel(
                     first, last = (w, m % 2) == (0, 0), (w, m % 2) == (1, 1)
                     score_pass(banks[m // 2][:, m % 2, :], m, w, codes[:], scales[:], first, last)
             for half in range(2):
-                finish(banks[half], c, 2 * half, 2)
+                finish(banks[half], CH * c, CH, 2 * half, 2)
 
         def cast_cand(w):
-            grouped = laid([P, N, 4], BF16, "n_g%d" % w, N_KIB[w])
+            grouped = placed([P, N, 4], BF16, "n_g%d" % w)
             for n0 in range(0, N, P):
                 nc.scalar.copy(grouped[:, n0 : n0 + P], n_raw[w][:, :, n0 : n0 + P].rearrange("p t n -> p n t"))
             return grouped[:].rearrange("p n t -> p (n t)")
@@ -315,19 +348,20 @@ def tile_list_ckg_sig_kernel(
                 times_arr(c)
                 if c + 1 < NCH:
                     relation("i", c + 1)
+            if c == 4:
+                n_q.extend(quant(n_g[w], "n%d" % w) for w in range(2))
+            due = {4: (0, 1), 7: (2, 3)}.get(c, ())
+            for group in due:
+                quant_h(group)
             times_ari(c)
             if c + 2 < NCH:
                 relation("r", c + 2)
-            if c in (3, 4):
-                n_q.append(quant(n_g[c - 3], "n%d" % (c - 3)))
-            for d in range(max(c - 2, 0), c - 1):
-                quant_h(d)
             if c + 1 < NCH:
                 add(c)
             if c < 2:
                 n_g.append(cast_cand(c))
             if c + 4 < NCH:
                 entity(c + 4)
-            for d in {4: (0, 1, 2), 5: (3,), 6: (4,), 7: (5,)}.get(c, ()):
-                score(d)
+            for group in due:
+                score(group)
         last_chunk(NCH - 1)

@@ -27,10 +27,10 @@ W_S, PASS_BYTES = J, J + 2 * R
 TAB2_K = 4
 BANKS = {"ab": (0, 3), "cd": (3, 3), "y": (6, 2)}
 TURNED = (3, 6)
-GROUPS = ((0, 1), (2,), (3, 4), (5,), (6,))
+GROUPS = ((0, 1), (2,), (3,), (4, 5), (6,))
 KIB = {
-    "h0": 64, "h1": 68, "y4": 66, "h2": 70, "h3": 74, "y7": 72, "h4": 76, "h_last1": 76,
-    "n_g0": 84, "h0_c": 84, "n_g1": 88, "h1_c": 88, "y2": 112, "h0_s": 112, "y5": 116, "h2_c": 116,
+    "h0": 64, "h1": 68, "x5": 65, "h3": 69, "h2": 74, "y7": 72, "h4": 76, "h_last1": 76,
+    "n_g0": 84, "h0_c": 84, "n_g1": 88, "h1_c": 88, "y2": 112, "n0_s": 112, "y5": 116, "h2_c": 116,
 }
 AB_KIB = (92, 96, 100, 28, 0, 8, 104, 108)
 
@@ -237,7 +237,7 @@ def tile_list_ckg_sig_kernel(
 
         def times_arr(c):
             arr = cd["r", c]
-            x = ring.tile([P, 2, CH, 4], F32, name="x", bufs=4, align_bytes=64)
+            x = placed([P, 2, CH, 4], F32, "x%d" % c)
             nc.vector.tensor_tensor(x[:], ab[c][:], arr.unsqueeze(1).to_broadcast([P, 2, CH, 4]), MULT)
             xs[c] = x
 
@@ -348,14 +348,17 @@ def tile_list_ckg_sig_kernel(
                 times_arr(c)
                 if c + 1 < NCH:
                     relation("i", c + 1)
-            if c == 4:
-                n_q.extend(quant(n_g[w], "n%d" % w) for w in range(2))
             due = {4: (0, 1), 7: (2, 3)}.get(c, ())
-            for group in due:
-                quant_h(group)
+            if c == 7:
+                for group in due:
+                    quant_h(group)
             times_ari(c)
             if c + 2 < NCH:
                 relation("r", c + 2)
+            if c == 4:
+                n_q.extend(quant(n_g[w], "n%d" % w) for w in range(2))
+                for group in due:
+                    quant_h(group)
             if c + 1 < NCH:
                 add(c)
             if c < 2:

@@ -20,19 +20,20 @@ SIGMOID = mybir.ActivationFunctionType.Sigmoid
 
 P = 128
 CH = 128
-NCH = J // CH
 HALF = 512
-TAB_ROW, TAB2_ROW = 96, 112
+ROW0, ROW1 = 96, 112
 W_S, PASS_BYTES = J, J + 2 * R
-TAB2_K = 4
-BANKS = {"ab": (0, 3), "cd": (3, 3), "y": (6, 2)}
-TURNED = (3, 6)
-GROUPS = ((0, 1), (2,), (3,), (4, 5), (6,))
+TURNED = (2, 3, 4)
+GROUPS = ((0, 1), (2, 3), (4,), (5,), (6,))
 KIB = {
-    "h0": 64, "h1": 68, "x5": 65, "h3": 69, "h2": 74, "y7": 72, "h4": 76, "h_last1": 76,
-    "n_g0": 84, "h0_c": 84, "n_g1": 88, "h1_c": 88, "y2": 112, "n0_s": 112, "y5": 116, "h2_c": 116,
+    "tab_w": 0, "n_raw0": 0, "n_raw1": 8, "ab5": 8, "h1": 12,
+    "n_s": 8, "h0_s": 9, "h1_s": 9.5, "h2_s": 10,
+    "tab2_w": 16, "x0": 16, "y0": 20, "y2": 24, "y3": 28,
+    "w_raw0": 31.75, "tab2_sg": 32,
+    "tab_sg": 80, "w_p0": 80, "wrr_raw": 34, "ab2": 33.75, "ab0": 37.75, "w_sraw": 41.5, "w_raw1": 42, "tab_p0": 42.25, "wri_raw": 43.5, "ab1": 44, "c4": 49,
+    "tab_g0": 76, "tab_g1": 77, "x3": 53, "wri_g": 56, "x2b": 57, "x4": 59,
+    "x7": 62, "h2": 64, "h3": 65.5, "h4": 67, "ab7": 70, "h4_s": 70, "ab6": 84, "h3_s": 84,
 }
-AB_KIB = (92, 96, 100, 28, 0, 8, 104, 108)
 
 
 def tile_list_ckg_sig_kernel(
@@ -42,329 +43,352 @@ def tile_list_ckg_sig_kernel(
     nc = tc.nc
     with ExitStack() as ctx:
         keep = ctx.enter_context(tc.tile_pool(name="keep", bufs=1))
-        ring = ctx.enter_context(tc.tile_pool(name="ring", bufs=3))
+        ring = ctx.enter_context(tc.tile_pool(name="ring", bufs=5))
         lay = ctx.enter_context(tc.tile_pool(name="lay", bufs=1))
         psum = ctx.enter_context(tc.psum_pool(name="psum", bufs=1))
 
-        def laid(shape, dtype, name, kib):
-            return lay.tile(shape, dtype, name=name, align_bytes=64, offset=int(1024 * kib))
+        def sbuf(shape, dtype, name):
+            if name in KIB:
+                return lay.tile(shape, dtype, name=name, align_bytes=64, offset=int(1024 * KIB[name]))
+            return keep.tile(shape, dtype, name=name, align_bytes=64)
 
-        turns = {"ab": 0, "cd": 0, "y": 0}
-
-        def next_bank(kind, shape):
-            first, count = BANKS[kind]
-            turn = turns[kind]
-            turns.update({kind: turn + 1})
-            return psum.tile(shape, F32, name="%s%d" % (kind, turn), offset=2048 * (first + turn % count))
+        def bank(shape, name, number):
+            return psum.tile(shape, F32, name=name, offset=2048 * number)
 
         idx = keep.tile([P, J // 16], U16, name="idx")
         idx2 = keep.tile([P, J // 16], U16, name="idx2")
-        tab_sw = keep.tile([P, T // 4], I32, name="tab_sw", align_bytes=64)
-        tab2_sw = laid([P, T // 4], I32, "tab2_sw", 24)
-        tab_w = laid([P, T], I32, "tab_w", 0)
-        wer_raw = keep.tile([P, 2, R // 2], I32, name="wer_raw", align_bytes=64)
-        wei_raw = keep.tile([P, 2, R // 2], I32, name="wei_raw", align_bytes=64)
-        planes = keep.tile([P, 2, PASS_BYTES // 4], I32, name="planes", align_bytes=64)
-        plane2 = keep.tile([P, J // 4], I32, name="plane2", align_bytes=64)
-        joined = keep.tile([P, PASS_BYTES // 4], I32, name="joined", align_bytes=64)
-        w_sraw = keep.tile([P, 2, R // 4], I32, name="w_sraw", align_bytes=64)
-        w_p = keep.tile([P, 2, 2, R // 2], I32, name="w_p", align_bytes=64)
+        tab_sw = sbuf([P, T // 4], I32, "tab_sw")
+        tab2_sw = sbuf([P, T // 4], I32, "tab2_sw")
+        tab_w = sbuf([P, T], I32, "tab_w")
+        w_raw = [sbuf([P, 2, R // 2], I32, "w_raw%d" % w) for w in range(2)]
+        w_sraw = sbuf([P, 2, R // 4], I32, "w_sraw")
+        planes = [sbuf([P, PASS_BYTES // 4], I32, "plane%d" % a) for a in range(2)]
+        plane2 = sbuf([P, J // 4], I32, "plane2")
+        joined = sbuf([P, PASS_BYTES // 4], I32, "joined")
 
         nc.sync.dma_start(idx[:], offs)
-        nc.sync.dma_start(tab_sw[TAB_ROW:P], tab_scales.bitcast(I32).rearrange("a q c -> (a q) c"))
+        nc.sync.dma_start(tab_sw[ROW0:P], tab_scales.bitcast(I32).rearrange("a q c -> (a q) c"))
         for w, src in enumerate((wer_scales, wei_scales)):
-            nc.sync.dma_start(w_sraw[TAB_ROW:P, w], src.bitcast(I32).rearrange("a q c -> (a q) c"))
+            nc.sync.dma_start(w_sraw[ROW0:P, w], src.bitcast(I32).rearrange("a q c -> (a q) c"))
         nc.sync.dma_start(idx2[:], offs2)
-        nc.sync.dma_start(tab2_sw[TAB2_ROW : TAB2_ROW + 16, :], tab2_scales.bitcast(I32)[0])
+        nc.sync.dma_start(tab2_sw[ROW1:P], tab2_scales.bitcast(I32)[0])
+        nc.sync.dma_start(w_raw[0][:], wer_words.bitcast(I32).rearrange("a p c -> p a c"))
         nc.sync.dma_start(tab_w[:], tab_words[0].rearrange("p t b -> p (t b)").bitcast(I32))
-        nc.sync.dma_start(wer_raw[:], wer_words.bitcast(I32).rearrange("a p c -> p a c"))
-        nc.sync.dma_start(wei_raw[:], wei_words.bitcast(I32).rearrange("a p c -> p a c"))
 
-        nc.vector.memset(tab_sw[0:TAB_ROW], 0)
-        nc.gpsimd.memset(planes[:], 0)
-        nc.gpsimd.memset(tab2_sw[0:TAB2_ROW], 0)
-        nc.gpsimd.memset(plane2[:], 0)
-        ident = keep.tile([P, P], F32, name="ident", align_bytes=64)
+        warm = sbuf([P, 2], F32, "warm")
+        nc.vector.memset(warm[:, 0:1], 0.0)
+        nc.scalar.activation(warm[:, 1:2], warm[:, 0:1], SIGMOID)
+        nc.vector.memset(tab_sw[0:ROW0], 0)
+        nc.gpsimd.memset(tab2_sw[0:ROW1], 0)
+        for a in range(2):
+            nc.vector.memset(planes[a][:], 0)
+        nc.vector.memset(plane2[:], 0)
+        ident = sbuf([P, P], F32, "ident")
         make_identity(nc, ident[:])
 
-        tab_sg = laid([P, J], U8, "tab_sg", 39.5)
-        nc.vector.tensor_copy(tab_sg[:], tab_sw[:].bitcast(U8).indirect(idx[:]))
-        nc.vector.tensor_copy(
-            joined[TAB_ROW:P, W_S // 4 :].rearrange("p (w t g e) -> p w t g e", w=2, t=4, e=2),
-            w_sraw[TAB_ROW:P].rearrange("p w (g t e) -> p w t g e", t=4, e=2),
-        )
-        nc.vector.tensor_copy(joined[TAB_ROW:P, 0 : W_S // 4], tab_sg[TAB_ROW:P].bitcast(I32))
-        tab2_w = laid([P, T], I32, "tab2_w", 40)
-        wrr_raw = laid([P, 4, R], F32, "wrr_raw", 32)
-        for a in range(2):
-            for r in range(4):
-                row = TAB_ROW + 16 * a
-                nc.sync.dma_start(planes[r:P:32, a, :], joined[row + r : row + 16 : 4, :])
-            if a == 0:
-                nc.sync.dma_start(wrr_raw[:], wrr.rearrange("(p j) c -> p j c", j=4))
-        nc.sync.dma_start(tab2_w[:], tab2_words[0].rearrange("p t b -> p (t b)").bitcast(I32))
-        planes8 = planes[:].bitcast(U8)
-        plane28 = plane2[TAB2_K:P, :].bitcast(U8)
+        w_p = {}
 
-        tab_g = [
-            keep.tile([P, HALF], U32, name="tab_g0", align_bytes=64),
-            keep.tile([P, HALF], U32, name="tab_g1", align_bytes=64),
-        ]
-        tab_p = {}
-        tab2_g = [keep.tile([P, HALF], U32, name="tab2_g%d" % h, align_bytes=64) for h in range(2)]
-
-        def gather_tab(h):
-            nc.vector.tensor_copy(tab_g[h][:], tab_w[:].bitcast(U32).indirect(idx[:, h * 32 : (h + 1) * 32]))
-
-        def part_tab(first, count, kib):
-            parted = laid([P, 2, 2 * CH * count], U8, "tab_p%d" % first, kib)
-            cols = slice(CH * (first % 4), CH * (first % 4 + count))
+        def order_columns(w):
+            w_p[w] = sbuf([P, 2, R // 2], I32, "w_p%d" % w)
             nc.vector.tensor_copy(
-                parted[:].bitcast(U16),
-                tab_g[first // 4][:, cols].bitcast(U16).rearrange("p (j a) -> p a j", a=2),
+                w_p[w][:].rearrange("p a (t g e) -> p a t g e", t=4, e=4),
+                w_raw[w][:].rearrange("p a (g t e) -> p a t g e", t=4, e=4),
+            )
+
+        def move_rows(a):
+            row = ROW0 + 16 * a
+            for r in range(4):
+                nc.sync.dma_start(planes[a][r:P:32, :], joined[row + r : row + 16 : 4, :])
+
+        tab_sg = sbuf([P, J], U8, "tab_sg")
+        nc.vector.tensor_copy(tab_sg[:], tab_sw[:].bitcast(U8).indirect(idx[:]))
+        nc.vector.tensor_copy(joined[ROW0:P, 0 : W_S // 4], tab_sg[ROW0:P].bitcast(I32))
+        nc.vector.tensor_copy(
+            joined[ROW0:P, W_S // 4 :].rearrange("p (w t g e) -> p w t g e", w=2, t=4, e=2),
+            w_sraw[ROW0:P].rearrange("p w (g t e) -> p w t g e", t=4, e=2),
+        )
+        wrr_raw = sbuf([P, 4, R], F32, "wrr_raw")
+        wrr_rows = wrr.rearrange("(p j) c -> p j c", j=4)
+        move_rows(0)
+        nc.sync.dma_start(w_raw[1][:], wei_words.bitcast(I32).rearrange("a p c -> p a c"))
+        nc.sync.dma_start(wrr_raw[:, 0:2], wrr_rows[:, 0:2])
+        move_rows(1)
+        nc.sync.dma_start(wrr_raw[:, 2:4], wrr_rows[:, 2:4])
+        order_columns(0)
+        tab2_w = sbuf([P, T], I32, "tab2_w")
+        nc.sync.dma_start(tab2_w[:], tab2_words[0].rearrange("p t b -> p (t b)").bitcast(I32))
+        tab2_sg = sbuf([P, J], U8, "tab2_sg")
+        nc.vector.tensor_copy(tab2_sg[:], tab2_sw[:].bitcast(U8).indirect(idx2[:]))
+        for r in range(4):
+            nc.sync.dma_start(plane2[r:P:32, :], tab2_sg[ROW1 + r : P : 4, :].bitcast(I32))
+        planes8 = [planes[a][:].bitcast(U8) for a in range(2)]
+
+        tab_g = [sbuf([P, HALF], U32, "tab_g%d" % h) for h in range(2)]
+        tab_p = {}
+        tab2_g = [sbuf([P, HALF], U32, "tab2_g%d" % h) for h in range(2)]
+
+        def gather(dst, window, offsets, h):
+            nc.vector.tensor_copy(dst[h][:], window[:].bitcast(U32).indirect(offsets[:, h * 32 : (h + 1) * 32]))
+
+        def part_tab(first, count):
+            h, cols = first // 4, slice(CH * (first % 4), CH * (first % 4 + count))
+            parted = sbuf([P, 2, 2 * CH * count], U8, "tab_p%d" % first)
+            nc.vector.tensor_copy(
+                parted[:].bitcast(U16), tab_g[h][:, cols].bitcast(U16).rearrange("p (j a) -> p a j", a=2)
             )
             for c in range(count):
                 tab_p[first + c] = parted[:, :, 2 * CH * c : 2 * CH * (c + 1)]
 
-        def gather_tab2(h):
-            nc.vector.tensor_copy(tab2_g[h][:], tab2_w[:].bitcast(U32).indirect(idx2[:, h * 32 : (h + 1) * 32]))
-
-        def order_columns(w, raw):
-            nc.vector.tensor_copy(
-                w_p[:, w].rearrange("p a (t g e) -> p a t g e", t=4, e=4),
-                raw[:].rearrange("p a (g t e) -> p a t g e", t=4, e=4),
-            )
-
-        tab2_sg = keep.tile([P, J], U8, name="tab2_sg", align_bytes=64)
-        nc.vector.tensor_copy(tab2_sg[:], tab2_sw[:].bitcast(U8).indirect(idx2[:]))
-        for r in range(4):
-            nc.sync.dma_start(plane2[TAB2_K + r : P : 32, :], tab2_sg[TAB2_ROW + r : P : 4, :].bitcast(I32))
-        wri_raw = laid([P, 4, R], F32, "wri_raw", 24)
+        gather(tab_g, tab_w, idx, 0)
+        part_tab(2, 1)
+        order_columns(1)
+        wri_raw = sbuf([P, 4, R], F32, "wri_raw")
         nc.sync.dma_start(wri_raw[:], wri.rearrange("(p j) c -> p j c", j=4))
-        gather_tab(0)
-        part_tab(0, 4, 60)
-        order_columns(0, wer_raw)
-        order_columns(1, wei_raw)
-        gather_tab(1)
-        n_raw = [laid([P, 4, N], F32, "n_raw%d" % w, 8 * w) for w in range(2)]
+        part_tab(0, 2)
+        part_tab(3, 1)
+        gather(tab_g, tab_w, idx, 1)
+        part_tab(4, 4)
+        n_raw = [sbuf([P, 4, N], F32, "n_raw%d" % w) for w in range(2)]
         for w, src in enumerate((nr, ni)):
             for t in range(4):
                 nc.sync.dma_start(n_raw[w][:, t, :], src.rearrange("(g t i) n -> t g i n", t=4, i=8)[t])
 
-        def cast_rel(raw, grouped, engines):
+        def cast_rel(raw, name, engines):
+            grouped = sbuf([P, 4, P, 4], BF16, name)
             for t in range(4):
-                dst = grouped[:, t].rearrange("p (g i) j -> p g i j", i=8)
-                src = raw[:].rearrange("p j (g t i) -> p t g i j", t=4, i=8)[:, t]
-                if engines[t] == "scalar":
-                    nc.scalar.copy(dst, src)
-                elif engines[t] == "vector":
-                    nc.vector.tensor_copy(dst, src)
+                if engines[t] != "gpsimd":
+                    dst = grouped[:, t].rearrange("p (g u i) j -> p g u j i", u=2, i=4)
+                    src = raw[:].rearrange("p j (g t u i) -> p t g u j i", t=4, u=2, i=4)[:, t]
+                    if engines[t] == "scalar":
+                        nc.scalar.copy(dst, src)
+                    else:
+                        nc.vector.tensor_copy(dst, src)
                 else:
+                    dst = grouped[:, t].rearrange("p (g i) j -> p g i j", i=8)
+                    src = raw[:].rearrange("p j (g t i) -> p t g i j", t=4, i=8)[:, t]
                     nc.gpsimd.tensor_scalar(dst, src, 1.0, 0.0, MULT, ADD)
             return grouped[:].rearrange("p t m j -> p (t m j)")
 
-        def placed(shape, dtype, name):
-            if name in KIB:
-                return laid(shape, dtype, name, KIB[name])
-            return keep.tile(shape, dtype, name=name, align_bytes=64)
-
         def quant(grouped, name):
             words = grouped.shape[1] // 4
-            codes = placed([P, words], U32, name + "_c")
-            scales = placed([P, words], U8, name + "_s")
+            codes = sbuf([P, words], U32, name + "_c")
+            scales = sbuf([P, words], U8, name + "_s")
             nc.vector.quantize_mx(out=codes[:].bitcast(FP8X4), scales=scales[:], in_=grouped)
             return codes, scales
 
-        ab = {}
-        xs = {}
-        cd = {}
-        wr_q = {}
-        ys = {}
-        hs = {}
-        hq = {}
+        ab, cd, xs, ys, hs, hq, wr_q = {}, {}, {}, {}, {}, {}, {}
 
-        def first_stage(bank, c, table, table_s, weight, weight_s, width, dtype, passes):
+        def first_stage(dst, c, table, table_s, weight, weight_s, width, dtype, passes):
             if c in TURNED:
                 for a in range(passes):
                     nc.tensor.matmul_mx(
-                        out=bank[:],
-                        lhsT=table(a).bitcast(dtype),
-                        lhsT_scale=table_s(a),
-                        rhs=weight(a).bitcast(dtype),
-                        rhs_scale=weight_s(a),
-                        start=(a == 0),
-                        stop=(a == passes - 1),
+                        out=dst[:], lhsT=table(a).bitcast(dtype), lhsT_scale=table_s(a),
+                        rhs=weight(a).bitcast(dtype), rhs_scale=weight_s(a),
+                        start=(a == 0), stop=(a == passes - 1),
                     )
-                return bank[:].rearrange("p (j t) -> p j t", t=4)
+                return dst[:].rearrange("p (j t) -> p j t", t=4)
             for t in range(4):
                 for a in range(passes):
                     nc.tensor.matmul_mx(
-                        out=bank[:, CH * t : CH * (t + 1)],
+                        out=dst[:, CH * t : CH * (t + 1)],
                         lhsT=weight(a)[:, width * t : width * (t + 1)].bitcast(dtype),
                         lhsT_scale=weight_s(a)[:, P * t : P * (t + 1)],
-                        rhs=table(a).bitcast(dtype),
-                        rhs_scale=table_s(a),
-                        start=(a == 0),
-                        stop=(a == passes - 1),
+                        rhs=table(a).bitcast(dtype), rhs_scale=table_s(a),
+                        start=(a == 0), stop=(a == passes - 1),
                     )
-            return bank[:].rearrange("p (t j) -> p j t", t=4)
+            return dst[:].rearrange("p (t j) -> p j t", t=4)
 
-        def entity(c):
-            ab[c] = laid([P, 2, CH, 4], F32, "ab%d" % c, AB_KIB[c])
+        def entity(c, banks):
+            ab[c] = sbuf([P, 2, CH, 4], F32, "ab%d" % c)
             for w in range(2):
-                bank = next_bank("ab", [P, R])
                 sums = first_stage(
-                    bank, c,
+                    bank([P, R], "e%d_%d" % (c, w), banks[w]), c,
                     lambda a: tab_p[c][:, a, :],
-                    lambda a: planes8[:, a, CH * c : CH * (c + 1)],
-                    lambda a: w_p[:, w, a, :].bitcast(U8),
-                    lambda a: planes8[:, a, W_S + R * w : W_S + R * (w + 1)],
+                    lambda a: planes8[a][:, CH * c : CH * (c + 1)],
+                    lambda a: w_p[w][:, a, :].bitcast(U8),
+                    lambda a: planes8[a][:, W_S + R * w : W_S + R * (w + 1)],
                     2 * P, FP4X4, 2,
                 )
                 nc.scalar.copy(ab[c][:, w], sums)
 
-        def relation(part, c):
-            wq = wr_q[part]
-            bank = next_bank("ab" if (part, c) == ("r", 0) else "cd", [P, R])
+        def relation(part, c, number):
+            codes, scales = wr_q[part]
             cd[part, c] = first_stage(
-                bank, c,
+                bank([P, R], "%s%d" % (part, c), number), c,
                 lambda a: tab2_g[c // 4][:, CH * (c % 4) : CH * (c % 4 + 1)],
-                lambda a: plane28[:, CH * c : CH * (c + 1)],
-                lambda a: wq[0][:],
-                lambda a: wq[1][:],
-                P, FP8X4, 1,
+                lambda a: plane2[:].bitcast(U8)[:, CH * c : CH * (c + 1)],
+                lambda a: codes[:], lambda a: scales[:], P, FP8X4, 1,
             )
 
         def times_arr(c):
-            arr = cd["r", c]
-            x = placed([P, 2, CH, 4], F32, "x%d" % c)
-            nc.vector.tensor_tensor(x[:], ab[c][:], arr.unsqueeze(1).to_broadcast([P, 2, CH, 4]), MULT)
-            xs[c] = x
+            x = sbuf([P, 2, CH, 4], F32, "x%d" % c)
+            nc.vector.tensor_tensor(x[:], ab[c][:], cd["r", c].unsqueeze(1).to_broadcast([P, 2, CH, 4]), MULT)
+            xs[c] = x[:].rearrange("p w j t -> p w (j t)")
+
+        def times_arr_half(c, w):
+            x = sbuf([P, CH, 4], F32, "x%d%s" % (c, "ab"[w]))
+            nc.vector.tensor_tensor(x[:], ab[c][:, w], cd["r", c], MULT)
+            xs[c, w] = x[:].rearrange("p j t -> p (j t)")
+
+        def copy_arr(c):
+            arr = sbuf([P, CH, 4], F32, "c%d" % c)
+            nc.scalar.copy(arr[:], cd["r", c])
+            cd["r", c] = arr[:]
+
+        def times_arr_gpsimd(c):
+            x = sbuf([P, 2, CH, 4], F32, "x%d" % c)
+            nc.gpsimd.tensor_tensor(x[:], ab[c][:], cd["r", c].unsqueeze(1).to_broadcast([P, 2, CH, 4]), MULT)
+            xs[c] = x[:].rearrange("p w j t -> p w (j t)")
+
+        def x_of(c, w):
+            return xs[c, w] if (c, w) in xs else xs[c][:, w]
 
         def times_ari(c):
             ari = cd["i", c]
-            y = placed([P, 2, CH, 4], F32, "y%d" % c)
+            y = sbuf([P, 2, CH, 4], F32, "y%d" % c)
             nc.vector.scalar_tensor_tensor(y[:, 0], ab[c][:, 1], -1.0, ari, MULT, MULT)
             nc.vector.tensor_tensor(y[:, 1], ab[c][:, 0], ari, MULT)
-            ys[c] = y
+            ys[c] = y[:].rearrange("p w j t -> p w (j t)")
 
-        def add(c):
+        def h_of(c):
             group = [c in members for members in GROUPS].index(True)
             if group not in hs:
-                hs[group] = placed([P, 2, CH * len(GROUPS[group]) * 4], BF16, "h%d" % group)
+                hs[group] = sbuf([P, 2, CH * len(GROUPS[group]) * 4], BF16, "h%d" % group)
             place = GROUPS[group].index(c)
-            h = hs[group][:, :, 4 * CH * place : 4 * CH * (place + 1)]
-            x = xs[c][:].rearrange("p w j t -> p w (j t)")
-            y = ys[c][:].rearrange("p w j t -> p w (j t)")
-            if c not in TURNED:
-                nc.gpsimd.tensor_tensor(h, x, y, ADD)
-            else:
-                for w in range(2):
-                    bank = next_bank("ab", [P, 4, CH])
-                    for t in range(4):
-                        cols = slice(P * t, P * (t + 1))
-                        nc.tensor.matmul(bank[:, t, :], y[:, w, cols], ident[:], start=True, stop=False, is_transpose=True)
-                        nc.tensor.matmul(bank[:, t, :], x[:, w, cols], ident[:], start=False, stop=True, is_transpose=True)
-                    nc.scalar.copy(h[:, w].rearrange("p (j t) -> p j t", t=4), bank[:].rearrange("p t j -> p j t"))
+            return hs[group][:, :, 4 * CH * place : 4 * CH * (place + 1)]
+
+        def add_gpsimd(c):
+            nc.gpsimd.tensor_tensor(h_of(c), xs[c], ys[c], ADD)
+
+        def add_turned(c, banks):
+            h = h_of(c)
+            for w in range(2):
+                dst = bank([P, 4, CH], "t%d_%d" % (c, w), banks[w])
+                for t in range(4):
+                    cols = slice(P * t, P * (t + 1))
+                    nc.tensor.matmul(dst[:, t, :], ys[c][:, w, cols], ident[:], start=True, stop=False, is_transpose=True)
+                    nc.tensor.matmul(dst[:, t, :], x_of(c, w)[:, cols], ident[:], start=False, stop=True, is_transpose=True)
+                nc.scalar.copy(h[:, w].rearrange("p (j t) -> p j t", t=4), dst[:].rearrange("p t j -> p j t"))
 
         def quant_h(group):
             hq[group] = quant(hs[group][:].rearrange("p w e -> p (w e)"), "h%d" % group)
 
-        def score(group):
+        def score_pass(dst, m, w, codes, scales, start, stop):
+            cols = slice(N * w + P * m, N * w + P * (m + 1))
+            nc.tensor.matmul_mx(
+                out=dst, lhsT=n_q[0][:, cols].bitcast(FP8X4), lhsT_scale=n_q[1][:, cols],
+                rhs=codes.bitcast(FP8X4), rhs_scale=scales, start=start, stop=stop,
+            )
+
+        def finish(sums, first, width, m0, count):
+            res = ring.tile([P, count, width], F32, name="res")
+            nc.scalar.activation(res[:], sums[:], SIGMOID)
+            rows = out[P * m0 : P * (m0 + count), first : first + width]
+            nc.sync.dma_start(rows.rearrange("(m p) j -> p m j", p=P), res[:])
+
+        def score(group, banks):
             codes, scales = hq[group]
             width = CH * len(GROUPS[group])
             step = R // width
             for m0 in range(0, 4, step):
-                bank = next_bank("y", [P, step, width])
+                sums = bank([P, step, width], "s%d_%d" % (group, m0), banks[m0 // step])
                 for m in range(m0, m0 + step):
                     for w in range(2):
                         cols = slice(width * w, width * (w + 1))
-                        score_pass(bank[:, m - m0, :], m, w, codes[:, cols], scales[:, cols], w == 0, w == 1)
-                finish(bank, CH * GROUPS[group][0], width, m0, step)
+                        score_pass(sums[:, m - m0, :], m, w, codes[:, cols], scales[:, cols], w == 0, w == 1)
+                finish(sums, CH * GROUPS[group][0], width, m0, step)
 
-        def score_pass(dst, m, w, codes, scales, start, stop):
-            nc.tensor.matmul_mx(
-                out=dst,
-                lhsT=n_q[w][0][:, P * m : P * (m + 1)].bitcast(FP8X4),
-                lhsT_scale=n_q[w][1][:, P * m : P * (m + 1)],
-                rhs=codes.bitcast(FP8X4),
-                rhs_scale=scales,
-                start=start,
-                stop=stop,
-            )
-
-        def finish(bank, first, width, m0, count):
-            res = ring.tile([P, count, width], F32, name="res", bufs=5)
-            nc.scalar.activation(res[:], bank[:], SIGMOID)
-            rows = out[P * m0 : P * (m0 + count), first : first + width]
-            nc.sync.dma_start(rows.rearrange("(m p) j -> p m j", p=P), res[:])
-
-        def last_chunk(c):
+        def last_chunk(c, group, group_banks, banks):
             halves = []
             for w in range(2):
-                h = placed([P, CH * 4], BF16, "h_last%d" % w)
-                nc.vector.tensor_tensor(
-                    h[:], xs[c][:, w].rearrange("p j t -> p (j t)"), ys[c][:, w].rearrange("p j t -> p (j t)"), ADD
-                )
+                h = sbuf([P, CH * 4], BF16, "h_last%d" % w)
+                nc.vector.tensor_tensor(h[:], xs[c][:, w], ys[c][:, w], ADD)
                 halves.append(h)
                 if w == 0:
-                    quant_h(len(GROUPS) - 1)
-                    score(len(GROUPS) - 1)
-            banks = [next_bank("cd", [P, 2, CH]) for half in range(2)]
+                    quant_h(group)
+                    score(group, group_banks)
+            sums = [bank([P, 2, CH], "last%d" % half, banks[half]) for half in range(2)]
             for w in range(2):
                 codes, scales = quant(halves[w][:], "h_last%d" % w)
                 for m in range(4):
                     first, last = (w, m % 2) == (0, 0), (w, m % 2) == (1, 1)
-                    score_pass(banks[m // 2][:, m % 2, :], m, w, codes[:], scales[:], first, last)
+                    score_pass(sums[m // 2][:, m % 2, :], m, w, codes[:], scales[:], first, last)
             for half in range(2):
-                finish(banks[half], CH * c, CH, 2 * half, 2)
+                finish(sums[half], CH * c, CH, 2 * half, 2)
+
+        n_g = sbuf([P, 2, N, 4], BF16, "n_g")
 
         def cast_cand(w):
-            grouped = placed([P, N, 4], BF16, "n_g%d" % w)
-            for n0 in range(0, N, P):
-                nc.scalar.copy(grouped[:, n0 : n0 + P], n_raw[w][:, :, n0 : n0 + P].rearrange("p t n -> p n t"))
-            return grouped[:].rearrange("p n t -> p (n t)")
+            for n0 in range(0, N, 2 * P):
+                nc.scalar.copy(
+                    n_g[:, w, n0 : n0 + 2 * P].rearrange("p (c i) t -> p c t i", i=4),
+                    n_raw[w][:, :, n0 : n0 + 2 * P].rearrange("p t (c i) -> p c t i", i=4),
+                )
 
-        for c in range(2):
-            entity(c)
-        wrr_g = laid([P, 4, P, 4], BF16, "wrr_g", 56)
-        wr_q["r"] = quant(cast_rel(wrr_raw, wrr_g, ("vector",) * 4), "wrr")
-        gather_tab2(0)
-        relation("r", 0)
-        gather_tab2(1)
-        entity(2)
-        wri_g = cast_rel(wri_raw, laid([P, 4, P, 4], BF16, "wri_g", 32), ("scalar", "scalar", "gpsimd", "gpsimd"))
+        wrr_g = cast_rel(wrr_raw, "wrr_g", ("scalar", "scalar", "gpsimd", "gpsimd"))
+        entity(2, (0, 1))
+        entity(0, (5, 6))
+        entity(3, (0, 1))
+        entity(4, (5, 6))
+        wr_q["r"] = quant(wrr_g, "wrr")
+        gather(tab2_g, tab2_w, idx2, 0)
+        relation("r", 0, 2)
+        relation("r", 2, 7)
+        relation("r", 3, 3)
+        gather(tab2_g, tab2_w, idx2, 1)
+        relation("r", 4, 4)
+        copy_arr(3)
+        wri_g = cast_rel(wri_raw, "wri_g", ("scalar", "scalar", "gpsimd", "gpsimd"))
+        copy_arr(4)
+        entity(1, (3, 4))
         times_arr(0)
+        times_arr_half(2, 0)
         wr_q["i"] = quant(wri_g, "wri")
-        relation("i", 0)
-        relation("r", 1)
-        relation("i", 1)
-        part_tab(4, 4, 32)
-        entity(3)
-        n_g = []
-        n_q = []
-        for c in range(NCH):
-            if c > 0:
-                times_arr(c)
-                if c + 1 < NCH:
-                    relation("i", c + 1)
-            due = {4: (0, 1), 7: (2, 3)}.get(c, ())
-            if c == 7:
-                for group in due:
-                    quant_h(group)
-            times_ari(c)
-            if c + 2 < NCH:
-                relation("r", c + 2)
-            if c == 4:
-                n_q.extend(quant(n_g[w], "n%d" % w) for w in range(2))
-                for group in due:
-                    quant_h(group)
-            if c + 1 < NCH:
-                add(c)
-            if c < 2:
-                n_g.append(cast_cand(c))
-            if c + 4 < NCH:
-                entity(c + 4)
-            for group in due:
-                score(group)
-        last_chunk(NCH - 1)
+        relation("i", 0, 2)
+        relation("i", 2, 0)
+        times_arr_half(2, 1)
+        times_arr_gpsimd(3)
+        times_arr_gpsimd(4)
+        relation("i", 3, 1)
+        relation("i", 4, 7)
+        cast_cand(0)
+        cast_cand(1)
+        times_ari(0)
+        relation("r", 1, 5)
+        add_gpsimd(0)
+        times_ari(2)
+        relation("i", 1, 6)
+        entity(5, (2, 0))
+        add_turned(2, (3, 4))
+        times_ari(3)
+        relation("r", 5, 1)
+        times_ari(4)
+        relation("i", 5, 7)
+        add_turned(3, (2, 0))
+        times_arr(1)
+        relation("r", 6, 5)
+        add_turned(4, (3, 4))
+        times_ari(1)
+        relation("i", 6, 6)
+        add_gpsimd(1)
+        entity(6, (2, 0))
+        times_arr(5)
+        relation("r", 7, 1)
+        entity(7, (3, 4))
+        times_ari(5)
+        relation("i", 7, 7)
+        n_q = quant(n_g[:].rearrange("p w n t -> p (w n t)"), "n")
+        for group in range(3):
+            quant_h(group)
+        add_gpsimd(5)
+        score(0, (2, 0))
+        times_arr(6)
+        score(1, (3, 4))
+        score(2, (5,))
+        times_ari(6)
+        quant_h(3)
+        add_gpsimd(6)
+        score(3, (6,))
+        times_arr(7)
+        times_ari(7)
+        last_chunk(7, 4, (2,), (3, 4))

@@ -24,15 +24,15 @@ HALF = 512
 ROW0, ROW1 = 96, 112
 W_S, PASS_BYTES = J, J + 2 * R
 TURNED = (2, 3, 4)
-GROUPS = ((0, 1), (2, 3), (4,), (5,), (6,))
+GROUPS = ((0, 1), (2, 3), (4, 5), (6,))
 KIB = {
-    "tab_w": 0, "n_raw0": 0, "n_raw1": 8, "ab5": 8, "h1": 12,
-    "n_s": 8, "h0_s": 9, "h1_s": 9.5, "h2_s": 10,
+    "tab_w": 0, "n_raw0": 0, "n_raw1": 8, "h1": 12,
+    "ab6": 84, "n_s": 84, "h0_s": 85, "h1_s": 85.5, "h2_s": 86,
     "tab2_w": 16, "x0": 16, "y0": 20, "y2": 24, "y3": 28,
     "w_raw0": 31.75, "tab2_sg": 32,
     "tab_sg": 80, "w_p0": 80, "wrr_raw": 34, "ab2": 33.75, "ab0": 37.75, "w_sraw": 41.5, "w_raw1": 42, "tab_p0": 42.25, "wri_raw": 43.5, "ab1": 44, "c4": 49,
     "tab_g0": 76, "tab_g1": 77, "x3": 53, "wri_g": 56, "x2b": 57, "x4": 59,
-    "x7": 62, "h2": 64, "h3": 65.5, "h4": 67, "ab7": 70, "h4_s": 70, "ab6": 84, "h3_s": 84,
+    "x7": 61, "h2": 64, "h3": 67, "ab7": 70, "h3_s": 70,
 }
 
 
@@ -299,14 +299,13 @@ def tile_list_ckg_sig_kernel(
                 finish(sums, CH * GROUPS[group][0], width, m0, step)
 
         def last_chunk(c, group, group_banks, banks):
+            quant_h(group)
+            score(group, group_banks)
             halves = []
             for w in range(2):
                 h = sbuf([P, CH * 4], BF16, "h_last%d" % w)
                 nc.vector.tensor_tensor(h[:], xs[c][:, w], ys[c][:, w], ADD)
                 halves.append(h)
-                if w == 0:
-                    quant_h(group)
-                    score(group, group_banks)
             sums = [bank([P, 2, CH], "last%d" % half, banks[half]) for half in range(2)]
             for w in range(2):
                 codes, scales = quant(halves[w][:], "h_last%d" % w)
@@ -351,44 +350,42 @@ def tile_list_ckg_sig_kernel(
         times_arr_gpsimd(4)
         relation("i", 3, 1)
         relation("i", 4, 7)
-        cast_cand(0)
-        cast_cand(1)
         times_ari(0)
         relation("r", 1, 5)
         add_gpsimd(0)
         times_ari(2)
         relation("i", 1, 6)
         entity(5, (2, 0))
+        entity(6, (2, 0))
+        cast_cand(0)
+        cast_cand(1)
         add_turned(2, (3, 4))
         times_ari(3)
         relation("r", 5, 1)
         times_ari(4)
         relation("i", 5, 7)
-        add_turned(3, (2, 0))
         times_arr(1)
         relation("r", 6, 5)
-        add_turned(4, (3, 4))
+        add_turned(3, (2, 0))
         times_ari(1)
         relation("i", 6, 6)
         add_gpsimd(1)
-        entity(6, (2, 0))
         times_arr(5)
         relation("r", 7, 1)
-        entity(7, (3, 4))
         times_ari(5)
         relation("i", 7, 7)
+        add_gpsimd(5)
+        add_turned(4, (3, 4))
+        entity(7, (2, 0))
+        times_arr(6)
+        times_ari(6)
         n_q = quant(n_g[:].rearrange("p w n t -> p (w n t)"), "n")
         for group in range(3):
             quant_h(group)
-        add_gpsimd(5)
-        score(0, (2, 0))
-        times_arr(6)
-        score(1, (3, 4))
-        score(2, (5,))
-        times_ari(6)
-        quant_h(3)
         add_gpsimd(6)
-        score(3, (6,))
+        score(0, (5, 6))
+        score(1, (3, 4))
+        score(2, (2, 0))
         times_arr(7)
         times_ari(7)
-        last_chunk(7, 4, (2,), (3, 4))
+        last_chunk(7, 3, (5,), (3, 4))

@@ -20,20 +20,13 @@ SIGMOID = mybir.ActivationFunctionType.Sigmoid
 
 P = 128
 CH = 128
-HALF = 512
+PIECES = (256, 768)
 ROW0, ROW1 = 96, 112
-W_S, PASS_BYTES = J, J + 2 * R
-TURNED = (2, 3, 4)
-GROUPS = ((0, 1), (2, 3), (4, 5), (6,))
-KIB = {
-    "tab_w": 0, "n_raw0": 0, "n_raw1": 8, "h1": 12,
-    "ab6": 84, "n_s": 84, "h0_s": 85, "h1_s": 85.5, "h2_s": 86,
-    "tab2_w": 16, "x0": 16, "y0": 20, "y2": 24, "y3": 28,
-    "w_raw0": 31.75, "tab2_sg": 32,
-    "tab_sg": 80, "w_p0": 80, "wrr_raw": 34, "ab2": 33.75, "ab0": 37.75, "w_sraw": 41.5, "w_raw1": 42, "tab_p0": 42.25, "wri_raw": 43.5, "ab1": 44, "c4": 49,
-    "tab_g0": 76, "tab_g1": 77, "x3": 53, "wri_g": 56, "x2b": 57, "x4": 59,
-    "x7": 61, "h2": 64, "h3": 67, "ab7": 70, "h3_s": 70,
-}
+PASS_BYTES = J + 2 * R
+AHEAD = (0, 1, 4, 2)
+TURNED = (1, 2, 4, 7)
+TIMES_ON_GPSIMD = (1, 2)
+PAIRS = ((0, 1), (2, 3), (4, 5))
 
 
 def tile_list_ckg_sig_kernel(
@@ -42,25 +35,39 @@ def tile_list_ckg_sig_kernel(
 ):
     nc = tc.nc
     with ExitStack() as ctx:
-        keep = ctx.enter_context(tc.tile_pool(name="keep", bufs=1))
-        ring = ctx.enter_context(tc.tile_pool(name="ring", bufs=5))
+        lists = ctx.enter_context(tc.tile_pool(name="lists", bufs=1))
+        ring = ctx.enter_context(tc.tile_pool(name="ring", bufs=4))
         lay = ctx.enter_context(tc.tile_pool(name="lay", bufs=1))
         psum = ctx.enter_context(tc.psum_pool(name="psum", bufs=1))
 
-        def sbuf(shape, dtype, name):
-            if name in KIB:
-                return lay.tile(shape, dtype, name=name, align_bytes=64, offset=int(1024 * KIB[name]))
-            return keep.tile(shape, dtype, name=name, align_bytes=64)
+        width = {F32: 4, I32: 4, U32: 4, BF16: 2, U8: 1}
+        place = {"free": 0}
 
-        def bank(shape, name, number):
+        def sbuf(shape, dtype, name, over=None, shift=0, room=0):
+            if over is None:
+                size = width[dtype]
+                for extent in shape[1:]:
+                    size = size * extent
+                place[name] = place["free"]
+                place["free"] = place["free"] + -(-max(size, room) // 64) * 64
+            else:
+                place[name] = place[over] + shift
+            return lay.tile(shape, dtype, name=name, align_bytes=64, offset=place[name])
+
+        banks = []
+
+        def bank(shape, name):
+            taken = len(banks)
+            banks.append(name)
+            number = taken % 4 if taken < 2 * len(AHEAD) else (taken - 4) % 8
             return psum.tile(shape, F32, name=name, offset=2048 * number)
 
-        idx = keep.tile([P, J // 16], U16, name="idx")
-        idx2 = keep.tile([P, J // 16], U16, name="idx2")
+        idx = lists.tile([P, J // 16], U16, name="idx")
+        idx2 = lists.tile([P, J // 16], U16, name="idx2")
         tab_sw = sbuf([P, T // 4], I32, "tab_sw")
-        tab2_sw = sbuf([P, T // 4], I32, "tab2_sw")
+        tab2_sw = sbuf([P, T // 4], I32, "tab2_sw", room=4 * T)
         tab_w = sbuf([P, T], I32, "tab_w")
-        w_raw = [sbuf([P, 2, R // 2], I32, "w_raw%d" % w) for w in range(2)]
+        w_raw = [sbuf([P, 2, R // 2], I32, "w_raw%d" % w, room=8192 * (1 - w)) for w in range(2)]
         w_sraw = sbuf([P, 2, R // 4], I32, "w_sraw")
         planes = [sbuf([P, PASS_BYTES // 4], I32, "plane%d" % a) for a in range(2)]
         plane2 = sbuf([P, J // 4], I32, "plane2")
@@ -72,8 +79,9 @@ def tile_list_ckg_sig_kernel(
             nc.sync.dma_start(w_sraw[ROW0:P, w], src.bitcast(I32).rearrange("a q c -> (a q) c"))
         nc.sync.dma_start(idx2[:], offs2)
         nc.sync.dma_start(tab2_sw[ROW1:P], tab2_scales.bitcast(I32)[0])
-        nc.sync.dma_start(w_raw[0][:], wer_words.bitcast(I32).rearrange("a p c -> p a c"))
         nc.sync.dma_start(tab_w[:], tab_words[0].rearrange("p t b -> p (t b)").bitcast(I32))
+        for w, src in enumerate((wer_words, wei_words)):
+            nc.sync.dma_start(w_raw[w][:], src.bitcast(I32).rearrange("a p c -> p a c"))
 
         warm = sbuf([P, 2], F32, "warm")
         nc.vector.memset(warm[:, 0:1], 0.0)
@@ -86,99 +94,61 @@ def tile_list_ckg_sig_kernel(
         ident = sbuf([P, P], F32, "ident")
         make_identity(nc, ident[:])
 
-        w_p = {}
-
-        def order_columns(w):
-            w_p[w] = sbuf([P, 2, R // 2], I32, "w_p%d" % w)
-            nc.vector.tensor_copy(
-                w_p[w][:].rearrange("p a (t g e) -> p a t g e", t=4, e=4),
-                w_raw[w][:].rearrange("p a (g t e) -> p a t g e", t=4, e=4),
-            )
-
-        def move_rows(a):
-            row = ROW0 + 16 * a
-            for r in range(4):
-                nc.sync.dma_start(planes[a][r:P:32, :], joined[row + r : row + 16 : 4, :])
-
-        tab_sg = sbuf([P, J], U8, "tab_sg")
-        nc.vector.tensor_copy(tab_sg[:], tab_sw[:].bitcast(U8).indirect(idx[:]))
-        nc.vector.tensor_copy(joined[ROW0:P, 0 : W_S // 4], tab_sg[ROW0:P].bitcast(I32))
-        nc.vector.tensor_copy(
-            joined[ROW0:P, W_S // 4 :].rearrange("p (w t g e) -> p w t g e", w=2, t=4, e=2),
-            w_sraw[ROW0:P].rearrange("p w (g t e) -> p w t g e", t=4, e=2),
+        nc.scalar.copy(
+            joined[ROW0:P, J // 4 :].bitcast(U32).rearrange("p (w t g e) -> p w t g e", w=2, t=4, e=2),
+            w_sraw[ROW0:P].bitcast(U32).rearrange("p w (g t e) -> p w t g e", t=4, e=2),
         )
-        wrr_raw = sbuf([P, 4, R], F32, "wrr_raw")
+        tab_sg = sbuf([P, J], U8, "tab_sg", room=8192)
+        nc.vector.tensor_copy(tab_sg[:], tab_sw[:].bitcast(U8).indirect(idx[:]))
+        nc.vector.tensor_copy(joined[ROW0:P, 0 : J // 4], tab_sg[ROW0:P].bitcast(I32))
+
+        def move_rows(plane, rows, first):
+            for r in range(4):
+                nc.sync.dma_start(plane[r:P:32, :], rows[first + r : first + 16 : 4, :])
+
+        wrr_raw = sbuf([P, 4, R], F32, "wrr_raw", over="tab_sg")
         wrr_rows = wrr.rearrange("(p j) c -> p j c", j=4)
-        move_rows(0)
-        nc.sync.dma_start(w_raw[1][:], wei_words.bitcast(I32).rearrange("a p c -> p a c"))
-        nc.sync.dma_start(wrr_raw[:, 0:2], wrr_rows[:, 0:2])
-        move_rows(1)
-        nc.sync.dma_start(wrr_raw[:, 2:4], wrr_rows[:, 2:4])
-        order_columns(0)
-        tab2_w = sbuf([P, T], I32, "tab2_w")
-        nc.sync.dma_start(tab2_w[:], tab2_words[0].rearrange("p t b -> p (t b)").bitcast(I32))
-        tab2_sg = sbuf([P, J], U8, "tab2_sg")
-        nc.vector.tensor_copy(tab2_sg[:], tab2_sw[:].bitcast(U8).indirect(idx2[:]))
-        for r in range(4):
-            nc.sync.dma_start(plane2[r:P:32, :], tab2_sg[ROW1 + r : P : 4, :].bitcast(I32))
+        for a in range(2):
+            move_rows(planes[a], joined, ROW0 + 16 * a)
+            rows = (slice(0, 3), slice(3, 4))[a]
+            nc.sync.dma_start(wrr_raw[:, rows], wrr_rows[:, rows])
         planes8 = [planes[a][:].bitcast(U8) for a in range(2)]
 
-        tab_g = [sbuf([P, HALF], U32, "tab_g%d" % h) for h in range(2)]
-        tab_p = {}
-        tab2_g = [sbuf([P, HALF], U32, "tab2_g%d" % h) for h in range(2)]
+        tab2_sg = sbuf([P, J], U8, "tab2_sg")
+        nc.vector.tensor_copy(tab2_sg[:], tab2_sw[:].bitcast(U8).indirect(idx2[:]))
+        tab2_w = sbuf([P, T], I32, "tab2_w", over="tab2_sw")
+        nc.sync.dma_start(tab2_w[:], tab2_words[0].rearrange("p t b -> p (t b)").bitcast(I32))
+        move_rows(plane2, tab2_sg[:].bitcast(I32), ROW1)
 
-        def gather(dst, window, offsets, h):
-            nc.vector.tensor_copy(dst[h][:], window[:].bitcast(U32).indirect(offsets[:, h * 32 : (h + 1) * 32]))
-
-        def part_tab(first, count):
-            h, cols = first // 4, slice(CH * (first % 4), CH * (first % 4 + count))
-            parted = sbuf([P, 2, 2 * CH * count], U8, "tab_p%d" % first)
-            nc.vector.tensor_copy(
-                parted[:].bitcast(U16), tab_g[h][:, cols].bitcast(U16).rearrange("p (j a) -> p a j", a=2)
+        w_p = []
+        for w in range(2):
+            w_p.append(sbuf([P, 2, R // 2], I32, "w_p%d" % w))
+            nc.scalar.copy(
+                w_p[w][:].bitcast(U32).rearrange("p a (t g e) -> p a t g e", t=4, e=4),
+                w_raw[w][:].bitcast(U32).rearrange("p a (g t e) -> p a t g e", t=4, e=4),
             )
-            for c in range(count):
-                tab_p[first + c] = parted[:, :, 2 * CH * c : 2 * CH * (c + 1)]
-
-        gather(tab_g, tab_w, idx, 0)
-        part_tab(2, 1)
-        order_columns(1)
-        wri_raw = sbuf([P, 4, R], F32, "wri_raw")
+        wri_raw = sbuf([P, 4, R], F32, "wri_raw", over="w_raw0")
         nc.sync.dma_start(wri_raw[:], wri.rearrange("(p j) c -> p j c", j=4))
-        part_tab(0, 2)
-        part_tab(3, 1)
-        gather(tab_g, tab_w, idx, 1)
-        part_tab(4, 4)
-        n_raw = [sbuf([P, 4, N], F32, "n_raw%d" % w) for w in range(2)]
+
+        tab_p = {}
+        first = 0
+        for piece, size in enumerate(PIECES):
+            words = sbuf([P, size], U32, "tab_g%d" % piece, over="tab_g0" if piece else None, room=8192)
+            nc.vector.tensor_copy(words[:], tab_w[:].bitcast(U32).indirect(idx[:, first // 16 : (first + size) // 16]))
+            parted = sbuf([P, 2, 2 * size], U8, "tab_p%d" % piece)
+            nc.vector.tensor_copy(parted[:].bitcast(U16), words[:].bitcast(U16).rearrange("p (j a) -> p a j", a=2))
+            for c in range(size // CH):
+                tab_p[first // CH + c] = parted[:, :, 2 * CH * c : 2 * CH * (c + 1)]
+            first = first + size
+
+        n_raw = [sbuf([P, 4, N], F32, "n_raw%d" % w, over=("tab_w", "tab_g0")[w]) for w in range(2)]
         for w, src in enumerate((nr, ni)):
             for t in range(4):
                 nc.sync.dma_start(n_raw[w][:, t, :], src.rearrange("(g t i) n -> t g i n", t=4, i=8)[t])
 
-        def cast_rel(raw, name, engines):
-            grouped = sbuf([P, 4, P, 4], BF16, name)
-            for t in range(4):
-                if engines[t] != "gpsimd":
-                    dst = grouped[:, t].rearrange("p (g u i) j -> p g u j i", u=2, i=4)
-                    src = raw[:].rearrange("p j (g t u i) -> p t g u j i", t=4, u=2, i=4)[:, t]
-                    if engines[t] == "scalar":
-                        nc.scalar.copy(dst, src)
-                    else:
-                        nc.vector.tensor_copy(dst, src)
-                else:
-                    dst = grouped[:, t].rearrange("p (g i) j -> p g i j", i=8)
-                    src = raw[:].rearrange("p j (g t i) -> p t g i j", t=4, i=8)[:, t]
-                    nc.gpsimd.tensor_scalar(dst, src, 1.0, 0.0, MULT, ADD)
-            return grouped[:].rearrange("p t m j -> p (t m j)")
+        ab, rel, xs, ys, hs, hq, wr_q = {}, {}, {}, {}, {}, {}, {}
 
-        def quant(grouped, name):
-            words = grouped.shape[1] // 4
-            codes = sbuf([P, words], U32, name + "_c")
-            scales = sbuf([P, words], U8, name + "_s")
-            nc.vector.quantize_mx(out=codes[:].bitcast(FP8X4), scales=scales[:], in_=grouped)
-            return codes, scales
-
-        ab, cd, xs, ys, hs, hq, wr_q = {}, {}, {}, {}, {}, {}, {}
-
-        def first_stage(dst, c, table, table_s, weight, weight_s, width, dtype, passes):
+        def first_stage(dst, c, table, table_s, weight, weight_s, step, dtype, passes):
             if c in TURNED:
                 for a in range(passes):
                     nc.tensor.matmul_mx(
@@ -187,91 +157,86 @@ def tile_list_ckg_sig_kernel(
                         start=(a == 0), stop=(a == passes - 1),
                     )
                 return dst[:].rearrange("p (j t) -> p j t", t=4)
-            for t in range(4):
-                for a in range(passes):
+            for a in range(passes):
+                for t in range(4):
                     nc.tensor.matmul_mx(
                         out=dst[:, CH * t : CH * (t + 1)],
-                        lhsT=weight(a)[:, width * t : width * (t + 1)].bitcast(dtype),
+                        lhsT=weight(a)[:, step * t : step * (t + 1)].bitcast(dtype),
                         lhsT_scale=weight_s(a)[:, P * t : P * (t + 1)],
                         rhs=table(a).bitcast(dtype), rhs_scale=table_s(a),
-                        start=(a == 0), stop=(a == passes - 1),
+                        start=((a, t) == (0, 0)), stop=((a, t) == (passes - 1, 3)),
                     )
             return dst[:].rearrange("p (t j) -> p j t", t=4)
 
-        def entity(c, banks):
-            ab[c] = sbuf([P, 2, CH, 4], F32, "ab%d" % c)
+        def entity(c, over=None, shift=0):
+            ab[c] = sbuf([P, 2, CH, 4], F32, "ab%d" % c, over, shift, room=8192 if c == 4 else 0)
             for w in range(2):
                 sums = first_stage(
-                    bank([P, R], "e%d_%d" % (c, w), banks[w]), c,
+                    bank([P, R], "e%d_%d" % (c, w)), c,
                     lambda a: tab_p[c][:, a, :],
                     lambda a: planes8[a][:, CH * c : CH * (c + 1)],
                     lambda a: w_p[w][:, a, :].bitcast(U8),
-                    lambda a: planes8[a][:, W_S + R * w : W_S + R * (w + 1)],
+                    lambda a: planes8[a][:, J + R * w : J + R * (w + 1)],
                     2 * P, FP4X4, 2,
                 )
                 nc.scalar.copy(ab[c][:, w], sums)
 
-        def relation(part, c, number):
+        def relation(part, c):
             codes, scales = wr_q[part]
-            cd[part, c] = first_stage(
-                bank([P, R], "%s%d" % (part, c), number), c,
-                lambda a: tab2_g[c // 4][:, CH * (c % 4) : CH * (c % 4 + 1)],
+            rel[part, c] = first_stage(
+                bank([P, R], "%s%d" % (part, c)), c,
+                lambda a: tab2_g[c],
                 lambda a: plane2[:].bitcast(U8)[:, CH * c : CH * (c + 1)],
                 lambda a: codes[:], lambda a: scales[:], P, FP8X4, 1,
             )
 
-        def times_arr(c):
-            x = sbuf([P, 2, CH, 4], F32, "x%d" % c)
-            nc.vector.tensor_tensor(x[:], ab[c][:], cd["r", c].unsqueeze(1).to_broadcast([P, 2, CH, 4]), MULT)
-            xs[c] = x[:].rearrange("p w j t -> p w (j t)")
+        def quantise(codes, scales, rounded):
+            nc.vector.quantize_mx(out=codes.bitcast(FP8X4), scales=scales, in_=rounded)
 
-        def times_arr_half(c, w):
-            x = sbuf([P, CH, 4], F32, "x%d%s" % (c, "ab"[w]))
-            nc.vector.tensor_tensor(x[:], ab[c][:, w], cd["r", c], MULT)
-            xs[c, w] = x[:].rearrange("p j t -> p (j t)")
+        def round_lines(engine, grouped, raw, slots):
+            for u in range(2):
+                dst = grouped.rearrange("p (t g u i j) -> p u t g j i", g=16, u=2, i=4, j=4)[:, u]
+                src = raw[:].rearrange("p j (g t u i) -> p u t g j i", t=4, u=2, i=4)[:, u, slots]
+                engine(dst, src)
 
-        def copy_arr(c):
-            arr = sbuf([P, CH, 4], F32, "c%d" % c)
-            nc.scalar.copy(arr[:], cd["r", c])
-            cd["r", c] = arr[:]
+        def times_arr(c, engine, x):
+            engine.tensor_tensor(x, ab[c][:], rel["r", c].unsqueeze(1).to_broadcast([P, 2, CH, 4]), MULT)
+            xs[c], xs[c, 0], xs[c, 1] = x, x[:, 0], x[:, 1]
 
-        def times_arr_gpsimd(c):
-            x = sbuf([P, 2, CH, 4], F32, "x%d" % c)
-            nc.gpsimd.tensor_tensor(x[:], ab[c][:], cd["r", c].unsqueeze(1).to_broadcast([P, 2, CH, 4]), MULT)
-            xs[c] = x[:].rearrange("p w j t -> p w (j t)")
+        def times_arr_vector(c):
+            times_arr(c, nc.vector, sbuf([P, 2, CH, 4], F32, "x%d" % c)[:])
 
-        def x_of(c, w):
-            return xs[c, w] if (c, w) in xs else xs[c][:, w]
+        def times_arr_part(c, w, over=None):
+            xs[c, w] = sbuf([P, CH, 4], F32, "x%d_%d" % (c, w), over)[:]
+            nc.vector.tensor_tensor(xs[c, w], ab[c][:, w], rel["r", c], MULT)
 
         def times_ari(c):
-            ari = cd["i", c]
-            y = sbuf([P, 2, CH, 4], F32, "y%d" % c)
-            nc.vector.scalar_tensor_tensor(y[:, 0], ab[c][:, 1], -1.0, ari, MULT, MULT)
-            nc.vector.tensor_tensor(y[:, 1], ab[c][:, 0], ari, MULT)
-            ys[c] = y[:].rearrange("p w j t -> p w (j t)")
-
-        def h_of(c):
-            group = [c in members for members in GROUPS].index(True)
-            if group not in hs:
-                hs[group] = sbuf([P, 2, CH * len(GROUPS[group]) * 4], BF16, "h%d" % group)
-            place = GROUPS[group].index(c)
-            return hs[group][:, :, 4 * CH * place : 4 * CH * (place + 1)]
+            ys[c] = sbuf([P, 2, CH, 4], F32, "y%d" % c)[:]
+            nc.vector.scalar_tensor_tensor(ys[c][:, 0], ab[c][:, 1], -1.0, rel["i", c], MULT, MULT)
+            nc.vector.tensor_tensor(ys[c][:, 1], ab[c][:, 0], rel["i", c], MULT)
 
         def add_gpsimd(c):
-            nc.gpsimd.tensor_tensor(h_of(c), xs[c], ys[c], ADD)
-
-        def add_turned(c, banks):
-            h = h_of(c)
+            x, y = (z[c].rearrange("p w j t -> p w (j t)") for z in (xs, ys))
             for w in range(2):
-                dst = bank([P, 4, CH], "t%d_%d" % (c, w), banks[w])
-                for t in range(4):
-                    cols = slice(P * t, P * (t + 1))
-                    nc.tensor.matmul(dst[:, t, :], ys[c][:, w, cols], ident[:], start=True, stop=False, is_transpose=True)
-                    nc.tensor.matmul(dst[:, t, :], x_of(c, w)[:, cols], ident[:], start=False, stop=True, is_transpose=True)
-                nc.scalar.copy(h[:, w].rearrange("p (j t) -> p j t", t=4), dst[:].rearrange("p t j -> p j t"))
+                nc.gpsimd.tensor_tensor(hs[c][:, w], x[:, w], y[:, w], ADD)
 
-        def quant_h(group):
-            hq[group] = quant(hs[group][:].rearrange("p w e -> p (w e)"), "h%d" % group)
+        def add_turned(c, w):
+            x, y = (z.rearrange("p j t -> p (j t)") for z in (xs[c, w], ys[c][:, w]))
+            dst = bank([P, 4, CH], "t%d_%d" % (c, w))
+            for k, term in enumerate((x, y)):
+                for t in range(4):
+                    nc.tensor.matmul(
+                        dst[:, t, :], term[:, P * t : P * (t + 1)], ident[:], is_transpose=True,
+                        start=((k, t) == (0, 0)), stop=((k, t) == (1, 3)),
+                    )
+            nc.scalar.copy(hs[c][:, w].rearrange("p (j t) -> p j t", t=4), dst[:].rearrange("p t j -> p j t"))
+
+        def round_candidates(w):
+            for n0 in range(0, N, 2 * P):
+                nc.scalar.copy(
+                    n_g[:, w, n0 : n0 + 2 * P].rearrange("p (c i) t -> p c t i", i=4),
+                    n_raw[w][:, :, n0 : n0 + 2 * P].rearrange("p t (c i) -> p c t i", i=4),
+                )
 
         def score_pass(dst, m, w, codes, scales, start, stop):
             cols = slice(N * w + P * m, N * w + P * (m + 1))
@@ -280,112 +245,142 @@ def tile_list_ckg_sig_kernel(
                 rhs=codes.bitcast(FP8X4), rhs_scale=scales, start=start, stop=stop,
             )
 
-        def finish(sums, first, width, m0, count):
-            res = ring.tile([P, count, width], F32, name="res")
+        def finish(sums, first, count, m0, rows):
+            res = ring.tile([P, rows, count], F32, name="res")
             nc.scalar.activation(res[:], sums[:], SIGMOID)
-            rows = out[P * m0 : P * (m0 + count), first : first + width]
-            nc.sync.dma_start(rows.rearrange("(m p) j -> p m j", p=P), res[:])
+            dst = out[P * m0 : P * (m0 + rows), first : first + count]
+            nc.sync.dma_start(dst.rearrange("(m p) j -> p m j", p=P), res[:])
 
-        def score(group, banks):
-            codes, scales = hq[group]
-            width = CH * len(GROUPS[group])
-            step = R // width
-            for m0 in range(0, 4, step):
-                sums = bank([P, step, width], "s%d_%d" % (group, m0), banks[m0 // step])
-                for m in range(m0, m0 + step):
+        def score(codes, scales, first, count):
+            rows = R // count
+            for m0 in range(0, 4, rows):
+                sums = bank([P, rows, count], "s%d_%d" % (first, m0))
+                for m in range(rows):
                     for w in range(2):
-                        cols = slice(width * w, width * (w + 1))
-                        score_pass(sums[:, m - m0, :], m, w, codes[:, cols], scales[:, cols], w == 0, w == 1)
-                finish(sums, CH * GROUPS[group][0], width, m0, step)
+                        cols = slice(count * w, count * (w + 1))
+                        score_pass(sums[:, m, :], m0 + m, w, codes[:, cols], scales[:, cols], w == 0, w == 1)
+                finish(sums, first, count, m0, rows)
 
-        def last_chunk(c, group, group_banks, banks):
-            quant_h(group)
-            score(group, group_banks)
-            halves = []
-            for w in range(2):
-                h = sbuf([P, CH * 4], BF16, "h_last%d" % w)
-                nc.vector.tensor_tensor(h[:], xs[c][:, w], ys[c][:, w], ADD)
-                halves.append(h)
-            sums = [bank([P, 2, CH], "last%d" % half, banks[half]) for half in range(2)]
-            for w in range(2):
-                codes, scales = quant(halves[w][:], "h_last%d" % w)
-                for m in range(4):
-                    first, last = (w, m % 2) == (0, 0), (w, m % 2) == (1, 1)
-                    score_pass(sums[m // 2][:, m % 2, :], m, w, codes[:], scales[:], first, last)
-            for half in range(2):
-                finish(sums[half], CH * c, CH, 2 * half, 2)
+        for c in AHEAD:
+            entity(c)
+
+        wrr_g = sbuf([P, 4 * R], BF16, "wrr_g")
+        round_lines(nc.vector.tensor_copy, wrr_g[:], wrr_raw, slice(0, 4))
+        wr_q["r"] = sbuf([P, R], U32, "wrr_c"), sbuf([P, R], U8, "wrr_s")
+        quantise(wr_q["r"][0][:], wr_q["r"][1][:], wrr_g[:])
+        tab2_g = {}
+        first = 0
+        for piece, size in enumerate(PIECES):
+            words = sbuf([P, size], U32, "tab2_g%d" % piece)
+            nc.vector.tensor_copy(words[:], tab2_w[:].bitcast(U32).indirect(idx2[:, first // 16 : (first + size) // 16]))
+            for c in range(size // CH):
+                tab2_g[first // CH + c] = words[:, CH * c : CH * (c + 1)]
+            first = first + size
+        for c in (0, 1, 2, 4):
+            relation("r", c)
+
+        wri_g = sbuf([P, 4 * R], BF16, "wri_g", room=10240)
+        round_lines(nc.scalar.copy, wri_g[:, 0 : 2 * R], wri_raw, slice(0, 2))
+        for t in (2, 3):
+            nc.gpsimd.tensor_scalar(
+                wri_g[:].rearrange("p (t g i j) -> p t g i j", g=16, i=8, j=4)[:, t],
+                wri_raw[:].rearrange("p j (g t i) -> p t g i j", t=4, i=8)[:, t],
+                1.0, 0.0, MULT, ADD,
+            )
+        for k, c in enumerate(TIMES_ON_GPSIMD):
+            arr = sbuf([P, CH, 4], F32, "arr%d" % c, over="wri_raw", shift=2048 * k)
+            nc.scalar.copy(arr[:], rel["r", c])
+            rel["r", c] = arr[:]
+        times_arr_vector(0)
+        times_arr_part(4, 0)
+        wr_q["i"] = sbuf([P, R], U32, "wri_c"), sbuf([P, R], U8, "wri_s")
+        quantise(wr_q["i"][0][:], wr_q["i"][1][:], wri_g[:])
+        for c in (0, 1, 2):
+            relation("i", c)
+        relation("r", 3)
+        times_arr_part(4, 1, over="wri_g")
+        x_gpsimd = sbuf([P, 2, 2, CH, 4], F32, "x_gpsimd", over="wri_g", shift=2048)
+        for k, c in enumerate(TIMES_ON_GPSIMD):
+            times_arr(c, nc.gpsimd, x_gpsimd[:, k])
+        entity(3, "wri_raw", 4096)
+        relation("i", 3)
 
         n_g = sbuf([P, 2, N, 4], BF16, "n_g")
+        pair_h = [sbuf([P, 2, 2 * R], BF16, "h%d" % k) for k in range(2)]
 
-        def cast_cand(w):
-            for n0 in range(0, N, 2 * P):
-                nc.scalar.copy(
-                    n_g[:, w, n0 : n0 + 2 * P].rearrange("p (c i) t -> p c t i", i=4),
-                    n_raw[w][:, :, n0 : n0 + 2 * P].rearrange("p t (c i) -> p c t i", i=4),
-                )
+        def open_pair(k):
+            for place_in_pair, c in enumerate(PAIRS[k]):
+                hs[c] = pair_h[k][:, :, R * place_in_pair : R * (place_in_pair + 1)]
 
-        wrr_g = cast_rel(wrr_raw, "wrr_g", ("scalar", "scalar", "gpsimd", "gpsimd"))
-        entity(2, (0, 1))
-        entity(0, (5, 6))
-        entity(3, (0, 1))
-        entity(4, (5, 6))
-        wr_q["r"] = quant(wrr_g, "wrr")
-        gather(tab2_g, tab2_w, idx2, 0)
-        relation("r", 0, 2)
-        relation("r", 2, 7)
-        relation("r", 3, 3)
-        gather(tab2_g, tab2_w, idx2, 1)
-        relation("r", 4, 4)
-        copy_arr(3)
-        wri_g = cast_rel(wri_raw, "wri_g", ("scalar", "scalar", "gpsimd", "gpsimd"))
-        copy_arr(4)
-        entity(1, (3, 4))
-        times_arr(0)
-        times_arr_half(2, 0)
-        wr_q["i"] = quant(wri_g, "wri")
-        relation("i", 0, 2)
-        relation("i", 2, 0)
-        times_arr_half(2, 1)
-        times_arr_gpsimd(3)
-        times_arr_gpsimd(4)
-        relation("i", 3, 1)
-        relation("i", 4, 7)
+        open_pair(0)
+        open_pair(1)
         times_ari(0)
-        relation("r", 1, 5)
+        entity(5)
+        round_candidates(0)
+        times_ari(1)
         add_gpsimd(0)
         times_ari(2)
-        relation("i", 1, 6)
-        entity(5, (2, 0))
-        entity(6, (2, 0))
-        cast_cand(0)
-        cast_cand(1)
-        add_turned(2, (3, 4))
+        for w in range(2):
+            add_turned(1, w)
+        times_arr_vector(3)
+        relation("r", 5)
+        relation("i", 5)
         times_ari(3)
-        relation("r", 5, 1)
-        times_ari(4)
-        relation("i", 5, 7)
-        times_arr(1)
-        relation("r", 6, 5)
-        add_turned(3, (2, 0))
-        times_ari(1)
-        relation("i", 6, 6)
-        add_gpsimd(1)
-        times_arr(5)
-        relation("r", 7, 1)
+        add_gpsimd(3)
+        round_candidates(1)
+        for w in range(2):
+            add_turned(2, w)
+        relation("i", 4)
+        entity(6)
+        relation("r", 6)
+        times_arr_vector(5)
+        relation("i", 6)
         times_ari(5)
-        relation("i", 7, 7)
+        times_ari(4)
+
+        codes = sbuf([P, 2 * N + 8 * CH], U32, "codes", over="ab4")
+        scales = sbuf([P, 2 * N + 8 * CH], U8, "scales")
+        n_q = codes[:, 0 : 2 * N], scales[:, 0 : 2 * N]
+        quantise(*n_q, n_g[:].rearrange("p w n t -> p (w n t)"))
+        for k in range(2):
+            cols = slice(2 * N + 4 * CH * k, 2 * N + 4 * CH * (k + 1))
+            hq[k] = codes[:, cols], scales[:, cols]
+            quantise(*hq[k], pair_h[k][:].rearrange("p w e -> p (w e)"))
+        wide = sbuf([P, 8 * N + 8 * R], BF16, "h2", over="n_g")
+        pair_h.append(wide[:, 0 : 4 * R].rearrange("p (w e) -> p w e", w=2))
+        open_pair(2)
         add_gpsimd(5)
-        add_turned(4, (3, 4))
-        entity(7, (2, 0))
-        times_arr(6)
+        for w in range(2):
+            add_turned(4, w)
+        entity(7)
+        score(*hq[0], 0, 2 * CH)
+        times_arr_vector(6)
+        relation("r", 7)
         times_ari(6)
-        n_q = quant(n_g[:].rearrange("p w n t -> p (w n t)"), "n")
-        for group in range(3):
-            quant_h(group)
+        relation("i", 7)
+        score(*hq[1], 2 * CH, 2 * CH)
+
+        codes, scales = sbuf([P, 4 * CH], U32, "h2_c", over="ab6"), sbuf([P, 4 * CH], U8, "h2_s")
+        quantise(codes[:], scales[:], wide[:, 0 : 4 * R])
+        h6 = sbuf([P, 2 * R], BF16, "h6", over="h2")
+        hs[6] = h6[:].rearrange("p (w e) -> p w e", w=2)
         add_gpsimd(6)
-        score(0, (5, 6))
-        score(1, (3, 4))
-        score(2, (2, 0))
-        times_arr(7)
+        score(codes, scales, 4 * CH, 2 * CH)
+        times_arr_vector(7)
         times_ari(7)
-        last_chunk(7, 3, (5,), (3, 4))
+
+        hs[7] = sbuf([P, 2, R], BF16, "h7")[:]
+        for w in range(2):
+            add_turned(7, w)
+        codes, scales = sbuf([P, 2 * CH], U32, "h6_c"), sbuf([P, 2 * CH], U8, "h6_s")
+        quantise(codes[:], scales[:], h6[:])
+        score(codes, scales, CH * 6, CH)
+        sums = [bank([P, 2, CH], "last%d" % half) for half in range(2)]
+        for w in range(2):
+            codes, scales = sbuf([P, CH], U32, "last_c%d" % w), sbuf([P, CH], U8, "last_s%d" % w)
+            quantise(codes[:], scales[:], hs[7][:, w])
+            for m in range(4):
+                start, stop = (w, m % 2) == (0, 0), (w, m % 2) == (1, 1)
+                score_pass(sums[m // 2][:, m % 2, :], m, w, codes[:], scales[:], start, stop)
+        for half in range(2):
+            finish(sums[half], CH * 7, CH, 2 * half, 2)

@@ -23,9 +23,9 @@ CH = 128
 PIECES = (256, 768)
 ROW0, ROW1 = 96, 112
 PASS_BYTES = J + 2 * R
-AHEAD = (0, 1, 4, 2)
-TURNED = (1, 2, 4, 7)
-TIMES_ON_GPSIMD = (1, 2)
+AHEAD = (0, 1, 2, 4)
+TURNED = (0, 1, 4)
+TIMES_ON_GPSIMD = (0, 1)
 PAIRS = ((0, 1), (2, 3), (4, 5))
 
 
@@ -36,7 +36,7 @@ def tile_list_ckg_sig_kernel(
     nc = tc.nc
     with ExitStack() as ctx:
         lists = ctx.enter_context(tc.tile_pool(name="lists", bufs=1))
-        ring = ctx.enter_context(tc.tile_pool(name="ring", bufs=4))
+        ring = ctx.enter_context(tc.tile_pool(name="ring", bufs=9))
         lay = ctx.enter_context(tc.tile_pool(name="lay", bufs=1))
         psum = ctx.enter_context(tc.psum_pool(name="psum", bufs=1))
 
@@ -169,7 +169,7 @@ def tile_list_ckg_sig_kernel(
             return dst[:].rearrange("p (t j) -> p j t", t=4)
 
         def entity(c, over=None, shift=0):
-            ab[c] = sbuf([P, 2, CH, 4], F32, "ab%d" % c, over, shift, room=8192 if c == 4 else 0)
+            ab[c] = sbuf([P, 2, CH, 4], F32, "ab%d" % c, over, shift, room=10240 if c == 6 else 0)
             for w in range(2):
                 sums = first_stage(
                     bank([P, R], "e%d_%d" % (c, w)), c,
@@ -217,8 +217,7 @@ def tile_list_ckg_sig_kernel(
 
         def add_gpsimd(c):
             x, y = (z[c].rearrange("p w j t -> p w (j t)") for z in (xs, ys))
-            for w in range(2):
-                nc.gpsimd.tensor_tensor(hs[c][:, w], x[:, w], y[:, w], ADD)
+            nc.gpsimd.tensor_tensor(hs[c], x, y, ADD)
 
         def add_turned(c, w):
             x, y = (z.rearrange("p j t -> p (j t)") for z in (xs[c, w], ys[c][:, w]))
@@ -261,22 +260,20 @@ def tile_list_ckg_sig_kernel(
                         score_pass(sums[:, m, :], m0 + m, w, codes[:, cols], scales[:, cols], w == 0, w == 1)
                 finish(sums, first, count, m0, rows)
 
-        for c in AHEAD:
-            entity(c)
-
         wrr_g = sbuf([P, 4 * R], BF16, "wrr_g")
-        round_lines(nc.vector.tensor_copy, wrr_g[:], wrr_raw, slice(0, 4))
+        round_lines(nc.scalar.copy, wrr_g[:], wrr_raw, slice(0, 4))
+        for k, c in enumerate(AHEAD):
+            entity(c, "wrr_raw" if k < 2 else None, 4096 * k)
+
         wr_q["r"] = sbuf([P, R], U32, "wrr_c"), sbuf([P, R], U8, "wrr_s")
         quantise(wr_q["r"][0][:], wr_q["r"][1][:], wrr_g[:])
         tab2_g = {}
-        first = 0
-        for piece, size in enumerate(PIECES):
-            words = sbuf([P, size], U32, "tab2_g%d" % piece)
-            nc.vector.tensor_copy(words[:], tab2_w[:].bitcast(U32).indirect(idx2[:, first // 16 : (first + size) // 16]))
-            for c in range(size // CH):
-                tab2_g[first // CH + c] = words[:, CH * c : CH * (c + 1)]
-            first = first + size
-        for c in (0, 1, 2, 4):
+        for half in range(2):
+            words = sbuf([P, J // 2], U32, "tab2_g%d" % half)
+            nc.vector.tensor_copy(words[:], tab2_w[:].bitcast(U32).indirect(idx2[:, 32 * half : 32 * (half + 1)]))
+            for c in range(4):
+                tab2_g[4 * half + c] = words[:, CH * c : CH * (c + 1)]
+        for c in (2, 0, 1, 4):
             relation("r", c)
 
         wri_g = sbuf([P, 4 * R], BF16, "wri_g", room=10240)
@@ -291,11 +288,11 @@ def tile_list_ckg_sig_kernel(
             arr = sbuf([P, CH, 4], F32, "arr%d" % c, over="wri_raw", shift=2048 * k)
             nc.scalar.copy(arr[:], rel["r", c])
             rel["r", c] = arr[:]
-        times_arr_vector(0)
+        times_arr_vector(2)
         times_arr_part(4, 0)
         wr_q["i"] = sbuf([P, R], U32, "wri_c"), sbuf([P, R], U8, "wri_s")
         quantise(wr_q["i"][0][:], wr_q["i"][1][:], wri_g[:])
-        for c in (0, 1, 2):
+        for c in (2, 0, 1):
             relation("i", c)
         relation("r", 3)
         times_arr_part(4, 1, over="wri_g")
@@ -306,79 +303,70 @@ def tile_list_ckg_sig_kernel(
         relation("i", 3)
 
         n_g = sbuf([P, 2, N, 4], BF16, "n_g")
-        pair_h = [sbuf([P, 2, 2 * R], BF16, "h%d" % k) for k in range(2)]
-
-        def open_pair(k):
-            for place_in_pair, c in enumerate(PAIRS[k]):
+        pair_h = [sbuf([P, 2, 2 * R], BF16, "h%d" % k) for k in range(len(PAIRS))]
+        for k, pair in enumerate(PAIRS):
+            for place_in_pair, c in enumerate(pair):
                 hs[c] = pair_h[k][:, :, R * place_in_pair : R * (place_in_pair + 1)]
 
-        open_pair(0)
-        open_pair(1)
-        times_ari(0)
+        times_ari(2)
         entity(5)
         round_candidates(0)
-        times_ari(1)
-        add_gpsimd(0)
-        times_ari(2)
-        for w in range(2):
-            add_turned(1, w)
-        times_arr_vector(3)
+        times_ari(0)
+        add_gpsimd(2)
         relation("r", 5)
+        times_ari(1)
         relation("i", 5)
+        times_arr_vector(3)
+        for w in range(2):
+            add_turned(0, w)
+        relation("i", 4)
         times_ari(3)
         add_gpsimd(3)
-        round_candidates(1)
-        for w in range(2):
-            add_turned(2, w)
-        relation("i", 4)
         entity(6)
-        relation("r", 6)
+        round_candidates(1)
         times_arr_vector(5)
-        relation("i", 6)
+        for w in range(2):
+            add_turned(1, w)
         times_ari(5)
-        times_ari(4)
-
-        codes = sbuf([P, 2 * N + 8 * CH], U32, "codes", over="ab4")
-        scales = sbuf([P, 2 * N + 8 * CH], U8, "scales")
-        n_q = codes[:, 0 : 2 * N], scales[:, 0 : 2 * N]
-        quantise(*n_q, n_g[:].rearrange("p w n t -> p (w n t)"))
-        for k in range(2):
-            cols = slice(2 * N + 4 * CH * k, 2 * N + 4 * CH * (k + 1))
-            hq[k] = codes[:, cols], scales[:, cols]
-            quantise(*hq[k], pair_h[k][:].rearrange("p w e -> p (w e)"))
-        wide = sbuf([P, 8 * N + 8 * R], BF16, "h2", over="n_g")
-        pair_h.append(wide[:, 0 : 4 * R].rearrange("p (w e) -> p w e", w=2))
-        open_pair(2)
         add_gpsimd(5)
+        relation("r", 6)
+        relation("i", 6)
+        times_ari(4)
         for w in range(2):
             add_turned(4, w)
         entity(7)
-        score(*hq[0], 0, 2 * CH)
         times_arr_vector(6)
         relation("r", 7)
         times_ari(6)
         relation("i", 7)
-        score(*hq[1], 2 * CH, 2 * CH)
 
-        codes, scales = sbuf([P, 4 * CH], U32, "h2_c", over="ab6"), sbuf([P, 4 * CH], U8, "h2_s")
-        quantise(codes[:], scales[:], wide[:, 0 : 4 * R])
-        h6 = sbuf([P, 2 * R], BF16, "h6", over="h2")
-        hs[6] = h6[:].rearrange("p (w e) -> p w e", w=2)
+        codes = sbuf([P, 2 * N + 4 * CH * len(PAIRS)], U32, "codes", over="ab6")
+        scales = sbuf([P, 2 * N + 4 * CH * len(PAIRS)], U8, "scales")
+        n_q = codes[:, 0 : 2 * N], scales[:, 0 : 2 * N]
+        quantise(*n_q, n_g[:].rearrange("p w n t -> p (w n t)"))
+        for k in range(len(PAIRS)):
+            cols = slice(2 * N + 4 * CH * k, 2 * N + 4 * CH * (k + 1))
+            hq[k] = codes[:, cols], scales[:, cols]
+            quantise(*hq[k], pair_h[k][:].rearrange("p w e -> p (w e)"))
+        h6 = sbuf([P, 8 * N + 4 * R * len(PAIRS)], BF16, "h6", over="n_g")[:, 0 : 2 * R]
+        hs[6] = h6.rearrange("p (w e) -> p w e", w=2)
         add_gpsimd(6)
-        score(codes, scales, 4 * CH, 2 * CH)
+        for k, pair in enumerate(PAIRS):
+            score(*hq[k], CH * pair[0], 2 * CH)
         times_arr_vector(7)
         times_ari(7)
 
-        hs[7] = sbuf([P, 2, R], BF16, "h7")[:]
-        for w in range(2):
-            add_turned(7, w)
         codes, scales = sbuf([P, 2 * CH], U32, "h6_c"), sbuf([P, 2 * CH], U8, "h6_s")
-        quantise(codes[:], scales[:], h6[:])
+        quantise(codes[:], scales[:], h6)
         score(codes, scales, CH * 6, CH)
+        halves = []
+        for w in range(2):
+            halves.append(sbuf([P, CH, 4], BF16, "h7_%d" % w))
+            nc.vector.tensor_tensor(halves[w][:], xs[7, w], ys[7][:, w], ADD)
         sums = [bank([P, 2, CH], "last%d" % half) for half in range(2)]
         for w in range(2):
             codes, scales = sbuf([P, CH], U32, "last_c%d" % w), sbuf([P, CH], U8, "last_s%d" % w)
-            quantise(codes[:], scales[:], hs[7][:, w])
+            quantise(codes[:], scales[:], halves[w][:].rearrange("p j t -> p (j t)"))
             for m in range(4):
                 start, stop = (w, m % 2) == (0, 0), (w, m % 2) == (1, 1)
                 score_pass(sums[m // 2][:, m % 2, :], m, w, codes[:], scales[:], start, stop)

@@ -20,7 +20,7 @@ SIGMOID = mybir.ActivationFunctionType.Sigmoid
 
 P = 128
 CH = 128
-PIECES = (256, 768)
+LEAD = 256
 ROW0, ROW1 = 96, 112
 PASS_BYTES = J + 2 * R
 AHEAD = (0, 1, 2, 4)
@@ -65,9 +65,9 @@ def tile_list_ckg_sig_kernel(
         idx = lists.tile([P, J // 16], U16, name="idx")
         idx2 = lists.tile([P, J // 16], U16, name="idx2")
         tab_sw = sbuf([P, T // 4], I32, "tab_sw")
-        tab2_sw = sbuf([P, T // 4], I32, "tab2_sw", room=4 * T)
+        tab2_sw = sbuf([P, T // 4], I32, "tab2_sw", room=8192)
         tab_w = sbuf([P, T], I32, "tab_w")
-        w_raw = [sbuf([P, 2, R // 2], I32, "w_raw%d" % w, room=8192 * (1 - w)) for w in range(2)]
+        w_raw = [sbuf([P, 2, R // 2], I32, "w_raw%d" % w, room=4 * T * (1 - w)) for w in range(2)]
         w_sraw = sbuf([P, 2, R // 4], I32, "w_sraw")
         planes = [sbuf([P, PASS_BYTES // 4], I32, "plane%d" % a) for a in range(2)]
         plane2 = sbuf([P, J // 4], I32, "plane2")
@@ -114,12 +114,6 @@ def tile_list_ckg_sig_kernel(
             nc.sync.dma_start(wrr_raw[:, rows], wrr_rows[:, rows])
         planes8 = [planes[a][:].bitcast(U8) for a in range(2)]
 
-        tab2_sg = sbuf([P, J], U8, "tab2_sg")
-        nc.vector.tensor_copy(tab2_sg[:], tab2_sw[:].bitcast(U8).indirect(idx2[:]))
-        tab2_w = sbuf([P, T], I32, "tab2_w", over="tab2_sw")
-        nc.sync.dma_start(tab2_w[:], tab2_words[0].rearrange("p t b -> p (t b)").bitcast(I32))
-        move_rows(plane2, tab2_sg[:].bitcast(I32), ROW1)
-
         w_p = []
         for w in range(2):
             w_p.append(sbuf([P, 2, R // 2], I32, "w_p%d" % w))
@@ -127,21 +121,28 @@ def tile_list_ckg_sig_kernel(
                 w_p[w][:].bitcast(U32).rearrange("p a (t g e) -> p a t g e", t=4, e=4),
                 w_raw[w][:].bitcast(U32).rearrange("p a (g t e) -> p a t g e", t=4, e=4),
             )
-        wri_raw = sbuf([P, 4, R], F32, "wri_raw", over="w_raw0")
-        nc.sync.dma_start(wri_raw[:], wri.rearrange("(p j) c -> p j c", j=4))
+        tab2_w = sbuf([P, T], I32, "tab2_w", over="w_raw0")
+        nc.sync.dma_start(tab2_w[:], tab2_words[0].rearrange("p t b -> p (t b)").bitcast(I32))
 
         tab_p = {}
-        first = 0
-        for piece, size in enumerate(PIECES):
-            words = sbuf([P, size], U32, "tab_g%d" % piece, over="tab_g0" if piece else None, room=8192)
-            nc.vector.tensor_copy(words[:], tab_w[:].bitcast(U32).indirect(idx[:, first // 16 : (first + size) // 16]))
-            parted = sbuf([P, 2, 2 * size], U8, "tab_p%d" % piece)
-            nc.vector.tensor_copy(parted[:].bitcast(U16), words[:].bitcast(U16).rearrange("p (j a) -> p a j", a=2))
+
+        def gather_tab(words, first):
+            size = words.shape[1]
+            nc.vector.tensor_copy(words, tab_w[:].bitcast(U32).indirect(idx[:, first // 16 : (first + size) // 16]))
+            parted = sbuf([P, 2, 2 * size], U8, "tab_p%d" % first)
+            nc.vector.tensor_copy(parted[:].bitcast(U16), words.bitcast(U16).rearrange("p (j a) -> p a j", a=2))
             for c in range(size // CH):
                 tab_p[first // CH + c] = parted[:, :, 2 * CH * c : 2 * CH * (c + 1)]
-            first = first + size
 
-        n_raw = [sbuf([P, 4, N], F32, "n_raw%d" % w, over=("tab_w", "tab_g0")[w]) for w in range(2)]
+        gather_tab(sbuf([P, 2 * LEAD], U32, "tab_g0", room=4 * LEAD + 8192)[:, 0:LEAD], 0)
+        tab2_sg = sbuf([P, J], U8, "tab2_sg", over="tab_g0")
+        nc.vector.tensor_copy(tab2_sg[:], tab2_sw[:].bitcast(U8).indirect(idx2[:]))
+        move_rows(plane2, tab2_sg[:].bitcast(I32), ROW1)
+        wri_raw = sbuf([P, 4, R], F32, "wri_raw", over="tab2_sw")
+        nc.sync.dma_start(wri_raw[:], wri.rearrange("(p j) c -> p j c", j=4))
+        gather_tab(sbuf([P, J - LEAD], U32, "tab_g1", over="tab_g0", shift=4 * LEAD)[:], LEAD)
+
+        n_raw = [sbuf([P, 4, N], F32, "n_raw%d" % w, over=("tab_w", "tab_g1")[w]) for w in range(2)]
         for w, src in enumerate((nr, ni)):
             for t in range(4):
                 nc.sync.dma_start(n_raw[w][:, t, :], src.rearrange("(g t i) n -> t g i n", t=4, i=8)[t])

@@ -21,6 +21,7 @@ SIGMOID = mybir.ActivationFunctionType.Sigmoid
 P = 128
 CH = 128
 LEAD = 256
+SPLIT = 320
 ROW0, ROW1 = 96, 112
 PASS_BYTES = J + 2 * R
 AHEAD = (0, 1, 2, 4)
@@ -57,17 +58,15 @@ def tile_list_ckg_sig_kernel(
         banks = []
 
         def bank(shape, name):
-            taken = len(banks)
             banks.append(name)
-            number = taken % 4 if taken < 2 * len(AHEAD) else (taken - 4) % 8
-            return psum.tile(shape, F32, name=name, offset=2048 * number)
+            return psum.tile(shape, F32, name=name, offset=2048 * ((len(banks) - 1) % 8))
 
         idx = lists.tile([P, J // 16], U16, name="idx")
         idx2 = lists.tile([P, J // 16], U16, name="idx2")
         tab_sw = sbuf([P, T // 4], I32, "tab_sw")
         tab2_sw = sbuf([P, T // 4], I32, "tab2_sw", room=8192)
         tab_w = sbuf([P, T], I32, "tab_w")
-        w_raw = [sbuf([P, 2, R // 2], I32, "w_raw%d" % w, room=4 * T * (1 - w)) for w in range(2)]
+        wer_raw = sbuf([P, 2, R // 2], I32, "wer_raw", room=4 * T)
         w_sraw = sbuf([P, 2, R // 4], I32, "w_sraw")
         planes = [sbuf([P, PASS_BYTES // 4], I32, "plane%d" % a) for a in range(2)]
         plane2 = sbuf([P, J // 4], I32, "plane2")
@@ -80,8 +79,7 @@ def tile_list_ckg_sig_kernel(
         nc.sync.dma_start(idx2[:], offs2)
         nc.sync.dma_start(tab2_sw[ROW1:P], tab2_scales.bitcast(I32)[0])
         nc.sync.dma_start(tab_w[:], tab_words[0].rearrange("p t b -> p (t b)").bitcast(I32))
-        for w, src in enumerate((wer_words, wei_words)):
-            nc.sync.dma_start(w_raw[w][:], src.bitcast(I32).rearrange("a p c -> p a c"))
+        nc.sync.dma_start(wer_raw[:], wer_words.bitcast(I32).rearrange("a p c -> p a c"))
 
         warm = sbuf([P, 2], F32, "warm")
         nc.vector.memset(warm[:, 0:1], 0.0)
@@ -98,20 +96,24 @@ def tile_list_ckg_sig_kernel(
             joined[ROW0:P, J // 4 :].bitcast(U32).rearrange("p (w t g e) -> p w t g e", w=2, t=4, e=2),
             w_sraw[ROW0:P].bitcast(U32).rearrange("p w (g t e) -> p w t g e", t=4, e=2),
         )
-        tab_sg = sbuf([P, J], U8, "tab_sg", room=8192)
-        nc.vector.tensor_copy(tab_sg[:], tab_sw[:].bitcast(U8).indirect(idx[:]))
+        tab_sg = sbuf([P, 12 * J], U8, "tab_sg", room=16384)[:, 0:J]
+        nc.vector.tensor_copy(tab_sg, tab_sw[:].bitcast(U8).indirect(idx[:]))
         nc.vector.tensor_copy(joined[ROW0:P, 0 : J // 4], tab_sg[ROW0:P].bitcast(I32))
 
         def move_rows(plane, rows, first):
             for r in range(4):
                 nc.sync.dma_start(plane[r:P:32, :], rows[first + r : first + 16 : 4, :])
 
-        wrr_raw = sbuf([P, 4, R], F32, "wrr_raw", over="tab_sg")
+        wei_raw = sbuf([P, 2, R // 2], I32, "wei_raw", over="tab_sg")
+        wrr_left = sbuf([P, 4, SPLIT], F32, "wrr_left", over="tab_sg", shift=2048)
+        wrr_right = sbuf([P, 4, R - SPLIT], F32, "wrr_right", over="tab_sg", shift=2048 + 8192)
         wrr_rows = wrr.rearrange("(p j) c -> p j c", j=4)
-        for a in range(2):
-            move_rows(planes[a], joined, ROW0 + 16 * a)
-            rows = (slice(0, 3), slice(3, 4))[a]
-            nc.sync.dma_start(wrr_raw[:, rows], wrr_rows[:, rows])
+        move_rows(planes[0], joined, ROW0)
+        nc.sync.dma_start(wei_raw[:], wei_words.bitcast(I32).rearrange("a p c -> p a c"))
+        nc.sync.dma_start(wrr_left[:], wrr_rows[:, :, 0:SPLIT])
+        move_rows(planes[1], joined, ROW0 + 16)
+        nc.sync.dma_start(wrr_right[:], wrr_rows[:, :, SPLIT:])
+        w_raw = wer_raw, wei_raw
         planes8 = [planes[a][:].bitcast(U8) for a in range(2)]
 
         w_p = []
@@ -121,26 +123,37 @@ def tile_list_ckg_sig_kernel(
                 w_p[w][:].bitcast(U32).rearrange("p a (t g e) -> p a t g e", t=4, e=4),
                 w_raw[w][:].bitcast(U32).rearrange("p a (g t e) -> p a t g e", t=4, e=4),
             )
-        tab2_w = sbuf([P, T], I32, "tab2_w", over="w_raw0")
+        tab2_w = sbuf([P, T], I32, "tab2_w", over="wer_raw")
         nc.sync.dma_start(tab2_w[:], tab2_words[0].rearrange("p t b -> p (t b)").bitcast(I32))
 
         tab_p = {}
 
-        def gather_tab(words, first):
+        def gather_tab(words, first, part):
             size = words.shape[1]
             nc.vector.tensor_copy(words, tab_w[:].bitcast(U32).indirect(idx[:, first // 16 : (first + size) // 16]))
-            parted = sbuf([P, 2, 2 * size], U8, "tab_p%d" % first)
-            nc.vector.tensor_copy(parted[:].bitcast(U16), words.bitcast(U16).rearrange("p (j a) -> p a j", a=2))
-            for c in range(size // CH):
-                tab_p[first // CH + c] = parted[:, :, 2 * CH * c : 2 * CH * (c + 1)]
+            for j0 in range(0, size, part):
+                parted = sbuf([P, 2, 2 * part], U8, "tab_p%d" % (first + j0))
+                src = words[:, j0 : j0 + part].bitcast(U16).rearrange("p (j a) -> p a j", a=2)
+                nc.vector.tensor_copy(parted[:].bitcast(U16), src)
+                for c in range(part // CH):
+                    tab_p[(first + j0) // CH + c] = parted[:, :, 2 * CH * c : 2 * CH * (c + 1)]
 
-        gather_tab(sbuf([P, 2 * LEAD], U32, "tab_g0", room=4 * LEAD + 8192)[:, 0:LEAD], 0)
-        tab2_sg = sbuf([P, J], U8, "tab2_sg", over="tab_g0")
-        nc.vector.tensor_copy(tab2_sg[:], tab2_sw[:].bitcast(U8).indirect(idx2[:]))
-        move_rows(plane2, tab2_sg[:].bitcast(I32), ROW1)
+        def gather_tab2_scales(half, over):
+            picked = sbuf([P, J // 2], U8, "tab2_sg%d" % half, over)
+            nc.vector.tensor_copy(picked[:], tab2_sw[:].bitcast(U8).indirect(idx2[:, 32 * half : 32 * (half + 1)]))
+            return picked
+
+        tab2_sg = [gather_tab2_scales(0, None)]
+        gather_tab(sbuf([P, 2 * LEAD], U32, "tab_g0", room=4 * LEAD + 8192)[:, 0:LEAD], 0, CH)
+        tab2_sg.append(gather_tab2_scales(1, "tab_g0"))
+        joined2 = sbuf([P, J // 4], I32, "joined2")
+        for half in range(2):
+            cols = slice(half * J // 8, (half + 1) * J // 8)
+            nc.vector.tensor_copy(joined2[ROW0:P, cols], tab2_sg[half][ROW0:P].bitcast(I32))
+        move_rows(plane2, joined2, ROW1)
         wri_raw = sbuf([P, 4, R], F32, "wri_raw", over="tab2_sw")
         nc.sync.dma_start(wri_raw[:], wri.rearrange("(p j) c -> p j c", j=4))
-        gather_tab(sbuf([P, J - LEAD], U32, "tab_g1", over="tab_g0", shift=4 * LEAD)[:], LEAD)
+        gather_tab(sbuf([P, J - LEAD], U32, "tab_g1", over="tab_g0", shift=4 * LEAD)[:], LEAD, LEAD)
 
         n_raw = [sbuf([P, 4, N], F32, "n_raw%d" % w, over=("tab_w", "tab_g1")[w]) for w in range(2)]
         for w, src in enumerate((nr, ni)):
@@ -150,22 +163,23 @@ def tile_list_ckg_sig_kernel(
         ab, rel, xs, ys, hs, hq, wr_q = {}, {}, {}, {}, {}, {}, {}
 
         def first_stage(dst, c, table, table_s, weight, weight_s, step, dtype, passes):
+            first, last = passes[0], passes[-1]
             if c in TURNED:
-                for a in range(passes):
+                for a in passes:
                     nc.tensor.matmul_mx(
                         out=dst[:], lhsT=table(a).bitcast(dtype), lhsT_scale=table_s(a),
                         rhs=weight(a).bitcast(dtype), rhs_scale=weight_s(a),
-                        start=(a == 0), stop=(a == passes - 1),
+                        start=(a == first), stop=(a == last),
                     )
                 return dst[:].rearrange("p (j t) -> p j t", t=4)
-            for a in range(passes):
+            for a in passes:
                 for t in range(4):
                     nc.tensor.matmul_mx(
                         out=dst[:, CH * t : CH * (t + 1)],
                         lhsT=weight(a)[:, step * t : step * (t + 1)].bitcast(dtype),
                         lhsT_scale=weight_s(a)[:, P * t : P * (t + 1)],
                         rhs=table(a).bitcast(dtype), rhs_scale=table_s(a),
-                        start=((a, t) == (0, 0)), stop=((a, t) == (passes - 1, 3)),
+                        start=((a, t) == (first, 0)), stop=((a, t) == (last, 3)),
                     )
             return dst[:].rearrange("p (t j) -> p j t", t=4)
 
@@ -178,7 +192,7 @@ def tile_list_ckg_sig_kernel(
                     lambda a: planes8[a][:, CH * c : CH * (c + 1)],
                     lambda a: w_p[w][:, a, :].bitcast(U8),
                     lambda a: planes8[a][:, J + R * w : J + R * (w + 1)],
-                    2 * P, FP4X4, 2,
+                    2 * P, FP4X4, (0, 1) if c < LEAD // CH else (1, 0),
                 )
                 nc.scalar.copy(ab[c][:, w], sums)
 
@@ -188,16 +202,16 @@ def tile_list_ckg_sig_kernel(
                 bank([P, R], "%s%d" % (part, c)), c,
                 lambda a: tab2_g[c],
                 lambda a: plane2[:].bitcast(U8)[:, CH * c : CH * (c + 1)],
-                lambda a: codes[:], lambda a: scales[:], P, FP8X4, 1,
+                lambda a: codes[:], lambda a: scales[:], P, FP8X4, (0,),
             )
 
         def quantise(codes, scales, rounded):
             nc.vector.quantize_mx(out=codes.bitcast(FP8X4), scales=scales, in_=rounded)
 
-        def round_lines(engine, grouped, raw, slots):
+        def round_lines(engine, grouped, raw, slots, blocks):
             for u in range(2):
-                dst = grouped.rearrange("p (t g u i j) -> p u t g j i", g=16, u=2, i=4, j=4)[:, u]
-                src = raw[:].rearrange("p j (g t u i) -> p u t g j i", t=4, u=2, i=4)[:, u, slots]
+                dst = grouped.rearrange("p (t g u i j) -> p u t g j i", g=16, u=2, i=4, j=4)[:, u, slots, blocks]
+                src = raw.rearrange("p j (g t u i) -> p u t g j i", t=4, u=2, i=4)[:, u, slots]
                 engine(dst, src)
 
         def times_arr(c, engine, x):
@@ -262,9 +276,10 @@ def tile_list_ckg_sig_kernel(
                 finish(sums, first, count, m0, rows)
 
         wrr_g = sbuf([P, 4 * R], BF16, "wrr_g")
-        round_lines(nc.scalar.copy, wrr_g[:], wrr_raw, slice(0, 4))
+        round_lines(nc.scalar.copy, wrr_g[:], wrr_left[:], slice(0, 4), slice(0, SPLIT // 32))
         for k, c in enumerate(AHEAD):
-            entity(c, "wrr_raw" if k < 2 else None, 4096 * k)
+            entity(c, "wrr_left" if k < 2 else None, 4096 * k)
+        round_lines(nc.vector.tensor_copy, wrr_g[:], wrr_right[:], slice(0, 4), slice(SPLIT // 32, 16))
 
         wr_q["r"] = sbuf([P, R], U32, "wrr_c"), sbuf([P, R], U8, "wrr_s")
         quantise(wr_q["r"][0][:], wr_q["r"][1][:], wrr_g[:])
@@ -278,7 +293,7 @@ def tile_list_ckg_sig_kernel(
             relation("r", c)
 
         wri_g = sbuf([P, 4 * R], BF16, "wri_g", room=10240)
-        round_lines(nc.scalar.copy, wri_g[:, 0 : 2 * R], wri_raw, slice(0, 2))
+        round_lines(nc.scalar.copy, wri_g[:], wri_raw[:], slice(0, 2), slice(0, 16))
         for t in (2, 3):
             nc.gpsimd.tensor_scalar(
                 wri_g[:].rearrange("p (t g i j) -> p t g i j", g=16, i=8, j=4)[:, t],

@@ -24,9 +24,9 @@ LEAD = 256
 SPLIT = 320
 ROW0, ROW1 = 96, 112
 PASS_BYTES = J + 2 * R
-AHEAD = (0, 1, 2, 4)
-TURNED = (0, 1, 4)
-TIMES_ON_GPSIMD = (0, 1)
+AHEAD = (0, 1, 2, 3, 4, 5)
+TURNED = (0, 1, 2, 3)
+TIMES_ON_GPSIMD = (0, 1, 2)
 PAIRS = ((0, 1), (2, 3), (4, 5))
 
 
@@ -64,7 +64,7 @@ def tile_list_ckg_sig_kernel(
         idx = lists.tile([P, J // 16], U16, name="idx")
         idx2 = lists.tile([P, J // 16], U16, name="idx2")
         tab_sw = sbuf([P, T // 4], I32, "tab_sw")
-        tab2_sw = sbuf([P, T // 4], I32, "tab2_sw", room=8192)
+        tab2_sw = sbuf([P, T // 4], I32, "tab2_sw")
         tab_w = sbuf([P, T], I32, "tab_w")
         wer_raw = sbuf([P, 2, R // 2], I32, "wer_raw", room=4 * T)
         w_sraw = sbuf([P, 2, R // 4], I32, "w_sraw")
@@ -96,7 +96,7 @@ def tile_list_ckg_sig_kernel(
             joined[ROW0:P, J // 4 :].bitcast(U32).rearrange("p (w t g e) -> p w t g e", w=2, t=4, e=2),
             w_sraw[ROW0:P].bitcast(U32).rearrange("p w (g t e) -> p w t g e", t=4, e=2),
         )
-        tab_sg = sbuf([P, 12 * J], U8, "tab_sg", room=16384)[:, 0:J]
+        tab_sg = sbuf([P, 14 * J], U8, "tab_sg", room=22 * 1024)[:, 0:J]
         nc.vector.tensor_copy(tab_sg, tab_sw[:].bitcast(U8).indirect(idx[:]))
         nc.vector.tensor_copy(joined[ROW0:P, 0 : J // 4], tab_sg[ROW0:P].bitcast(I32))
 
@@ -113,6 +113,8 @@ def tile_list_ckg_sig_kernel(
         nc.sync.dma_start(wrr_left[:], wrr_rows[:, :, 0:SPLIT])
         move_rows(planes[1], joined, ROW0 + 16)
         nc.sync.dma_start(wrr_right[:], wrr_rows[:, :, SPLIT:])
+        wri_raw = sbuf([P, 4, R], F32, "wri_raw", over="tab_sg", shift=13 * 1024)
+        nc.sync.dma_start(wri_raw[:], wri.rearrange("(p j) c -> p j c", j=4))
         w_raw = wer_raw, wei_raw
         planes8 = [planes[a][:].bitcast(U8) for a in range(2)]
 
@@ -151,8 +153,6 @@ def tile_list_ckg_sig_kernel(
             cols = slice(half * J // 8, (half + 1) * J // 8)
             nc.vector.tensor_copy(joined2[ROW0:P, cols], tab2_sg[half][ROW0:P].bitcast(I32))
         move_rows(plane2, joined2, ROW1)
-        wri_raw = sbuf([P, 4, R], F32, "wri_raw", over="tab2_sw")
-        nc.sync.dma_start(wri_raw[:], wri.rearrange("(p j) c -> p j c", j=4))
         gather_tab(sbuf([P, J - LEAD], U32, "tab_g1", over="tab_g0", shift=4 * LEAD)[:], LEAD, LEAD)
 
         n_raw = [sbuf([P, 4, N], F32, "n_raw%d" % w, over=("tab_w", "tab_g1")[w]) for w in range(2)]
@@ -160,6 +160,7 @@ def tile_list_ckg_sig_kernel(
             for t in range(4):
                 nc.sync.dma_start(n_raw[w][:, t, :], src.rearrange("(g t i) n -> t g i n", t=4, i=8)[t])
 
+        spare = {("x", 6): ("wrr_g",), ("y", 6): ("wri_g",), ("x", 7): ("tab_w", 8192), ("y", 7): ("tab_w", 12288)}
         ab, rel, xs, ys, hs, hq, wr_q = {}, {}, {}, {}, {}, {}, {}
 
         def first_stage(dst, c, table, table_s, weight, weight_s, step, dtype, passes):
@@ -219,14 +220,10 @@ def tile_list_ckg_sig_kernel(
             xs[c], xs[c, 0], xs[c, 1] = x, x[:, 0], x[:, 1]
 
         def times_arr_vector(c):
-            times_arr(c, nc.vector, sbuf([P, 2, CH, 4], F32, "x%d" % c)[:])
-
-        def times_arr_part(c, w, over=None):
-            xs[c, w] = sbuf([P, CH, 4], F32, "x%d_%d" % (c, w), over)[:]
-            nc.vector.tensor_tensor(xs[c, w], ab[c][:, w], rel["r", c], MULT)
+            times_arr(c, nc.vector, sbuf([P, 2, CH, 4], F32, "x%d" % c, *spare.get(("x", c), ()))[:])
 
         def times_ari(c):
-            ys[c] = sbuf([P, 2, CH, 4], F32, "y%d" % c)[:]
+            ys[c] = sbuf([P, 2, CH, 4], F32, "y%d" % c, *spare.get(("y", c), ()))[:]
             nc.vector.scalar_tensor_tensor(ys[c][:, 0], ab[c][:, 1], -1.0, rel["i", c], MULT, MULT)
             nc.vector.tensor_tensor(ys[c][:, 1], ab[c][:, 0], rel["i", c], MULT)
 
@@ -283,40 +280,16 @@ def tile_list_ckg_sig_kernel(
 
         wr_q["r"] = sbuf([P, R], U32, "wrr_c"), sbuf([P, R], U8, "wrr_s")
         quantise(wr_q["r"][0][:], wr_q["r"][1][:], wrr_g[:])
-        tab2_g = {}
-        for half in range(2):
-            words = sbuf([P, J // 2], U32, "tab2_g%d" % half)
-            nc.vector.tensor_copy(words[:], tab2_w[:].bitcast(U32).indirect(idx2[:, 32 * half : 32 * (half + 1)]))
-            for c in range(4):
-                tab2_g[4 * half + c] = words[:, CH * c : CH * (c + 1)]
-        for c in (2, 0, 1, 4):
-            relation("r", c)
-
-        wri_g = sbuf([P, 4 * R], BF16, "wri_g", room=10240)
-        round_lines(nc.scalar.copy, wri_g[:], wri_raw[:], slice(0, 2), slice(0, 16))
-        for t in (2, 3):
-            nc.gpsimd.tensor_scalar(
-                wri_g[:].rearrange("p (t g i j) -> p t g i j", g=16, i=8, j=4)[:, t],
-                wri_raw[:].rearrange("p j (g t i) -> p t g i j", t=4, i=8)[:, t],
-                1.0, 0.0, MULT, ADD,
-            )
-        for k, c in enumerate(TIMES_ON_GPSIMD):
-            arr = sbuf([P, CH, 4], F32, "arr%d" % c, over="wri_raw", shift=2048 * k)
-            nc.scalar.copy(arr[:], rel["r", c])
-            rel["r", c] = arr[:]
-        times_arr_vector(2)
-        times_arr_part(4, 0)
+        wri_g = sbuf([P, 4 * R], BF16, "wri_g")
+        round_lines(nc.vector.tensor_copy, wri_g[:], wri_raw[:], slice(0, 4), slice(0, 16))
         wr_q["i"] = sbuf([P, R], U32, "wri_c"), sbuf([P, R], U8, "wri_s")
         quantise(wr_q["i"][0][:], wr_q["i"][1][:], wri_g[:])
-        for c in (2, 0, 1):
-            relation("i", c)
-        relation("r", 3)
-        times_arr_part(4, 1, over="wri_g")
-        x_gpsimd = sbuf([P, 2, 2, CH, 4], F32, "x_gpsimd", over="wri_g", shift=2048)
-        for k, c in enumerate(TIMES_ON_GPSIMD):
-            times_arr(c, nc.gpsimd, x_gpsimd[:, k])
-        entity(3, "wri_raw", 4096)
-        relation("i", 3)
+        tab2_g = {}
+        for first, size in ((0, LEAD), (LEAD, J - LEAD)):
+            words = sbuf([P, size], U32, "tab2_g%d" % first)
+            nc.vector.tensor_copy(words[:], tab2_w[:].bitcast(U32).indirect(idx2[:, first // 16 : (first + size) // 16]))
+            for c in range(size // CH):
+                tab2_g[first // CH + c] = words[:, CH * c : CH * (c + 1)]
 
         n_g = sbuf([P, 2, N, 4], BF16, "n_g")
         pair_h = [sbuf([P, 2, 2 * R], BF16, "h%d" % k) for k in range(len(PAIRS))]
@@ -324,37 +297,54 @@ def tile_list_ckg_sig_kernel(
             for place_in_pair, c in enumerate(pair):
                 hs[c] = pair_h[k][:, :, R * place_in_pair : R * (place_in_pair + 1)]
 
-        times_ari(2)
-        entity(5)
-        round_candidates(0)
+        def times_arr_gpsimd(c):
+            arr = sbuf([P, CH, 4], F32, "arr%d" % c)
+            nc.scalar.copy(arr[:], rel["r", c])
+            rel["r", c] = arr[:]
+            times_arr(c, nc.gpsimd, sbuf([P, 2, CH, 4], F32, "x%d" % c)[:])
+
+        for c in range(2):
+            relation("r", c)
+            relation("i", c)
+        relation("r", 2)
+        relation("r", 4)
+        relation("i", 4)
+        relation("i", 2)
+        for c in TIMES_ON_GPSIMD:
+            times_arr_gpsimd(c)
         times_ari(0)
-        add_gpsimd(2)
-        relation("r", 5)
+        entity(6)
+        round_candidates(0)
         times_ari(1)
-        relation("i", 5)
-        times_arr_vector(3)
         for w in range(2):
             add_turned(0, w)
-        relation("i", 4)
-        times_ari(3)
-        add_gpsimd(3)
-        entity(6)
+        times_arr_vector(4)
+        relation("r", 5)
+        relation("i", 5)
+        times_ari(4)
+        add_gpsimd(4)
+        times_ari(2)
         round_candidates(1)
-        times_arr_vector(5)
         for w in range(2):
             add_turned(1, w)
+        relation("r", 3)
+        relation("i", 3)
+        for w in range(2):
+            add_turned(2, w)
+        times_arr_vector(5)
+        relation("r", 6)
         times_ari(5)
         add_gpsimd(5)
-        relation("r", 6)
         relation("i", 6)
-        times_ari(4)
-        for w in range(2):
-            add_turned(4, w)
         entity(7)
-        times_arr_vector(6)
+        times_arr_vector(3)
+        times_ari(3)
+        for w in range(2):
+            add_turned(3, w)
         relation("r", 7)
-        times_ari(6)
         relation("i", 7)
+        times_arr_vector(6)
+        times_ari(6)
 
         codes = sbuf([P, 2 * N + 4 * CH * len(PAIRS)], U32, "codes", over="ab6")
         scales = sbuf([P, 2 * N + 4 * CH * len(PAIRS)], U8, "scales")

@@ -22,9 +22,9 @@ P = 128
 CH = 128
 LEAD = 256
 SPLIT = 320
+COVER = 3 * T // 4
 ROW0, ROW1 = 96, 112
 PASS_BYTES = J + 2 * R
-AHEAD = (0, 1, 2, 3, 4, 5)
 TURNED = (0, 1, 2, 3)
 TIMES_ON_GPSIMD = (0, 1, 2)
 PAIRS = ((0, 1), (2, 3), (4, 5))
@@ -66,7 +66,7 @@ def tile_list_ckg_sig_kernel(
         tab_sw = sbuf([P, T // 4], I32, "tab_sw")
         tab2_sw = sbuf([P, T // 4], I32, "tab2_sw")
         tab_w = sbuf([P, T], I32, "tab_w")
-        wer_raw = sbuf([P, 2, R // 2], I32, "wer_raw", room=4 * T)
+        wer_raw = sbuf([P, 2, R // 2], I32, "wer_raw")
         w_sraw = sbuf([P, 2, R // 4], I32, "w_sraw")
         planes = [sbuf([P, PASS_BYTES // 4], I32, "plane%d" % a) for a in range(2)]
         plane2 = sbuf([P, J // 4], I32, "plane2")
@@ -125,8 +125,6 @@ def tile_list_ckg_sig_kernel(
                 w_p[w][:].bitcast(U32).rearrange("p a (t g e) -> p a t g e", t=4, e=4),
                 w_raw[w][:].bitcast(U32).rearrange("p a (g t e) -> p a t g e", t=4, e=4),
             )
-        tab2_w = sbuf([P, T], I32, "tab2_w", over="wer_raw")
-        nc.sync.dma_start(tab2_w[:], tab2_words[0].rearrange("p t b -> p (t b)").bitcast(I32))
 
         tab_p = {}
 
@@ -141,7 +139,7 @@ def tile_list_ckg_sig_kernel(
                     tab_p[(first + j0) // CH + c] = parted[:, :, 2 * CH * c : 2 * CH * (c + 1)]
 
         def gather_tab2_scales(half, over):
-            picked = sbuf([P, J // 2], U8, "tab2_sg%d" % half, over)
+            picked = sbuf([P, J // 2], U8, "tab2_sg%d" % half, over, room=4 * T)
             nc.vector.tensor_copy(picked[:], tab2_sw[:].bitcast(U8).indirect(idx2[:, 32 * half : 32 * (half + 1)]))
             return picked
 
@@ -152,7 +150,11 @@ def tile_list_ckg_sig_kernel(
         for half in range(2):
             cols = slice(half * J // 8, (half + 1) * J // 8)
             nc.vector.tensor_copy(joined2[ROW0:P, cols], tab2_sg[half][ROW0:P].bitcast(I32))
+        tab2_w = sbuf([P, T], I32, "tab2_w", over="tab2_sg0")
+        tab2_src = tab2_words[0].rearrange("p t b -> p (t b)").bitcast(I32)
+        nc.sync.dma_start(tab2_w[:, 0:COVER], tab2_src[:, 0:COVER])
         move_rows(plane2, joined2, ROW1)
+        nc.sync.dma_start(tab2_w[:, COVER:], tab2_src[:, COVER:])
         gather_tab(sbuf([P, J - LEAD], U32, "tab_g1", over="tab_g0", shift=4 * LEAD)[:], LEAD, LEAD)
 
         n_raw = [sbuf([P, 4, N], F32, "n_raw%d" % w, over=("tab_w", "tab_g1")[w]) for w in range(2)]
@@ -184,7 +186,7 @@ def tile_list_ckg_sig_kernel(
                     )
             return dst[:].rearrange("p (t j) -> p j t", t=4)
 
-        def entity(c, over=None, shift=0):
+        def entity(c, over=None, shift=0, copy=nc.scalar.copy):
             ab[c] = sbuf([P, 2, CH, 4], F32, "ab%d" % c, over, shift, room=10240 if c == 6 else 0)
             for w in range(2):
                 sums = first_stage(
@@ -195,7 +197,7 @@ def tile_list_ckg_sig_kernel(
                     lambda a: planes8[a][:, J + R * w : J + R * (w + 1)],
                     2 * P, FP4X4, (0, 1) if c < LEAD // CH else (1, 0),
                 )
-                nc.scalar.copy(ab[c][:, w], sums)
+                copy(ab[c][:, w], sums)
 
         def relation(part, c):
             codes, scales = wr_q[part]
@@ -274,16 +276,25 @@ def tile_list_ckg_sig_kernel(
 
         wrr_g = sbuf([P, 4 * R], BF16, "wrr_g")
         round_lines(nc.scalar.copy, wrr_g[:], wrr_left[:], slice(0, 4), slice(0, SPLIT // 32))
-        for k, c in enumerate(AHEAD):
-            entity(c, "wrr_left" if k < 2 else None, 4096 * k)
+        for c in range(3):
+            entity(c, "wrr_left" if c < 2 else None, 4096 * c)
         round_lines(nc.vector.tensor_copy, wrr_g[:], wrr_right[:], slice(0, 4), slice(SPLIT // 32, 16))
 
         wr_q["r"] = sbuf([P, R], U32, "wrr_c"), sbuf([P, R], U8, "wrr_s")
         quantise(wr_q["r"][0][:], wr_q["r"][1][:], wrr_g[:])
         wri_g = sbuf([P, 4 * R], BF16, "wri_g")
-        round_lines(nc.vector.tensor_copy, wri_g[:], wri_raw[:], slice(0, 4), slice(0, 16))
+        round_lines(nc.vector.tensor_copy, wri_g[:], wri_raw[:], slice(0, 2), slice(0, 16))
+        for t in (2, 3):
+            nc.gpsimd.tensor_scalar(
+                wri_g[:].rearrange("p (t g i j) -> p t g i j", g=16, i=8, j=4)[:, t],
+                wri_raw[:].rearrange("p j (g t i) -> p t g i j", t=4, i=8)[:, t],
+                1.0, 0.0, MULT, ADD,
+            )
         wr_q["i"] = sbuf([P, R], U32, "wri_c"), sbuf([P, R], U8, "wri_s")
         quantise(wr_q["i"][0][:], wr_q["i"][1][:], wri_g[:])
+        entity(3, "wri_g", copy=nc.vector.tensor_copy)
+        entity(4)
+        entity(5)
         tab2_g = {}
         for first, size in ((0, LEAD), (LEAD, J - LEAD)):
             words = sbuf([P, size], U32, "tab2_g%d" % first)

@@ -21,8 +21,6 @@ SIGMOID = mybir.ActivationFunctionType.Sigmoid
 P = 128
 CH = 128
 LEAD = 256
-SPLIT = 320
-COVER = 3 * T // 4
 ROW0, ROW1 = 96, 112
 PASS_BYTES = J + 2 * R
 TURNED = (0, 1, 2, 3)
@@ -66,7 +64,7 @@ def tile_list_ckg_sig_kernel(
         tab_sw = sbuf([P, T // 4], I32, "tab_sw")
         tab2_sw = sbuf([P, T // 4], I32, "tab2_sw")
         tab_w = sbuf([P, T], I32, "tab_w")
-        wer_raw = sbuf([P, 2, R // 2], I32, "wer_raw")
+        w_raw = [sbuf([P, 2, R // 2], I32, "w_raw%d" % w, room=4 * T * (1 - w)) for w in range(2)]
         w_sraw = sbuf([P, 2, R // 4], I32, "w_sraw")
         planes = [sbuf([P, PASS_BYTES // 4], I32, "plane%d" % a) for a in range(2)]
         plane2 = sbuf([P, J // 4], I32, "plane2")
@@ -79,7 +77,8 @@ def tile_list_ckg_sig_kernel(
         nc.sync.dma_start(idx2[:], offs2)
         nc.sync.dma_start(tab2_sw[ROW1:P], tab2_scales.bitcast(I32)[0])
         nc.sync.dma_start(tab_w[:], tab_words[0].rearrange("p t b -> p (t b)").bitcast(I32))
-        nc.sync.dma_start(wer_raw[:], wer_words.bitcast(I32).rearrange("a p c -> p a c"))
+        for w, src in enumerate((wer_words, wei_words)):
+            nc.sync.dma_start(w_raw[w][:], src.bitcast(I32).rearrange("a p c -> p a c"))
 
         warm = sbuf([P, 2], F32, "warm")
         nc.vector.memset(warm[:, 0:1], 0.0)
@@ -96,7 +95,7 @@ def tile_list_ckg_sig_kernel(
             joined[ROW0:P, J // 4 :].bitcast(U32).rearrange("p (w t g e) -> p w t g e", w=2, t=4, e=2),
             w_sraw[ROW0:P].bitcast(U32).rearrange("p w (g t e) -> p w t g e", t=4, e=2),
         )
-        tab_sg = sbuf([P, 14 * J], U8, "tab_sg", room=22 * 1024)[:, 0:J]
+        tab_sg = sbuf([P, 9 * J], U8, "tab_sg", room=16384)[:, 0:J]
         nc.vector.tensor_copy(tab_sg, tab_sw[:].bitcast(U8).indirect(idx[:]))
         nc.vector.tensor_copy(joined[ROW0:P, 0 : J // 4], tab_sg[ROW0:P].bitcast(I32))
 
@@ -104,18 +103,13 @@ def tile_list_ckg_sig_kernel(
             for r in range(4):
                 nc.sync.dma_start(plane[r:P:32, :], rows[first + r : first + 16 : 4, :])
 
-        wei_raw = sbuf([P, 2, R // 2], I32, "wei_raw", over="tab_sg")
-        wrr_left = sbuf([P, 4, SPLIT], F32, "wrr_left", over="tab_sg", shift=2048)
-        wrr_right = sbuf([P, 4, R - SPLIT], F32, "wrr_right", over="tab_sg", shift=2048 + 8192)
+        wrr_raw = sbuf([P, 4, R], F32, "wrr_raw", over="tab_sg")
+        wri_raw = sbuf([P, 4, R], F32, "wri_raw", over="tab_sg", shift=8192)
         wrr_rows = wrr.rearrange("(p j) c -> p j c", j=4)
-        move_rows(planes[0], joined, ROW0)
-        nc.sync.dma_start(wei_raw[:], wei_words.bitcast(I32).rearrange("a p c -> p a c"))
-        nc.sync.dma_start(wrr_left[:], wrr_rows[:, :, 0:SPLIT])
-        move_rows(planes[1], joined, ROW0 + 16)
-        nc.sync.dma_start(wrr_right[:], wrr_rows[:, :, SPLIT:])
-        wri_raw = sbuf([P, 4, R], F32, "wri_raw", over="tab_sg", shift=13 * 1024)
+        for a, rows in enumerate((slice(0, 3), slice(3, 4))):
+            move_rows(planes[a], joined, ROW0 + 16 * a)
+            nc.sync.dma_start(wrr_raw[:, rows], wrr_rows[:, rows])
         nc.sync.dma_start(wri_raw[:], wri.rearrange("(p j) c -> p j c", j=4))
-        w_raw = wer_raw, wei_raw
         planes8 = [planes[a][:].bitcast(U8) for a in range(2)]
 
         w_p = []
@@ -125,6 +119,9 @@ def tile_list_ckg_sig_kernel(
                 w_p[w][:].bitcast(U32).rearrange("p a (t g e) -> p a t g e", t=4, e=4),
                 w_raw[w][:].bitcast(U32).rearrange("p a (g t e) -> p a t g e", t=4, e=4),
             )
+
+        tab2_w = sbuf([P, T], I32, "tab2_w", over="w_raw0")
+        nc.sync.dma_start(tab2_w[:], tab2_words[0].rearrange("p t b -> p (t b)").bitcast(I32))
 
         tab_p = {}
 
@@ -139,7 +136,7 @@ def tile_list_ckg_sig_kernel(
                     tab_p[(first + j0) // CH + c] = parted[:, :, 2 * CH * c : 2 * CH * (c + 1)]
 
         def gather_tab2_scales(half, over):
-            picked = sbuf([P, J // 2], U8, "tab2_sg%d" % half, over, room=4 * T)
+            picked = sbuf([P, J // 2], U8, "tab2_sg%d" % half, over)
             nc.vector.tensor_copy(picked[:], tab2_sw[:].bitcast(U8).indirect(idx2[:, 32 * half : 32 * (half + 1)]))
             return picked
 
@@ -150,11 +147,7 @@ def tile_list_ckg_sig_kernel(
         for half in range(2):
             cols = slice(half * J // 8, (half + 1) * J // 8)
             nc.vector.tensor_copy(joined2[ROW0:P, cols], tab2_sg[half][ROW0:P].bitcast(I32))
-        tab2_w = sbuf([P, T], I32, "tab2_w", over="tab2_sg0")
-        tab2_src = tab2_words[0].rearrange("p t b -> p (t b)").bitcast(I32)
-        nc.sync.dma_start(tab2_w[:, 0:COVER], tab2_src[:, 0:COVER])
         move_rows(plane2, joined2, ROW1)
-        nc.sync.dma_start(tab2_w[:, COVER:], tab2_src[:, COVER:])
         gather_tab(sbuf([P, J - LEAD], U32, "tab_g1", over="tab_g0", shift=4 * LEAD)[:], LEAD, LEAD)
 
         n_raw = [sbuf([P, 4, N], F32, "n_raw%d" % w, over=("tab_w", "tab_g1")[w]) for w in range(2)]
@@ -211,9 +204,9 @@ def tile_list_ckg_sig_kernel(
         def quantise(codes, scales, rounded):
             nc.vector.quantize_mx(out=codes.bitcast(FP8X4), scales=scales, in_=rounded)
 
-        def round_lines(engine, grouped, raw, slots, blocks):
+        def round_lines(engine, grouped, raw, slots):
             for u in range(2):
-                dst = grouped.rearrange("p (t g u i j) -> p u t g j i", g=16, u=2, i=4, j=4)[:, u, slots, blocks]
+                dst = grouped.rearrange("p (t g u i j) -> p u t g j i", g=16, u=2, i=4, j=4)[:, u, slots]
                 src = raw.rearrange("p j (g t u i) -> p u t g j i", t=4, u=2, i=4)[:, u, slots]
                 engine(dst, src)
 
@@ -264,10 +257,14 @@ def tile_list_ckg_sig_kernel(
             dst = out[P * m0 : P * (m0 + rows), first : first + count]
             nc.sync.dma_start(dst.rearrange("(m p) j -> p m j", p=P), res[:])
 
-        def score(codes, scales, first, count):
+        def score_banks(first, count):
             rows = R // count
-            for m0 in range(0, 4, rows):
-                sums = bank([P, rows, count], "s%d_%d" % (first, m0))
+            return [bank([P, rows, count], "s%d_%d" % (first, m0)) for m0 in range(0, 4, rows)]
+
+        def score(codes, scales, first, count, into=None):
+            rows = R // count
+            for k, sums in enumerate(into or score_banks(first, count)):
+                m0 = k * rows
                 for m in range(rows):
                     for w in range(2):
                         cols = slice(count * w, count * (w + 1))
@@ -275,15 +272,14 @@ def tile_list_ckg_sig_kernel(
                 finish(sums, first, count, m0, rows)
 
         wrr_g = sbuf([P, 4 * R], BF16, "wrr_g")
-        round_lines(nc.scalar.copy, wrr_g[:], wrr_left[:], slice(0, 4), slice(0, SPLIT // 32))
+        round_lines(nc.scalar.copy, wrr_g[:], wrr_raw[:], slice(0, 4))
         for c in range(3):
-            entity(c, "wrr_left" if c < 2 else None, 4096 * c)
-        round_lines(nc.vector.tensor_copy, wrr_g[:], wrr_right[:], slice(0, 4), slice(SPLIT // 32, 16))
+            entity(c, "wrr_raw" if c < 2 else None, 4096 * c)
 
         wr_q["r"] = sbuf([P, R], U32, "wrr_c"), sbuf([P, R], U8, "wrr_s")
         quantise(wr_q["r"][0][:], wr_q["r"][1][:], wrr_g[:])
         wri_g = sbuf([P, 4 * R], BF16, "wri_g")
-        round_lines(nc.vector.tensor_copy, wri_g[:], wri_raw[:], slice(0, 2), slice(0, 16))
+        round_lines(nc.vector.tensor_copy, wri_g[:], wri_raw[:], slice(0, 2))
         for t in (2, 3):
             nc.gpsimd.tensor_scalar(
                 wri_g[:].rearrange("p (t g i j) -> p t g i j", g=16, i=8, j=4)[:, t],
@@ -347,15 +343,16 @@ def tile_list_ckg_sig_kernel(
         times_ari(5)
         add_gpsimd(5)
         relation("i", 6)
-        entity(7)
         times_arr_vector(3)
         times_ari(3)
         for w in range(2):
             add_turned(3, w)
         relation("r", 7)
         relation("i", 7)
+        first_scores = score_banks(0, 2 * CH)
         times_arr_vector(6)
         times_ari(6)
+        entity(7)
 
         codes = sbuf([P, 2 * N + 4 * CH * len(PAIRS)], U32, "codes", over="ab6")
         scales = sbuf([P, 2 * N + 4 * CH * len(PAIRS)], U8, "scales")
@@ -369,7 +366,7 @@ def tile_list_ckg_sig_kernel(
         hs[6] = h6.rearrange("p (w e) -> p w e", w=2)
         add_gpsimd(6)
         for k, pair in enumerate(PAIRS):
-            score(*hq[k], CH * pair[0], 2 * CH)
+            score(*hq[k], CH * pair[0], 2 * CH, None if k else first_scores)
         times_arr_vector(7)
         times_ari(7)
 

@@ -24,8 +24,10 @@ LEAD = 256
 ROW0, ROW1 = 96, 112
 PASS_BYTES = J + 2 * R
 TURNED = (0, 1, 2, 3)
-TIMES_ON_GPSIMD = (0, 1, 2)
-PAIRS = ((0, 1), (2, 3), (4, 5))
+TIMES_ON_GPSIMD = (0, 2, 3)
+COVER = 1
+AHEAD = (4, 5, 2)
+PAIRS = ((0, 1), (4, 5), (2, 3))
 
 
 def tile_list_ckg_sig_kernel(
@@ -53,20 +55,25 @@ def tile_list_ckg_sig_kernel(
                 place[name] = place[over] + shift
             return lay.tile(shape, dtype, name=name, align_bytes=64, offset=place[name])
 
-        banks = []
+        free_banks, held = {"Scalar": [0, 1, 2, 3], "Vector": [4, 5, 6, 7]}, {}
 
-        def bank(shape, name):
-            banks.append(name)
-            return psum.tile(shape, F32, name=name, offset=2048 * ((len(banks) - 1) % 8))
+        def bank(shape, name, reader="Scalar", pick=0):
+            held[name] = reader, free_banks[reader].pop(pick)
+            return psum.tile(shape, F32, name=name, offset=2048 * held[name][1])
+
+        def release(name):
+            reader, number = held.pop(name)
+            free_banks[reader].append(number)
 
         idx = lists.tile([P, J // 16], U16, name="idx")
         idx2 = lists.tile([P, J // 16], U16, name="idx2")
         tab_sw = sbuf([P, T // 4], I32, "tab_sw")
         tab2_sw = sbuf([P, T // 4], I32, "tab2_sw")
         tab_w = sbuf([P, T], I32, "tab_w")
-        w_raw = [sbuf([P, 2, R // 2], I32, "w_raw%d" % w, room=4 * T * (1 - w)) for w in range(2)]
+        wer_raw = sbuf([P, 2, R // 2], I32, "wer_raw")
         w_sraw = sbuf([P, 2, R // 4], I32, "w_sraw")
-        planes = [sbuf([P, PASS_BYTES // 4], I32, "plane%d" % a) for a in range(2)]
+        plane0 = sbuf([P, PASS_BYTES // 4], I32, "plane0")
+        plane1 = sbuf([P, PASS_BYTES // 4], I32, "plane1")
         plane2 = sbuf([P, J // 4], I32, "plane2")
         joined = sbuf([P, PASS_BYTES // 4], I32, "joined")
 
@@ -77,25 +84,24 @@ def tile_list_ckg_sig_kernel(
         nc.sync.dma_start(idx2[:], offs2)
         nc.sync.dma_start(tab2_sw[ROW1:P], tab2_scales.bitcast(I32)[0])
         nc.sync.dma_start(tab_w[:], tab_words[0].rearrange("p t b -> p (t b)").bitcast(I32))
-        for w, src in enumerate((wer_words, wei_words)):
-            nc.sync.dma_start(w_raw[w][:], src.bitcast(I32).rearrange("a p c -> p a c"))
+        nc.sync.dma_start(wer_raw[:], wer_words.bitcast(I32).rearrange("a p c -> p a c"))
 
         warm = sbuf([P, 2], F32, "warm")
         nc.vector.memset(warm[:, 0:1], 0.0)
         nc.scalar.activation(warm[:, 1:2], warm[:, 0:1], SIGMOID)
         nc.vector.memset(tab_sw[0:ROW0], 0)
         nc.gpsimd.memset(tab2_sw[0:ROW1], 0)
-        for a in range(2):
-            nc.vector.memset(planes[a][:], 0)
+        nc.vector.memset(plane0[:], 0)
+        nc.vector.memset(plane1[:], 0)
         nc.vector.memset(plane2[:], 0)
         ident = sbuf([P, P], F32, "ident")
         make_identity(nc, ident[:])
 
         nc.scalar.copy(
-            joined[ROW0:P, J // 4 :].bitcast(U32).rearrange("p (w t g e) -> p w t g e", w=2, t=4, e=2),
+            joined[ROW0:P, J // 4 : PASS_BYTES // 4].bitcast(U32).rearrange("p (w t g e) -> p w t g e", w=2, t=4, e=2),
             w_sraw[ROW0:P].bitcast(U32).rearrange("p w (g t e) -> p w t g e", t=4, e=2),
         )
-        tab_sg = sbuf([P, 9 * J], U8, "tab_sg", room=16384)[:, 0:J]
+        tab_sg = sbuf([P, 11 * J], U8, "tab_sg", room=27 * J)[:, 0:J]
         nc.vector.tensor_copy(tab_sg, tab_sw[:].bitcast(U8).indirect(idx[:]))
         nc.vector.tensor_copy(joined[ROW0:P, 0 : J // 4], tab_sg[ROW0:P].bitcast(I32))
 
@@ -103,151 +109,188 @@ def tile_list_ckg_sig_kernel(
             for r in range(4):
                 nc.sync.dma_start(plane[r:P:32, :], rows[first + r : first + 16 : 4, :])
 
-        wrr_raw = sbuf([P, 4, R], F32, "wrr_raw", over="tab_sg")
-        wri_raw = sbuf([P, 4, R], F32, "wri_raw", over="tab_sg", shift=8192)
+        wei_raw = sbuf([P, 2, R // 2], I32, "wei_raw", over="tab_sg")
+        wr_raw = {"r": sbuf([P, 4, R], F32, "wrr_raw", over="tab_sg", shift=2 * J)}
+        tab2_w = sbuf([P, T], I32, "tab2_w", over="tab_sg", shift=11 * J - 64)
         wrr_rows = wrr.rearrange("(p j) c -> p j c", j=4)
-        for a, rows in enumerate((slice(0, 3), slice(3, 4))):
-            move_rows(planes[a], joined, ROW0 + 16 * a)
-            nc.sync.dma_start(wrr_raw[:, rows], wrr_rows[:, rows])
-        nc.sync.dma_start(wri_raw[:], wri.rearrange("(p j) c -> p j c", j=4))
-        planes8 = [planes[a][:].bitcast(U8) for a in range(2)]
+        move_rows(plane0, joined, ROW0)
+        nc.sync.dma_start(wei_raw[:], wei_words.bitcast(I32).rearrange("a p c -> p a c"))
+        nc.sync.dma_start(wr_raw["r"][:, 0:COVER], wrr_rows[:, 0:COVER])
+        move_rows(plane1, joined, ROW1)
+        nc.sync.dma_start(wr_raw["r"][:, COVER:4], wrr_rows[:, COVER:4])
+        nc.sync.dma_start(tab2_w[:], tab2_words[0].rearrange("p t b -> p (t b)").bitcast(I32))
+
+        def gather_tab2_scales(half, over, shift, room):
+            picked = sbuf([P, room], U8, "tab2_sg%d" % half, over, shift)[:, 0 : J // 2]
+            nc.vector.tensor_copy(picked, tab2_sw[:].bitcast(U8).indirect(idx2[:, 32 * half : 32 * (half + 1)]))
+            return picked
+
+        tab2_sg = [gather_tab2_scales(0, "tab_sg", 10 * J, J // 2)]
+        planes8 = [plane0[:].bitcast(U8), plane1[:].bitcast(U8)]
 
         w_p = []
-        for w in range(2):
+        for w, raw in enumerate((wer_raw, wei_raw)):
             w_p.append(sbuf([P, 2, R // 2], I32, "w_p%d" % w))
             nc.scalar.copy(
                 w_p[w][:].bitcast(U32).rearrange("p a (t g e) -> p a t g e", t=4, e=4),
-                w_raw[w][:].bitcast(U32).rearrange("p a (g t e) -> p a t g e", t=4, e=4),
+                raw[:].bitcast(U32).rearrange("p a (g t e) -> p a t g e", t=4, e=4),
             )
-
-        tab2_w = sbuf([P, T], I32, "tab2_w", over="w_raw0")
-        nc.sync.dma_start(tab2_w[:], tab2_words[0].rearrange("p t b -> p (t b)").bitcast(I32))
 
         tab_p = {}
 
-        def gather_tab(words, first, part):
-            size = words.shape[1]
+        def gather_tab(first, size, over, shift, room):
+            words = sbuf([P, room], U32, "tab_g%d" % first, over, shift, room=32 * J)[:, 0:size]
             nc.vector.tensor_copy(words, tab_w[:].bitcast(U32).indirect(idx[:, first // 16 : (first + size) // 16]))
-            for j0 in range(0, size, part):
-                parted = sbuf([P, 2, 2 * part], U8, "tab_p%d" % (first + j0))
+            return words
+
+        def part_tab(words, first, parts):
+            j0 = 0
+            for part in parts:
+                parted = sbuf([P, 2, 2 * part], U8, "tab_p%d" % (first + j0), room=8 * R if first + j0 == 5 * CH else 0)
                 src = words[:, j0 : j0 + part].bitcast(U16).rearrange("p (j a) -> p a j", a=2)
                 nc.vector.tensor_copy(parted[:].bitcast(U16), src)
                 for c in range(part // CH):
                     tab_p[(first + j0) // CH + c] = parted[:, :, 2 * CH * c : 2 * CH * (c + 1)]
+                j0 = j0 + part
 
-        def gather_tab2_scales(half, over):
-            picked = sbuf([P, J // 2], U8, "tab2_sg%d" % half, over)
-            nc.vector.tensor_copy(picked[:], tab2_sw[:].bitcast(U8).indirect(idx2[:, 32 * half : 32 * (half + 1)]))
-            return picked
-
-        tab2_sg = [gather_tab2_scales(0, None)]
-        gather_tab(sbuf([P, 2 * LEAD], U32, "tab_g0", room=4 * LEAD + 8192)[:, 0:LEAD], 0, CH)
-        tab2_sg.append(gather_tab2_scales(1, "tab_g0"))
+        part_tab(gather_tab(0, LEAD, None, 0, J), 0, (CH, CH))
+        rest = gather_tab(LEAD, J - LEAD, "tab_g0", 0, J - LEAD)
+        tab2_sg.append(gather_tab2_scales(1, "tab_g0", 3 * J, 21 * J + 64))
+        part_tab(rest, LEAD, (2 * CH, CH, CH, CH, CH))
         joined2 = sbuf([P, J // 4], I32, "joined2")
         for half in range(2):
             cols = slice(half * J // 8, (half + 1) * J // 8)
             nc.vector.tensor_copy(joined2[ROW0:P, cols], tab2_sg[half][ROW0:P].bitcast(I32))
         move_rows(plane2, joined2, ROW1)
-        gather_tab(sbuf([P, J - LEAD], U32, "tab_g1", over="tab_g0", shift=4 * LEAD)[:], LEAD, LEAD)
+        wr_raw["i"] = sbuf([P, 4, R], F32, "wri_raw", over="tab_g0", shift=8 * J)
+        nc.sync.dma_start(wr_raw["i"][:], wri.rearrange("(p j) c -> p j c", j=4))
 
-        n_raw = [sbuf([P, 4, N], F32, "n_raw%d" % w, over=("tab_w", "tab_g1")[w]) for w in range(2)]
+        n_raw = [sbuf([P, 4, N], F32, "n_raw%d" % w, over="tab_g0", shift=16 * J + 8 * J * w) for w in range(2)]
         for w, src in enumerate((nr, ni)):
             for t in range(4):
                 nc.sync.dma_start(n_raw[w][:, t, :], src.rearrange("(g t i) n -> t g i n", t=4, i=8)[t])
 
-        spare = {("x", 6): ("wrr_g",), ("y", 6): ("wri_g",), ("x", 7): ("tab_w", 8192), ("y", 7): ("tab_w", 12288)}
-        ab, rel, xs, ys, hs, hq, wr_q = {}, {}, {}, {}, {}, {}, {}
+        spare = {("x", 0): ("tab_w",), ("x", 1): ("tab_w", 4096), ("y", 0): ("tab_w", 8192), ("y", 1): ("tab_w", 12288),
+                 ("x", 5): ("wri_g", -2048), ("x", 2): ("wri_g", 2048), ("x", 6): ("wrr_raw",), ("y", 6): ("wrr_raw", 4096),
+                 ("arr", 2): ("wri_raw",), ("arr", 3): ("wri_raw", 2048), ("ab", 3): ("wri_raw", 4096),
+                 ("x", 7): ("tab2_w",), ("y", 7): ("tab2_w", 4096), ("x", 4): ("tab2_w", 8192), ("y", 4): ("tab2_w", 12288),
+                 "nr": ("ab6",), "pair0": ("ab6", 512), "ni": ("ab6", 1024), "pair1": ("ab6", 1536), "pair2": ("ab6", 2048)}
+        ent, ab, rel, xs, ys, hs, hq, wr_g, wr_q, n_q = {}, {}, {}, {}, {}, {}, {}, {}, {}, {}
 
-        def first_stage(dst, c, table, table_s, weight, weight_s, step, dtype, passes):
-            first, last = passes[0], passes[-1]
+        def first_stage(dst, c, table, table_s, weight, weight_s, step, dtype, first, last):
             if c in TURNED:
-                for a in passes:
-                    nc.tensor.matmul_mx(
-                        out=dst[:], lhsT=table(a).bitcast(dtype), lhsT_scale=table_s(a),
-                        rhs=weight(a).bitcast(dtype), rhs_scale=weight_s(a),
-                        start=(a == first), stop=(a == last),
-                    )
+                nc.tensor.matmul_mx(
+                    out=dst[:], lhsT=table.bitcast(dtype), lhsT_scale=table_s, rhs=weight.bitcast(dtype), rhs_scale=weight_s,
+                    start=first, stop=last,
+                )
                 return dst[:].rearrange("p (j t) -> p j t", t=4)
-            for a in passes:
-                for t in range(4):
-                    nc.tensor.matmul_mx(
-                        out=dst[:, CH * t : CH * (t + 1)],
-                        lhsT=weight(a)[:, step * t : step * (t + 1)].bitcast(dtype),
-                        lhsT_scale=weight_s(a)[:, P * t : P * (t + 1)],
-                        rhs=table(a).bitcast(dtype), rhs_scale=table_s(a),
-                        start=((a, t) == (first, 0)), stop=((a, t) == (last, 3)),
-                    )
+            for t in range(4):
+                nc.tensor.matmul_mx(
+                    out=dst[:, CH * t : CH * (t + 1)],
+                    lhsT=weight[:, step * t : step * (t + 1)].bitcast(dtype), lhsT_scale=weight_s[:, P * t : P * (t + 1)],
+                    rhs=table.bitcast(dtype), rhs_scale=table_s,
+                    start=(first and t == 0), stop=(last and t == 3),
+                )
             return dst[:].rearrange("p (t j) -> p j t", t=4)
 
-        def entity(c, over=None, shift=0, copy=nc.scalar.copy):
-            ab[c] = sbuf([P, 2, CH, 4], F32, "ab%d" % c, over, shift, room=10240 if c == 6 else 0)
+        def entity_pass(c, w, a, first, ring="Scalar"):
+            if first:
+                ent[c, w] = bank([P, R], "e%d_%d" % (c, w), ring)
+            return first_stage(
+                ent[c, w], c, tab_p[c][:, a, :], planes8[a][:, CH * c : CH * (c + 1)],
+                w_p[w][:, a, :].bitcast(U8), planes8[a][:, J + R * w : J + R * (w + 1)], 2 * P, FP4X4, first, not first,
+            )
+
+        def entity_half(c, w, copy=nc.scalar.copy, begun=False, ring="Scalar"):
+            if w == 0:
+                ab[c] = sbuf([P, 2, CH, 4], F32, "ab%d" % c, *spare.get(("ab", c), ()))
+            if not begun:
+                entity_pass(c, w, 1, True, ring)
+            copy(ab[c][:, w], entity_pass(c, w, int(begun), False))
+            release("e%d_%d" % (c, w))
+
+        def entity(c, copy=nc.scalar.copy, begun=False):
             for w in range(2):
-                sums = first_stage(
-                    bank([P, R], "e%d_%d" % (c, w)), c,
-                    lambda a: tab_p[c][:, a, :],
-                    lambda a: planes8[a][:, CH * c : CH * (c + 1)],
-                    lambda a: w_p[w][:, a, :].bitcast(U8),
-                    lambda a: planes8[a][:, J + R * w : J + R * (w + 1)],
-                    2 * P, FP4X4, (0, 1) if c < LEAD // CH else (1, 0),
-                )
-                copy(ab[c][:, w], sums)
+                entity_half(c, w, copy, begun)
 
         def relation(part, c):
             codes, scales = wr_q[part]
+            reader = "Scalar" if part == "r" and c in TIMES_ON_GPSIMD else "Vector"
             rel[part, c] = first_stage(
-                bank([P, R], "%s%d" % (part, c)), c,
-                lambda a: tab2_g[c],
-                lambda a: plane2[:].bitcast(U8)[:, CH * c : CH * (c + 1)],
-                lambda a: codes[:], lambda a: scales[:], P, FP8X4, (0,),
+                bank([P, R], "%s%d" % (part, c), reader), c, tab2_g[c],
+                plane2[:].bitcast(U8)[:, CH * c : CH * (c + 1)], codes[:], scales[:], P, FP8X4, True, True,
             )
 
         def quantise(codes, scales, rounded):
             nc.vector.quantize_mx(out=codes.bitcast(FP8X4), scales=scales, in_=rounded)
 
-        def round_lines(engine, grouped, raw, slots):
-            for u in range(2):
-                dst = grouped.rearrange("p (t g u i j) -> p u t g j i", g=16, u=2, i=4, j=4)[:, u, slots]
-                src = raw.rearrange("p j (g t u i) -> p u t g j i", t=4, u=2, i=4)[:, u, slots]
-                engine(dst, src)
+        def quantised(name, rounded):
+            words = rounded.shape[1] // 4
+            codes = sbuf([P, words], U32, name + "_c")
+            scales = sbuf([P, words], U8, name + "_s", *spare.get(name, ()))
+            quantise(codes[:], scales[:], rounded)
+            return codes, scales
 
-        def times_arr(c, engine, x):
-            engine.tensor_tensor(x, ab[c][:], rel["r", c].unsqueeze(1).to_broadcast([P, 2, CH, 4]), MULT)
-            xs[c], xs[c, 0], xs[c, 1] = x, x[:, 0], x[:, 1]
+        def round_weight(part, engine, slots):
+            if part not in wr_g:
+                place["free"] = place["free"] + 4 * R
+                wr_g[part] = sbuf([P, 4 * R], BF16, "wr%s_g" % part, room=12 * R)
+            for t in slots:
+                if engine is nc.gpsimd:
+                    dst = wr_g[part][:].rearrange("p (t g i j) -> p t g i j", g=16, i=8, j=4)[:, t]
+                    src = wr_raw[part][:].rearrange("p j (g t i) -> p t g i j", t=4, i=8)[:, t]
+                    nc.gpsimd.tensor_scalar(dst, src, 1.0, 0.0, MULT, ADD)
+                    continue
+                dst = wr_g[part][:].rearrange("p (t g u i j) -> p t g u j i", g=16, u=2, i=4, j=4)[:, t]
+                src = wr_raw[part][:].rearrange("p j (g t u i) -> p t g u j i", t=4, u=2, i=4)[:, t]
+                (nc.vector.tensor_copy if engine is nc.vector else nc.scalar.copy)(dst, src)
 
-        def times_arr_vector(c):
-            times_arr(c, nc.vector, sbuf([P, 2, CH, 4], F32, "x%d" % c, *spare.get(("x", c), ()))[:])
+        def quantise_weight(part):
+            wr_q[part] = quantised("wr" + part, wr_g[part][:])
+
+        def times_arr(c):
+            x = sbuf([P, 2, CH, 4], F32, "x%d" % c, *spare.get(("x", c), ()))[:]
+            engine, arr = nc.vector, rel["r", c]
+            if c in TIMES_ON_GPSIMD:
+                engine, arr = nc.gpsimd, sbuf([P, CH, 4], F32, "arr%d" % c, *spare.get(("arr", c), ()))[:]
+                nc.scalar.copy(arr, rel["r", c])
+            engine.tensor_tensor(x, ab[c][:], arr.unsqueeze(1).to_broadcast([P, 2, CH, 4]), MULT)
+            xs[c] = x
+            release("r%d" % c)
 
         def times_ari(c):
             ys[c] = sbuf([P, 2, CH, 4], F32, "y%d" % c, *spare.get(("y", c), ()))[:]
             nc.vector.scalar_tensor_tensor(ys[c][:, 0], ab[c][:, 1], -1.0, rel["i", c], MULT, MULT)
             nc.vector.tensor_tensor(ys[c][:, 1], ab[c][:, 0], rel["i", c], MULT)
+            release("i%d" % c)
 
         def add_gpsimd(c):
             x, y = (z[c].rearrange("p w j t -> p w (j t)") for z in (xs, ys))
             nc.gpsimd.tensor_tensor(hs[c], x, y, ADD)
 
-        def add_turned(c, w):
-            x, y = (z.rearrange("p j t -> p (j t)") for z in (xs[c, w], ys[c][:, w]))
-            dst = bank([P, 4, CH], "t%d_%d" % (c, w))
-            for k, term in enumerate((x, y)):
+        def add_turned(c, w, pick=0):
+            x, y = (z[c][:, w].rearrange("p j t -> p (j t)") for z in (xs, ys))
+            dst = bank([P, 4, CH], "t%d_%d" % (c, w), pick=pick)
+            for k, term in enumerate((x, y) if c in TIMES_ON_GPSIMD else (y, x)):
                 for t in range(4):
                     nc.tensor.matmul(
                         dst[:, t, :], term[:, P * t : P * (t + 1)], ident[:], is_transpose=True,
                         start=((k, t) == (0, 0)), stop=((k, t) == (1, 3)),
                     )
             nc.scalar.copy(hs[c][:, w].rearrange("p (j t) -> p j t", t=4), dst[:].rearrange("p t j -> p j t"))
+            release("t%d_%d" % (c, w))
 
-        def round_candidates(w):
-            for n0 in range(0, N, 2 * P):
-                nc.scalar.copy(
-                    n_g[:, w, n0 : n0 + 2 * P].rearrange("p (c i) t -> p c t i", i=4),
-                    n_raw[w][:, :, n0 : n0 + 2 * P].rearrange("p t (c i) -> p c t i", i=4),
-                )
+        def round_candidates(w, half):
+            n0 = 2 * P * half
+            nc.scalar.copy(
+                n_g[:, w, n0 : n0 + 2 * P].rearrange("p (c i) t -> p c t i", i=4),
+                n_raw[w][:, :, n0 : n0 + 2 * P].rearrange("p t (c i) -> p c t i", i=4),
+            )
 
         def score_pass(dst, m, w, codes, scales, start, stop):
-            cols = slice(N * w + P * m, N * w + P * (m + 1))
+            cols = slice(P * m, P * (m + 1))
             nc.tensor.matmul_mx(
-                out=dst, lhsT=n_q[0][:, cols].bitcast(FP8X4), lhsT_scale=n_q[1][:, cols],
+                out=dst, lhsT=n_q[w][0][:, cols].bitcast(FP8X4), lhsT_scale=n_q[w][1][:, cols],
                 rhs=codes.bitcast(FP8X4), rhs_scale=scales, start=start, stop=stop,
             )
 
@@ -257,130 +300,119 @@ def tile_list_ckg_sig_kernel(
             dst = out[P * m0 : P * (m0 + rows), first : first + count]
             nc.sync.dma_start(dst.rearrange("(m p) j -> p m j", p=P), res[:])
 
-        def score_banks(first, count):
+        def score(codes, scales, first, count):
             rows = R // count
-            return [bank([P, rows, count], "s%d_%d" % (first, m0)) for m0 in range(0, 4, rows)]
-
-        def score(codes, scales, first, count, into=None):
-            rows = R // count
-            for k, sums in enumerate(into or score_banks(first, count)):
-                m0 = k * rows
-                for m in range(rows):
-                    for w in range(2):
+            for m0 in range(0, 4, rows):
+                sums = bank([P, rows, count], "s%d_%d" % (first, m0))
+                for w in range(2):
+                    for m in range(rows):
                         cols = slice(count * w, count * (w + 1))
-                        score_pass(sums[:, m, :], m0 + m, w, codes[:, cols], scales[:, cols], w == 0, w == 1)
+                        start, stop = (w, m) == (0, 0), (w, m) == (1, rows - 1)
+                        score_pass(sums[:, m, :], m0 + m, w, codes[:, cols], scales[:, cols], start, stop)
                 finish(sums, first, count, m0, rows)
+                release("s%d_%d" % (first, m0))
 
-        wrr_g = sbuf([P, 4 * R], BF16, "wrr_g")
-        round_lines(nc.scalar.copy, wrr_g[:], wrr_raw[:], slice(0, 4))
-        for c in range(3):
-            entity(c, "wrr_raw" if c < 2 else None, 4096 * c)
-
-        wr_q["r"] = sbuf([P, R], U32, "wrr_c"), sbuf([P, R], U8, "wrr_s")
-        quantise(wr_q["r"][0][:], wr_q["r"][1][:], wrr_g[:])
-        wri_g = sbuf([P, 4 * R], BF16, "wri_g")
-        round_lines(nc.vector.tensor_copy, wri_g[:], wri_raw[:], slice(0, 2))
-        for t in (2, 3):
-            nc.gpsimd.tensor_scalar(
-                wri_g[:].rearrange("p (t g i j) -> p t g i j", g=16, i=8, j=4)[:, t],
-                wri_raw[:].rearrange("p j (g t i) -> p t g i j", t=4, i=8)[:, t],
-                1.0, 0.0, MULT, ADD,
-            )
-        wr_q["i"] = sbuf([P, R], U32, "wri_c"), sbuf([P, R], U8, "wri_s")
-        quantise(wr_q["i"][0][:], wr_q["i"][1][:], wri_g[:])
-        entity(3, "wri_g", copy=nc.vector.tensor_copy)
-        entity(4)
-        entity(5)
+        for w in range(2):
+            for c in range(2):
+                entity_pass(c, w, 0, True)
+        for c in range(2):
+            entity(c, begun=True)
+        round_weight("r", nc.vector, range(4))
+        quantise_weight("r")
+        for c in AHEAD:
+            entity(c)
+        held_sums = []
+        for w in range(2):
+            entity_pass(3, w, 1, True)
+            held_sums.append(entity_pass(3, w, 0, False))
         tab2_g = {}
+        tab2_words_g = sbuf([P, J], U32, "tab2_g", over="tab_p640")
         for first, size in ((0, LEAD), (LEAD, J - LEAD)):
-            words = sbuf([P, size], U32, "tab2_g%d" % first)
-            nc.vector.tensor_copy(words[:], tab2_w[:].bitcast(U32).indirect(idx2[:, first // 16 : (first + size) // 16]))
+            words = tab2_words_g[:, first : first + size]
+            nc.vector.tensor_copy(words, tab2_w[:].bitcast(U32).indirect(idx2[:, first // 16 : (first + size) // 16]))
             for c in range(size // CH):
                 tab2_g[first // CH + c] = words[:, CH * c : CH * (c + 1)]
 
         n_g = sbuf([P, 2, N, 4], BF16, "n_g")
-        pair_h = [sbuf([P, 2, 2 * R], BF16, "h%d" % k) for k in range(len(PAIRS))]
+        pair_h = [sbuf([P, 2, 2 * R], BF16, "h%d" % pair[0], *spare.get(("h", pair[0]), ())) for pair in PAIRS]
         for k, pair in enumerate(PAIRS):
             for place_in_pair, c in enumerate(pair):
                 hs[c] = pair_h[k][:, :, R * place_in_pair : R * (place_in_pair + 1)]
 
-        def times_arr_gpsimd(c):
-            arr = sbuf([P, CH, 4], F32, "arr%d" % c)
-            nc.scalar.copy(arr[:], rel["r", c])
-            rel["r", c] = arr[:]
-            times_arr(c, nc.gpsimd, sbuf([P, 2, CH, 4], F32, "x%d" % c)[:])
-
-        for c in range(2):
-            relation("r", c)
-            relation("i", c)
-        relation("r", 2)
+        relation("r", 0)
+        relation("r", 1)
+        times_arr(0)
         relation("r", 4)
-        relation("i", 4)
-        relation("i", 2)
-        for c in TIMES_ON_GPSIMD:
-            times_arr_gpsimd(c)
-        times_ari(0)
-        entity(6)
-        round_candidates(0)
-        times_ari(1)
-        for w in range(2):
-            add_turned(0, w)
-        times_arr_vector(4)
         relation("r", 5)
+        relation("r", 2)
+        round_weight("i", nc.scalar, range(4))
+        times_arr(1)
+        times_arr(4)
+        quantise_weight("i")
+        times_arr(2)
+        relation("r", 3)
+        ab[3] = sbuf([P, 2, CH, 4], F32, "ab3", *spare["ab", 3])
+        for w in range(2):
+            nc.scalar.copy(ab[3][:, w], held_sums[w])
+            release("e3_%d" % w)
+        times_arr(3)
+        relation("i", 0)
+        relation("i", 1)
+        relation("i", 4)
+        times_arr(5)
         relation("i", 5)
+        round_candidates(0, 0)
+        round_candidates(0, 1)
+        times_ari(0)
+        relation("i", 2)
+        add_turned(0, 0)
+        add_turned(0, 1)
+        entity(6)
+        times_ari(1)
+        relation("i", 3)
+        round_candidates(1, 0)
+        add_turned(1, 0)
+        add_turned(1, 1)
         times_ari(4)
         add_gpsimd(4)
-        times_ari(2)
-        round_candidates(1)
-        for w in range(2):
-            add_turned(1, w)
-        relation("r", 3)
-        relation("i", 3)
-        for w in range(2):
-            add_turned(2, w)
-        times_arr_vector(5)
         relation("r", 6)
+        round_candidates(1, 1)
+        times_ari(2)
+        relation("i", 6)
+        add_turned(2, 0)
+        add_turned(2, 1)
         times_ari(5)
         add_gpsimd(5)
-        relation("i", 6)
-        times_arr_vector(3)
-        times_ari(3)
-        for w in range(2):
-            add_turned(3, w)
         relation("r", 7)
+        times_ari(3)
         relation("i", 7)
-        first_scores = score_banks(0, 2 * CH)
-        times_arr_vector(6)
+        add_turned(3, 0)
+        add_turned(3, 1)
+        times_arr(6)
         times_ari(6)
-        entity(7)
+        entity_half(7, 0, ring="Vector")
+        entity_half(7, 1, ring="Vector")
 
-        codes = sbuf([P, 2 * N + 4 * CH * len(PAIRS)], U32, "codes", over="ab6")
-        scales = sbuf([P, 2 * N + 4 * CH * len(PAIRS)], U8, "scales")
-        n_q = codes[:, 0 : 2 * N], scales[:, 0 : 2 * N]
-        quantise(*n_q, n_g[:].rearrange("p w n t -> p (w n t)"))
-        for k in range(len(PAIRS)):
-            cols = slice(2 * N + 4 * CH * k, 2 * N + 4 * CH * (k + 1))
-            hq[k] = codes[:, cols], scales[:, cols]
-            quantise(*hq[k], pair_h[k][:].rearrange("p w e -> p (w e)"))
-        h6 = sbuf([P, 8 * N + 4 * R * len(PAIRS)], BF16, "h6", over="n_g")[:, 0 : 2 * R]
+        n_q[0] = quantised("nr", n_g[:, 0].rearrange("p n t -> p (n t)"))
+        hq[0] = quantised("pair0", pair_h[0][:].rearrange("p w e -> p (w e)"))
+        n_q[1] = quantised("ni", n_g[:, 1].rearrange("p n t -> p (n t)"))
+        for k in (1, 2):
+            hq[k] = quantised("pair%d" % k, pair_h[k][:].rearrange("p w e -> p (w e)"))
+        h6 = sbuf([P, 2 * R], BF16, "h6", over="h2")[:]
         hs[6] = h6.rearrange("p (w e) -> p w e", w=2)
         add_gpsimd(6)
-        for k, pair in enumerate(PAIRS):
-            score(*hq[k], CH * pair[0], 2 * CH, None if k else first_scores)
-        times_arr_vector(7)
+        times_arr(7)
         times_ari(7)
-
-        codes, scales = sbuf([P, 2 * CH], U32, "h6_c"), sbuf([P, 2 * CH], U8, "h6_s")
-        quantise(codes[:], scales[:], h6)
+        for k, pair in enumerate(PAIRS):
+            score(*hq[k], CH * pair[0], 2 * CH)
+        codes, scales = quantised("h6", h6)
         score(codes, scales, CH * 6, CH)
-        halves = []
+        halves = [sbuf([P, CH, 4], BF16, "h7_%d" % w) for w in range(2)]
         for w in range(2):
-            halves.append(sbuf([P, CH, 4], BF16, "h7_%d" % w))
-            nc.vector.tensor_tensor(halves[w][:], xs[7, w], ys[7][:, w], ADD)
-        sums = [bank([P, 2, CH], "last%d" % half) for half in range(2)]
+            nc.vector.tensor_tensor(halves[w][:], xs[7][:, w], ys[7][:, w], ADD)
+        sums = [bank([P, 2, CH], "last%d" % half, "Vector") for half in range(2)]
         for w in range(2):
-            codes, scales = sbuf([P, CH], U32, "last_c%d" % w), sbuf([P, CH], U8, "last_s%d" % w)
-            quantise(codes[:], scales[:], halves[w][:].rearrange("p j t -> p (j t)"))
+            codes, scales = quantised("last%d" % w, halves[w][:].rearrange("p j t -> p (j t)"))
             for m in range(4):
                 start, stop = (w, m % 2) == (0, 0), (w, m % 2) == (1, 1)
                 score_pass(sums[m // 2][:, m % 2, :], m, w, codes[:], scales[:], start, stop)

@@ -170,9 +170,10 @@ def tile_list_ckg_sig_kernel(
             for t in range(4):
                 nc.sync.dma_start(n_raw[w][:, t, :], src.rearrange("(g t i) n -> t g i n", t=4, i=8)[t])
 
+        held_sums = {}
         spare = {("x", 0): ("tab_w",), ("x", 1): ("tab_w", 4096), ("y", 0): ("tab_w", 8192), ("y", 1): ("tab_w", 12288),
                  ("x", 5): ("wri_g", -2048), ("x", 2): ("wri_g", 2048), ("x", 6): ("wrr_raw",), ("y", 6): ("wrr_raw", 4096),
-                 ("arr", 2): ("wri_raw",), ("arr", 3): ("wri_raw", 2048), ("ab", 3): ("wri_raw", 4096),
+                 ("arr", 2): ("wri_raw", 2048), ("ab", 6): ("wri_raw", -2048), ("ab", 3): ("wri_raw", 4096),
                  ("x", 7): ("tab2_w",), ("y", 7): ("tab2_w", 4096), ("x", 4): ("tab2_w", 8192), ("y", 4): ("tab2_w", 12288),
                  "nr": ("ab6",), "pair0": ("ab6", 512), "ni": ("ab6", 1024), "pair1": ("ab6", 1536), "pair2": ("ab6", 2048)}
         ent, ab, rel, xs, ys, hs, hq, wr_g, wr_q, n_q = {}, {}, {}, {}, {}, {}, {}, {}, {}, {}
@@ -208,6 +209,16 @@ def tile_list_ckg_sig_kernel(
                 entity_pass(c, w, 1, True, ring)
             copy(ab[c][:, w], entity_pass(c, w, int(begun), False))
             release("e%d_%d" % (c, w))
+
+        def entity_sums(c, w, ring="Scalar"):
+            entity_pass(c, w, 1, True, ring)
+            held_sums[c, w] = entity_pass(c, w, 0, False)
+
+        def copy_held(c, copy=nc.scalar.copy):
+            ab[c] = sbuf([P, 2, CH, 4], F32, "ab%d" % c, *spare["ab", c])
+            for w in range(2):
+                copy(ab[c][:, w], held_sums[c, w])
+                release("e%d_%d" % (c, w))
 
         def entity(c, copy=nc.scalar.copy, begun=False):
             for w in range(2):
@@ -321,10 +332,8 @@ def tile_list_ckg_sig_kernel(
         quantise_weight("r")
         for c in AHEAD:
             entity(c)
-        held_sums = []
         for w in range(2):
-            entity_pass(3, w, 1, True)
-            held_sums.append(entity_pass(3, w, 0, False))
+            entity_sums(3, w)
         tab2_g = {}
         tab2_words_g = sbuf([P, J], U32, "tab2_g", over="tab_p640")
         for first, size in ((0, LEAD), (LEAD, J - LEAD)):
@@ -345,21 +354,22 @@ def tile_list_ckg_sig_kernel(
         relation("r", 4)
         relation("r", 5)
         relation("r", 2)
+        entity_sums(6, 0)
         round_weight("i", nc.scalar, range(4))
         times_arr(1)
+        free_banks["Vector"].reverse()
+        entity_sums(6, 1, "Vector")
         times_arr(4)
         quantise_weight("i")
         times_arr(2)
-        relation("r", 3)
-        ab[3] = sbuf([P, 2, CH, 4], F32, "ab3", *spare["ab", 3])
-        for w in range(2):
-            nc.scalar.copy(ab[3][:, w], held_sums[w])
-            release("e3_%d" % w)
-        times_arr(3)
         relation("i", 0)
         relation("i", 1)
-        relation("i", 4)
+        relation("r", 3)
+        copy_held(3)
+        times_arr(3)
         times_arr(5)
+        relation("i", 4)
+        copy_held(6)
         relation("i", 5)
         round_candidates(0, 0)
         round_candidates(0, 1)
@@ -367,7 +377,6 @@ def tile_list_ckg_sig_kernel(
         relation("i", 2)
         add_turned(0, 0)
         add_turned(0, 1)
-        entity(6)
         times_ari(1)
         relation("i", 3)
         round_candidates(1, 0)

@@ -27,7 +27,7 @@ TURNED = (0, 1, 2, 3)
 TIMES_ON_GPSIMD = (0, 2, 3)
 COVER = 1
 AHEAD = (4, 5, 2)
-PAIRS = ((0, 1), (4, 5), (2, 3))
+PAIRS = ((0, 1), (2, 3))
 
 
 def tile_list_ckg_sig_kernel(
@@ -171,8 +171,8 @@ def tile_list_ckg_sig_kernel(
                 nc.sync.dma_start(n_raw[w][:, t, :], src.rearrange("(g t i) n -> t g i n", t=4, i=8)[t])
 
         held_sums = {}
-        spare = {("x", 0): ("tab_w",), ("x", 1): ("tab_w", 4096), ("y", 0): ("tab_w", 8192), ("y", 1): ("tab_w", 12288),
-                 ("x", 5): ("wri_g", -2048), ("x", 2): ("wri_g", 2048), ("x", 6): ("wrr_raw",), ("y", 6): ("wrr_raw", 4096),
+        spare = {("x", 0): ("tab_w",), ("x", 1, 0): ("tab_w", 4096), ("x", 5): ("tab2_sw",), ("y", 0): ("tab_w", 8192), ("y", 1): ("tab_w", 12288),
+                 ("x", 1, 1): ("wri_g",), ("x", 2): ("wri_g", 2048), ("x", 6): ("wrr_raw",), ("y", 6): ("wrr_raw", 4096),
                  ("arr", 2): ("wri_raw", 2048), ("ab", 6): ("wri_raw", -2048), ("ab", 3): ("wri_raw", 4096),
                  ("x", 7): ("tab2_w",), ("y", 7): ("tab2_w", 4096), ("x", 4): ("tab2_w", 8192), ("y", 4): ("tab2_w", 12288),
                  "nr": ("ab6",), "pair0": ("ab6", 512), "ni": ("ab6", 1024), "pair1": ("ab6", 1536), "pair2": ("ab6", 2048)}
@@ -266,8 +266,12 @@ def tile_list_ckg_sig_kernel(
                 engine, arr = nc.gpsimd, sbuf([P, CH, 4], F32, "arr%d" % c, *spare.get(("arr", c), ()))[:]
                 nc.scalar.copy(arr, rel["r", c])
             engine.tensor_tensor(x, ab[c][:], arr.unsqueeze(1).to_broadcast([P, 2, CH, 4]), MULT)
-            xs[c] = x
+            xs[c], xs[c, 0], xs[c, 1] = x, x[:, 0], x[:, 1]
             release("r%d" % c)
+
+        def times_arr_half(c, w):
+            xs[c, w] = sbuf([P, CH, 4], F32, "x%d_%d" % (c, w), *spare["x", c, w])[:]
+            nc.vector.tensor_tensor(xs[c, w], ab[c][:, w], rel["r", c], MULT)
 
         def times_ari(c):
             ys[c] = sbuf([P, 2, CH, 4], F32, "y%d" % c, *spare.get(("y", c), ()))[:]
@@ -280,7 +284,7 @@ def tile_list_ckg_sig_kernel(
             nc.gpsimd.tensor_tensor(hs[c], x, y, ADD)
 
         def add_turned(c, w, pick=0):
-            x, y = (z[c][:, w].rearrange("p j t -> p (j t)") for z in (xs, ys))
+            x, y = (z.rearrange("p j t -> p (j t)") for z in (xs[c, w], ys[c][:, w]))
             dst = bank([P, 4, CH], "t%d_%d" % (c, w), pick=pick)
             for k, term in enumerate((x, y) if c in TIMES_ON_GPSIMD else (y, x)):
                 for t in range(4):
@@ -347,6 +351,8 @@ def tile_list_ckg_sig_kernel(
         for k, pair in enumerate(PAIRS):
             for place_in_pair, c in enumerate(pair):
                 hs[c] = pair_h[k][:, :, R * place_in_pair : R * (place_in_pair + 1)]
+        for c in (4, 5):
+            hs[c] = sbuf([P, 2, R], BF16, "h%d" % c)[:]
 
         relation("r", 0)
         relation("r", 1)
@@ -356,10 +362,11 @@ def tile_list_ckg_sig_kernel(
         relation("r", 2)
         entity_sums(6, 0)
         round_weight("i", nc.scalar, range(4))
-        times_arr(1)
+        times_arr_half(1, 0)
+        times_arr(4)
         free_banks["Vector"].reverse()
         entity_sums(6, 1, "Vector")
-        times_arr(4)
+        times_arr(5)
         quantise_weight("i")
         times_arr(2)
         relation("i", 0)
@@ -367,7 +374,8 @@ def tile_list_ckg_sig_kernel(
         relation("r", 3)
         copy_held(3)
         times_arr(3)
-        times_arr(5)
+        times_arr_half(1, 1)
+        release("r1")
         relation("i", 4)
         copy_held(6)
         relation("i", 5)
@@ -405,15 +413,19 @@ def tile_list_ckg_sig_kernel(
         n_q[0] = quantised("nr", n_g[:, 0].rearrange("p n t -> p (n t)"))
         hq[0] = quantised("pair0", pair_h[0][:].rearrange("p w e -> p (w e)"))
         n_q[1] = quantised("ni", n_g[:, 1].rearrange("p n t -> p (n t)"))
-        for k in (1, 2):
-            hq[k] = quantised("pair%d" % k, pair_h[k][:].rearrange("p w e -> p (w e)"))
+        hq[2] = sbuf([P, R], U32, "pair2_c"), sbuf([P, R], U8, "pair2_s", *spare["pair2"])
+        for c in (4, 5):
+            for w in range(2):
+                cols = slice(CH * (2 * w + c - 4), CH * (2 * w + c - 3))
+                quantise(hq[2][0][:, cols], hq[2][1][:, cols], hs[c][:, w])
+        hq[1] = quantised("pair1", pair_h[1][:].rearrange("p w e -> p (w e)"))
         h6 = sbuf([P, 2 * R], BF16, "h6", over="h2")[:]
         hs[6] = h6.rearrange("p (w e) -> p w e", w=2)
         add_gpsimd(6)
         times_arr(7)
         times_ari(7)
-        for k, pair in enumerate(PAIRS):
-            score(*hq[k], CH * pair[0], 2 * CH)
+        for k in (0, 2, 1):
+            score(*hq[k], 2 * CH * k, 2 * CH)
         codes, scales = quantised("h6", h6)
         score(codes, scales, CH * 6, CH)
         halves = [sbuf([P, CH, 4], BF16, "h7_%d" % w) for w in range(2)]

@@ -172,8 +172,8 @@ def tile_list_ckg_sig_kernel(
 
         held_sums = {}
         spare = {("x", 0): ("tab_w",), ("x", 1, 0): ("tab_w", 4096), ("x", 5): ("tab2_sw",), ("y", 0): ("tab_w", 8192), ("y", 1): ("tab_w", 12288),
-                 ("x", 1, 1): ("wri_g",), ("x", 2): ("wri_g", 2048), ("x", 6): ("wrr_raw",), ("y", 6): ("wrr_raw", 4096),
-                 ("arr", 2): ("wri_raw", 2048), ("ab", 6): ("wri_raw", -2048), ("ab", 3): ("wri_raw", 4096),
+                 ("x", 1, 1): ("wri_g", 1024), ("x", 2): ("wri_g", 3072), ("x", 6): ("wrr_raw",), ("y", 6): ("wrr_raw", 4096),
+                 ("arr", 2): ("wri_raw",), ("arr", 3): ("wri_raw", 2048), ("ab", 6): ("wri_g", -3072), ("ab", 3): ("wri_raw", 4096),
                  ("x", 7): ("tab2_w",), ("y", 7): ("tab2_w", 4096), ("x", 4): ("tab2_w", 8192), ("y", 4): ("tab2_w", 12288),
                  "nr": ("ab6",), "pair0": ("ab6", 512), "ni": ("ab6", 1024), "pair1": ("ab6", 1536), "pair2": ("ab6", 2048)}
         ent, ab, rel, xs, ys, hs, hq, wr_g, wr_q, n_q = {}, {}, {}, {}, {}, {}, {}, {}, {}, {}
@@ -194,9 +194,9 @@ def tile_list_ckg_sig_kernel(
                 )
             return dst[:].rearrange("p (t j) -> p j t", t=4)
 
-        def entity_pass(c, w, a, first, ring="Scalar"):
+        def entity_pass(c, w, a, first, ring="Scalar", pick=0):
             if first:
-                ent[c, w] = bank([P, R], "e%d_%d" % (c, w), ring)
+                ent[c, w] = bank([P, R], "e%d_%d" % (c, w), ring, pick)
             return first_stage(
                 ent[c, w], c, tab_p[c][:, a, :], planes8[a][:, CH * c : CH * (c + 1)],
                 w_p[w][:, a, :].bitcast(U8), planes8[a][:, J + R * w : J + R * (w + 1)], 2 * P, FP4X4, first, not first,
@@ -210,8 +210,8 @@ def tile_list_ckg_sig_kernel(
             copy(ab[c][:, w], entity_pass(c, w, int(begun), False))
             release("e%d_%d" % (c, w))
 
-        def entity_sums(c, w, ring="Scalar"):
-            entity_pass(c, w, 1, True, ring)
+        def entity_sums(c, w, ring, pick=-1):
+            entity_pass(c, w, 1, True, ring, pick)
             held_sums[c, w] = entity_pass(c, w, 0, False)
 
         def copy_held(c, copy=nc.scalar.copy):
@@ -244,8 +244,8 @@ def tile_list_ckg_sig_kernel(
 
         def round_weight(part, engine, slots):
             if part not in wr_g:
-                place["free"] = place["free"] + 4 * R
-                wr_g[part] = sbuf([P, 4 * R], BF16, "wr%s_g" % part, room=12 * R)
+                place["free"] = place["free"] + 6 * R
+                wr_g[part] = sbuf([P, 4 * R], BF16, "wr%s_g" % part, room=14 * R)
             for t in slots:
                 if engine is nc.gpsimd:
                     dst = wr_g[part][:].rearrange("p (t g i j) -> p t g i j", g=16, i=8, j=4)[:, t]
@@ -336,8 +336,7 @@ def tile_list_ckg_sig_kernel(
         quantise_weight("r")
         for c in AHEAD:
             entity(c)
-        for w in range(2):
-            entity_sums(3, w)
+        entity_sums(3, 0, "Scalar", 0)
         tab2_g = {}
         tab2_words_g = sbuf([P, J], U32, "tab2_g", over="tab_p640")
         for first, size in ((0, LEAD), (LEAD, J - LEAD)):
@@ -359,19 +358,19 @@ def tile_list_ckg_sig_kernel(
         times_arr(0)
         relation("r", 4)
         relation("r", 5)
+        entity_sums(3, 1, "Scalar")
         relation("r", 2)
-        entity_sums(6, 0)
+        relation("r", 3)
         round_weight("i", nc.scalar, range(4))
         times_arr_half(1, 0)
         times_arr(4)
-        free_banks["Vector"].reverse()
-        entity_sums(6, 1, "Vector")
+        entity_sums(6, 0, "Vector")
         times_arr(5)
         quantise_weight("i")
         times_arr(2)
         relation("i", 0)
         relation("i", 1)
-        relation("r", 3)
+        entity_sums(6, 1, "Scalar")
         copy_held(3)
         times_arr(3)
         times_arr_half(1, 1)

@@ -23,11 +23,11 @@ CH = 128
 LEAD = 256
 ROW0, ROW1 = 96, 112
 PASS_BYTES = J + 2 * R
-TURNED = (0, 1, 2, 3)
+TURNED = (0, 2, 3, 4)
 TIMES_ON_GPSIMD = (0, 2, 3)
 COVER = 1
-AHEAD = (4, 5, 2)
-PAIRS = ((0, 1), (2, 3))
+AHEAD = (5, 4, 2)
+PAIRS = ((2, 3),)
 
 
 def tile_list_ckg_sig_kernel(
@@ -171,10 +171,10 @@ def tile_list_ckg_sig_kernel(
                 nc.sync.dma_start(n_raw[w][:, t, :], src.rearrange("(g t i) n -> t g i n", t=4, i=8)[t])
 
         held_sums = {}
-        spare = {("x", 0): ("tab_w",), ("x", 1, 0): ("tab_w", 4096), ("x", 5): ("tab2_sw",), ("y", 0): ("tab_w", 8192), ("y", 1): ("tab_w", 12288),
-                 ("x", 1, 1): ("wri_g", 1024), ("x", 2): ("wri_g", 3072), ("x", 6): ("wrr_raw",), ("y", 6): ("wrr_raw", 4096),
-                 ("arr", 2): ("wri_raw",), ("arr", 3): ("wri_raw", 2048), ("ab", 6): ("wri_g", -3072), ("ab", 3): ("wri_raw", 4096),
-                 ("x", 7): ("tab2_w",), ("y", 7): ("tab2_w", 4096), ("x", 4): ("tab2_w", 8192), ("y", 4): ("tab2_w", 12288),
+        spare = {("x", 0): ("tab_w",), ("x", 1): ("tab_w", 4096), ("x", 5): ("tab2_sw",), ("y", 0): ("tab_w", 8192), ("y", 1): ("tab_w", 12288),
+                 ("x", 4, 1): ("wri_raw", 2048), ("x", 2): ("wri_g", 3072), ("x", 6): ("wrr_raw",), ("y", 6): ("wrr_raw", 4096),
+                 ("arr", 2): ("wri_raw",), ("arr", 3): ("wri_g", 1024), ("ab", 6): ("wri_g", -3072), ("ab", 3): ("wri_raw", 4096),
+                 ("x", 7): ("tab2_w",), ("y", 7): ("tab2_w", 4096), ("x", 4, 0): ("tab2_w", 8192), ("y", 4): ("tab2_w", 12288),
                  "nr": ("ab6",), "pair0": ("ab6", 512), "ni": ("ab6", 1024), "pair1": ("ab6", 1536), "pair2": ("ab6", 2048)}
         ent, ab, rel, xs, ys, hs, hq, wr_g, wr_q, n_q = {}, {}, {}, {}, {}, {}, {}, {}, {}, {}
 
@@ -350,32 +350,32 @@ def tile_list_ckg_sig_kernel(
         for k, pair in enumerate(PAIRS):
             for place_in_pair, c in enumerate(pair):
                 hs[c] = pair_h[k][:, :, R * place_in_pair : R * (place_in_pair + 1)]
-        for c in (4, 5):
+        for c in (0, 1, 4, 5):
             hs[c] = sbuf([P, 2, R], BF16, "h%d" % c)[:]
 
         relation("r", 0)
         relation("r", 1)
         times_arr(0)
-        relation("r", 4)
         relation("r", 5)
+        relation("r", 4)
         entity_sums(3, 1, "Scalar")
         relation("r", 2)
         relation("r", 3)
         round_weight("i", nc.scalar, range(4))
-        times_arr_half(1, 0)
-        times_arr(4)
+        times_arr(1)
         entity_sums(6, 0, "Vector")
         times_arr(5)
+        times_arr_half(4, 0)
         quantise_weight("i")
         times_arr(2)
         relation("i", 0)
-        relation("i", 1)
+        relation("i", 4)
         entity_sums(6, 1, "Scalar")
         copy_held(3)
         times_arr(3)
-        times_arr_half(1, 1)
-        release("r1")
-        relation("i", 4)
+        times_arr_half(4, 1)
+        release("r4")
+        relation("i", 1)
         copy_held(6)
         relation("i", 5)
         round_candidates(0, 0)
@@ -384,13 +384,13 @@ def tile_list_ckg_sig_kernel(
         relation("i", 2)
         add_turned(0, 0)
         add_turned(0, 1)
-        times_ari(1)
+        times_ari(4)
         relation("i", 3)
         round_candidates(1, 0)
-        add_turned(1, 0)
-        add_turned(1, 1)
-        times_ari(4)
-        add_gpsimd(4)
+        add_turned(4, 0)
+        add_turned(4, 1)
+        times_ari(1)
+        add_gpsimd(1)
         relation("r", 6)
         round_candidates(1, 1)
         times_ari(2)
@@ -409,15 +409,20 @@ def tile_list_ckg_sig_kernel(
         entity_half(7, 0, ring="Vector")
         entity_half(7, 1, ring="Vector")
 
+        def quantised_pair(first):
+            name = "pair%d" % (first // 2)
+            codes, scales = sbuf([P, R], U32, name + "_c"), sbuf([P, R], U8, name + "_s", *spare[name])
+            for c in range(2):
+                for w in range(2):
+                    cols = slice(CH * (2 * w + c), CH * (2 * w + c + 1))
+                    quantise(codes[:, cols], scales[:, cols], hs[first + c][:, w])
+            return codes, scales
+
         n_q[0] = quantised("nr", n_g[:, 0].rearrange("p n t -> p (n t)"))
-        hq[0] = quantised("pair0", pair_h[0][:].rearrange("p w e -> p (w e)"))
+        hq[0] = quantised_pair(0)
         n_q[1] = quantised("ni", n_g[:, 1].rearrange("p n t -> p (n t)"))
-        hq[2] = sbuf([P, R], U32, "pair2_c"), sbuf([P, R], U8, "pair2_s", *spare["pair2"])
-        for c in (4, 5):
-            for w in range(2):
-                cols = slice(CH * (2 * w + c - 4), CH * (2 * w + c - 3))
-                quantise(hq[2][0][:, cols], hq[2][1][:, cols], hs[c][:, w])
-        hq[1] = quantised("pair1", pair_h[1][:].rearrange("p w e -> p (w e)"))
+        hq[2] = quantised_pair(4)
+        hq[1] = quantised("pair1", pair_h[0][:].rearrange("p w e -> p (w e)"))
         h6 = sbuf([P, 2 * R], BF16, "h6", over="h2")[:]
         hs[6] = h6.rearrange("p (w e) -> p w e", w=2)
         add_gpsimd(6)

@@ -172,10 +172,10 @@ def tile_list_ckg_sig_kernel(
 
         held_sums = {}
         spare = {("x", 0): ("tab_w",), ("x", 1): ("tab_w", 4096), ("x", 5): ("tab2_sw",), ("y", 0): ("tab_w", 8192), ("y", 1): ("tab_w", 12288),
-                 ("x", 4, 1): ("wri_raw", 2048), ("x", 2): ("wri_g", 3072), ("x", 6): ("wrr_raw",), ("y", 6): ("wrr_raw", 4096),
-                 ("arr", 2): ("wri_raw",), ("arr", 3): ("wri_g", 1024), ("ab", 6): ("wri_g", -3072), ("ab", 3): ("wri_raw", 4096),
+                 ("x", 4, 1): ("wri_raw", 2048), ("x", 2): ("wri_g", 4672), ("x", 6): ("wrr_raw",), ("y", 6): ("wrr_raw", 4096),
+                 ("arr", 2): ("wri_raw",), ("arr", 3): ("wri_g", 2624), ("ab6", 0): ("wri_g", -1984), ("ab6", 1): ("wri_g", 64), ("ab", 3): ("wri_raw", 4096),
                  ("x", 7): ("tab2_w",), ("y", 7): ("tab2_w", 4096), ("x", 4, 0): ("tab2_w", 8192), ("y", 4): ("tab2_w", 12288),
-                 "nr": ("ab6",), "pair0": ("ab6", 512), "ni": ("ab6", 1024), "pair1": ("ab6", 1536), "pair2": ("ab6", 2048)}
+                 "nr": ("ab6_1",), "pair0": ("ab6_1", 512), "ni": ("ab6_1", 1024), "pair1": ("ab6_1", 1536), "pair2": ("ab6_1", 2048)}
         ent, ab, rel, xs, ys, hs, hq, wr_g, wr_q, n_q = {}, {}, {}, {}, {}, {}, {}, {}, {}, {}
 
         def first_stage(dst, c, table, table_s, weight, weight_s, step, dtype, first, last):
@@ -215,7 +215,7 @@ def tile_list_ckg_sig_kernel(
             held_sums[c, w] = entity_pass(c, w, 0, False)
 
         def copy_held(c, copy=nc.scalar.copy):
-            ab[c] = sbuf([P, 2, CH, 4], F32, "ab%d" % c, *spare["ab", c])
+            ab[c] = sbuf([P, 2, CH, 4], F32, "ab%d" % c, *spare.get(("ab", c), ()))
             for w in range(2):
                 copy(ab[c][:, w], held_sums[c, w])
                 release("e%d_%d" % (c, w))
@@ -224,9 +224,9 @@ def tile_list_ckg_sig_kernel(
             for w in range(2):
                 entity_half(c, w, copy, begun)
 
-        def relation(part, c):
+        def relation(part, c, reader=None):
             codes, scales = wr_q[part]
-            reader = "Scalar" if part == "r" and c in TIMES_ON_GPSIMD else "Vector"
+            reader = reader or ("Scalar" if part == "r" and c in TIMES_ON_GPSIMD else "Vector")
             rel[part, c] = first_stage(
                 bank([P, R], "%s%d" % (part, c), reader), c, tab2_g[c],
                 plane2[:].bitcast(U8)[:, CH * c : CH * (c + 1)], codes[:], scales[:], P, FP8X4, True, True,
@@ -244,20 +244,20 @@ def tile_list_ckg_sig_kernel(
 
         def round_weight(part, engine, slots):
             if part not in wr_g:
-                place["free"] = place["free"] + 6 * R
-                wr_g[part] = sbuf([P, 4 * R], BF16, "wr%s_g" % part, room=14 * R)
+                place["free"] = place["free"] + 4 * R
+                wr_g[part] = sbuf([P, 5 * R], BF16, "wr%s_g" % part, room=18 * R)[:, 0 : 4 * R]
             for t in slots:
                 if engine is nc.gpsimd:
-                    dst = wr_g[part][:].rearrange("p (t g i j) -> p t g i j", g=16, i=8, j=4)[:, t]
+                    dst = wr_g[part].rearrange("p (t g i j) -> p t g i j", g=16, i=8, j=4)[:, t]
                     src = wr_raw[part][:].rearrange("p j (g t i) -> p t g i j", t=4, i=8)[:, t]
                     nc.gpsimd.tensor_scalar(dst, src, 1.0, 0.0, MULT, ADD)
                     continue
-                dst = wr_g[part][:].rearrange("p (t g u i j) -> p t g u j i", g=16, u=2, i=4, j=4)[:, t]
+                dst = wr_g[part].rearrange("p (t g u i j) -> p t g u j i", g=16, u=2, i=4, j=4)[:, t]
                 src = wr_raw[part][:].rearrange("p j (g t u i) -> p t g u j i", t=4, u=2, i=4)[:, t]
                 (nc.vector.tensor_copy if engine is nc.vector else nc.scalar.copy)(dst, src)
 
         def quantise_weight(part):
-            wr_q[part] = quantised("wr" + part, wr_g[part][:])
+            wr_q[part] = quantised("wr" + part, wr_g[part])
 
         def times_arr(c):
             x = sbuf([P, 2, CH, 4], F32, "x%d" % c, *spare.get(("x", c), ()))[:]
@@ -376,7 +376,10 @@ def tile_list_ckg_sig_kernel(
         times_arr_half(4, 1)
         release("r4")
         relation("i", 1)
-        copy_held(6)
+        parts6 = [sbuf([P, CH + 32 * w, 4], F32, "ab6_%d" % w, *spare["ab6", w])[:, 0:CH] for w in range(2)]
+        for w in range(2):
+            nc.scalar.copy(parts6[w], held_sums[6, w])
+            release("e6_%d" % w)
         relation("i", 5)
         round_candidates(0, 0)
         round_candidates(0, 1)
@@ -404,8 +407,14 @@ def tile_list_ckg_sig_kernel(
         relation("i", 7)
         add_turned(3, 0)
         add_turned(3, 1)
-        times_arr(6)
-        times_ari(6)
+        xs[6] = sbuf([P, 2, CH, 4], F32, "x6", *spare["x", 6])[:]
+        ys[6] = sbuf([P, 2, CH, 4], F32, "y6", *spare["y", 6])[:]
+        for w in range(2):
+            nc.vector.tensor_tensor(xs[6][:, w], parts6[w], rel["r", 6], MULT)
+        release("r6")
+        nc.vector.scalar_tensor_tensor(ys[6][:, 0], parts6[1], -1.0, rel["i", 6], MULT, MULT)
+        nc.vector.tensor_tensor(ys[6][:, 1], parts6[0], rel["i", 6], MULT)
+        release("i6")
         entity_half(7, 0, ring="Vector")
         entity_half(7, 1, ring="Vector")
 

@@ -170,12 +170,12 @@ def tile_list_ckg_sig_kernel(
             for t in range(4):
                 nc.sync.dma_start(n_raw[w][:, t, :], src.rearrange("(g t i) n -> t g i n", t=4, i=8)[t])
 
-        held_sums = {}
+        held_sums, rests = {}, {}
         spare = {("x", 0): ("tab_w",), ("x", 1): ("tab_w", 4096), ("x", 5): ("tab2_sw",), ("y", 0): ("tab_w", 8192), ("y", 1): ("tab_w", 12288),
                  ("x", 4, 1): ("wri_raw", 2048), ("x", 2): ("wri_g", 4672), ("x", 6): ("wrr_raw",), ("y", 6): ("wrr_raw", 4096),
-                 ("arr", 2): ("wri_raw",), ("arr", 3): ("wri_g", 2624), ("ab6", 0): ("wri_g", -1984), ("ab6", 1): ("wri_g", 64), ("ab", 3): ("wri_raw", 4096),
+                 ("arr", 2): ("wri_raw", 64), ("arr", 3): ("wri_g", 2624), ("ab6", 0): ("wri_g", -1984), ("ab6", 1): ("wri_g", 64), ("ab", 3): ("wri_raw", 4096),
                  ("x", 7): ("tab2_w",), ("y", 7): ("tab2_w", 4096), ("x", 4, 0): ("tab2_w", 8192), ("y", 4): ("tab2_w", 12288),
-                 "nr": ("ab6_1",), "pair0": ("ab6_1", 512), "ni": ("ab6_1", 1024), "pair1": ("ab6_1", 1536), "pair2": ("ab6_1", 2048)}
+                 "rest": ("wri_raw", -960), "nr": ("ab6_1",), "pair0": ("ab6_1", 512), "ni": ("ab6_1", 1024), "pair1": ("ab6_1", 1536), "pair2": ("ab6_1", 2048)}
         ent, ab, rel, xs, ys, hs, hq, wr_g, wr_q, n_q = {}, {}, {}, {}, {}, {}, {}, {}, {}, {}
 
         def first_stage(dst, c, table, table_s, weight, weight_s, step, dtype, first, last):
@@ -285,11 +285,13 @@ def tile_list_ckg_sig_kernel(
 
         def add_turned(c, w, pick=0):
             x, y = (z.rearrange("p j t -> p (j t)") for z in (xs[c, w], ys[c][:, w]))
+            blocks = {"x": [x[:, P * t : P * (t + 1)] for t in range(x.shape[1] // P)] + rests.get((c, w), []),
+                      "y": [y[:, P * t : P * (t + 1)] for t in range(4)]}
             dst = bank([P, 4, CH], "t%d_%d" % (c, w), pick=pick)
-            for k, term in enumerate((x, y) if c in TIMES_ON_GPSIMD else (y, x)):
+            for k, term in enumerate("xy" if c in TIMES_ON_GPSIMD else "yx"):
                 for t in range(4):
                     nc.tensor.matmul(
-                        dst[:, t, :], term[:, P * t : P * (t + 1)], ident[:], is_transpose=True,
+                        dst[:, t, :], blocks[term][t], ident[:], is_transpose=True,
                         start=((k, t) == (0, 0)), stop=((k, t) == (1, 3)),
                     )
             nc.scalar.copy(hs[c][:, w].rearrange("p (j t) -> p j t", t=4), dst[:].rearrange("p t j -> p j t"))
@@ -367,15 +369,26 @@ def tile_list_ckg_sig_kernel(
         times_arr(5)
         times_arr_half(4, 0)
         quantise_weight("i")
-        times_arr(2)
+        most = 3 * CH // 4
+        arr = sbuf([P, most, 4], F32, "arr2", *spare["arr", 2])[:]
+        nc.scalar.copy(arr, rel["r", 2][:, 0:most])
+        x = sbuf([P, 2, most, 4], F32, "x2", *spare["x", 2])[:]
+        nc.gpsimd.tensor_tensor(x, ab[2][:, :, 0:most], arr.unsqueeze(1).to_broadcast([P, 2, most, 4]), MULT)
+        xs[2, 0], xs[2, 1] = x[:, 0], x[:, 1]
+        rest = sbuf([P, 2, CH - most, 4], F32, "x2_rest", *spare["rest"])[:]
+        sums = rel["r", 2][:, most:CH].unsqueeze(1).to_broadcast([P, 2, CH - most, 4])
+        nc.vector.tensor_tensor(rest, ab[2][:, :, most:CH], sums, MULT)
+        release("r2")
+        for w in range(2):
+            rests[2, w] = [rest[:, w].rearrange("p j t -> p (j t)")]
         relation("i", 0)
-        relation("i", 4)
+        relation("i", 1)
         entity_sums(6, 1, "Scalar")
         copy_held(3)
         times_arr(3)
         times_arr_half(4, 1)
         release("r4")
-        relation("i", 1)
+        relation("i", 4)
         parts6 = [sbuf([P, CH + 32 * w, 4], F32, "ab6_%d" % w, *spare["ab6", w])[:, 0:CH] for w in range(2)]
         for w in range(2):
             nc.scalar.copy(parts6[w], held_sums[6, w])
@@ -387,13 +400,13 @@ def tile_list_ckg_sig_kernel(
         relation("i", 2)
         add_turned(0, 0)
         add_turned(0, 1)
-        times_ari(4)
-        relation("i", 3)
-        round_candidates(1, 0)
-        add_turned(4, 0)
-        add_turned(4, 1)
         times_ari(1)
         add_gpsimd(1)
+        relation("i", 3)
+        round_candidates(1, 0)
+        times_ari(4)
+        add_turned(4, 0)
+        add_turned(4, 1)
         relation("r", 6)
         round_candidates(1, 1)
         times_ari(2)

from contextlib import ExitStack

import concourse.mybir as mybir
from concourse.masks import make_identity

K, L, R, N, T, J = 1024, 512, 512, 512, 4096, 1024
FLOPS = 2 * J * (2 * K * R + 2 * L * R + 2 * R * N)

F32 = mybir.dt.float32
BF16 = mybir.dt.bfloat16
I32 = mybir.dt.int32
U32 = mybir.dt.uint32
U16 = mybir.dt.uint16
U8 = mybir.dt.uint8
FP8X4 = mybir.dt.float8_e4m3fn_x4
FP4X4 = mybir.dt.float4_e2m1fn_x4
MULT = mybir.AluOpType.mult
ADD = mybir.AluOpType.add
SIGMOID = mybir.ActivationFunctionType.Sigmoid

P = 128
CH = 128
LEAD = 256
ROW0, ROW1 = 96, 112
PASS_BYTES = J + 2 * R
TURNED = (0, 2, 3, 4)
TIMES_ON_GPSIMD = (0, 2, 3)
COVER = 1
AHEAD = (5, 4, 2)
PAIRS = ((2, 3),)


def tile_list_ckg_sig_kernel(
    tc, tab_words, tab_scales, tab2_words, tab2_scales, wer_words, wer_scales, wei_words, wei_scales,
    wrr, wri, nr, ni, offs, offs2, out
):
    nc = tc.nc
    with ExitStack() as ctx:
        lists = ctx.enter_context(tc.tile_pool(name="lists", bufs=1))
        ring = ctx.enter_context(tc.tile_pool(name="ring", bufs=9))
        lay = ctx.enter_context(tc.tile_pool(name="lay", bufs=1))
        psum = ctx.enter_context(tc.psum_pool(name="psum", bufs=1))

        width = {F32: 4, I32: 4, U32: 4, BF16: 2, U8: 1}
        place = {"free": 0}

        def sbuf(shape, dtype, name, over=None, shift=0, room=0):
            if over is None:
                size = width[dtype]
                for extent in shape[1:]:
                    size = size * extent
                place[name] = place["free"]
                place["free"] = place["free"] + -(-max(size, room) // 64) * 64
            else:
                place[name] = place[over] + shift
            return lay.tile(shape, dtype, name=name, align_bytes=64, offset=place[name])

        free_banks, held = {"Scalar": [0, 1, 2, 3], "Vector": [4, 5, 6, 7]}, {}

        def bank(shape, name, reader="Scalar", pick=0):
            held[name] = reader, free_banks[reader].pop(pick)
            return psum.tile(shape, F32, name=name, offset=2048 * held[name][1])

        def release(name):
            reader, number = held.pop(name)
            free_banks[reader].append(number)

        idx = lists.tile([P, J // 16], U16, name="idx")
        idx2 = lists.tile([P, J // 16], U16, name="idx2")
        tab_sw = sbuf([P, T // 4], I32, "tab_sw")
        tab2_sw = sbuf([P, T // 4], I32, "tab2_sw")
        tab_w = sbuf([P, T], I32, "tab_w")
        wer_raw = sbuf([P, 2, R // 2], I32, "wer_raw")
        w_sraw = sbuf([P, 2, R // 4], I32, "w_sraw")
        plane0 = sbuf([P, PASS_BYTES // 4], I32, "plane0")
        plane1 = sbuf([P, PASS_BYTES // 4], I32, "plane1")
        plane2 = sbuf([P, J // 4], I32, "plane2")
        joined = sbuf([P, PASS_BYTES // 4], I32, "joined")

        nc.sync.dma_start(idx[:], offs)
        nc.sync.dma_start(tab_sw[ROW0:P], tab_scales.bitcast(I32).rearrange("a q c -> (a q) c"))
        for w, src in enumerate((wer_scales, wei_scales)):
            nc.sync.dma_start(w_sraw[ROW0:P, w], src.bitcast(I32).rearrange("a q c -> (a q) c"))
        nc.sync.dma_start(idx2[:], offs2)
        nc.sync.dma_start(tab2_sw[ROW1:P], tab2_scales.bitcast(I32)[0])
        nc.sync.dma_start(tab_w[:], tab_words[0].rearrange("p t b -> p (t b)").bitcast(I32))
        nc.sync.dma_start(wer_raw[:], wer_words.bitcast(I32).rearrange("a p c -> p a c"))

        warm = sbuf([P, 2], F32, "warm")
        nc.vector.memset(warm[:, 0:1], 0.0)
        nc.scalar.activation(warm[:, 1:2], warm[:, 0:1], SIGMOID)
        nc.vector.memset(tab_sw[0:ROW0], 0)
        nc.gpsimd.memset(tab2_sw[0:ROW1], 0)
        nc.vector.memset(plane0[:], 0)
        nc.vector.memset(plane1[:], 0)
        nc.vector.memset(plane2[:], 0)
        ident = sbuf([P, P], F32, "ident")
        make_identity(nc, ident[:])

        nc.scalar.copy(
            joined[ROW0:P, J // 4 : PASS_BYTES // 4].bitcast(U32).rearrange("p (w t g e) -> p w t g e", w=2, t=4, e=2),
            w_sraw[ROW0:P].bitcast(U32).rearrange("p w (g t e) -> p w t g e", t=4, e=2),
        )
        tab_sg = sbuf([P, 11 * J], U8, "tab_sg", room=27 * J)[:, 0:J]
        nc.vector.tensor_copy(tab_sg, tab_sw[:].bitcast(U8).indirect(idx[:]))
        nc.vector.tensor_copy(joined[ROW0:P, 0 : J // 4], tab_sg[ROW0:P].bitcast(I32))

        def move_rows(plane, rows, first):
            for r in range(4):
                nc.sync.dma_start(plane[r:P:32, :], rows[first + r : first + 16 : 4, :])

        wei_raw = sbuf([P, 2, R // 2], I32, "wei_raw", over="tab_sg")
        wr_raw = {"r": sbuf([P, 4, R], F32, "wrr_raw", over="tab_sg", shift=2 * J)}
        tab2_w = sbuf([P, T], I32, "tab2_w", over="tab_sg", shift=11 * J - 64)
        wrr_rows = wrr.rearrange("(p j) c -> p j c", j=4)
        move_rows(plane0, joined, ROW0)
        nc.sync.dma_start(wei_raw[:], wei_words.bitcast(I32).rearrange("a p c -> p a c"))
        nc.sync.dma_start(wr_raw["r"][:, 0:COVER], wrr_rows[:, 0:COVER])
        move_rows(plane1, joined, ROW1)
        nc.sync.dma_start(wr_raw["r"][:, COVER:4], wrr_rows[:, COVER:4])
        nc.sync.dma_start(tab2_w[:], tab2_words[0].rearrange("p t b -> p (t b)").bitcast(I32))

        def gather_tab2_scales(half, over, shift, room):
            picked = sbuf([P, room], U8, "tab2_sg%d" % half, over, shift)[:, 0 : J // 2]
            nc.vector.tensor_copy(picked, tab2_sw[:].bitcast(U8).indirect(idx2[:, 32 * half : 32 * (half + 1)]))
            return picked

        tab2_sg = [gather_tab2_scales(0, "tab_sg", 10 * J, J // 2)]
        planes8 = [plane0[:].bitcast(U8), plane1[:].bitcast(U8)]

        w_p = []
        for w, raw in enumerate((wer_raw, wei_raw)):
            w_p.append(sbuf([P, 2, R // 2], I32, "w_p%d" % w))
            nc.scalar.copy(
                w_p[w][:].bitcast(U32).rearrange("p a (t g e) -> p a t g e", t=4, e=4),
                raw[:].bitcast(U32).rearrange("p a (g t e) -> p a t g e", t=4, e=4),
            )

        tab_p = {}

        def gather_tab(first, size, over, shift, room):
            words = sbuf([P, room], U32, "tab_g%d" % first, over, shift, room=32 * J)[:, 0:size]
            nc.vector.tensor_copy(words, tab_w[:].bitcast(U32).indirect(idx[:, first // 16 : (first + size) // 16]))
            return words

        def part_tab(words, first, parts):
            j0 = 0
            for part in parts:
                parted = sbuf([P, 2, 2 * part], U8, "tab_p%d" % (first + j0), room=8 * R if first + j0 == 5 * CH else 0)
                src = words[:, j0 : j0 + part].bitcast(U16).rearrange("p (j a) -> p a j", a=2)
                nc.vector.tensor_copy(parted[:].bitcast(U16), src)
                for c in range(part // CH):
                    tab_p[(first + j0) // CH + c] = parted[:, :, 2 * CH * c : 2 * CH * (c + 1)]
                j0 = j0 + part

        part_tab(gather_tab(0, LEAD, None, 0, J), 0, (CH, CH))
        rest = gather_tab(LEAD, J - LEAD, "tab_g0", 0, J - LEAD)
        tab2_sg.append(gather_tab2_scales(1, "tab_g0", 3 * J, 21 * J + 64))
        part_tab(rest, LEAD, (2 * CH, CH, CH, CH, CH))
        joined2 = sbuf([P, J // 4], I32, "joined2")
        for half in range(2):
            cols = slice(half * J // 8, (half + 1) * J // 8)
            nc.vector.tensor_copy(joined2[ROW0:P, cols], tab2_sg[half][ROW0:P].bitcast(I32))
        move_rows(plane2, joined2, ROW1)
        wr_raw["i"] = sbuf([P, 4, R], F32, "wri_raw", over="tab_g0", shift=8 * J)
        nc.sync.dma_start(wr_raw["i"][:], wri.rearrange("(p j) c -> p j c", j=4))

        n_raw = [sbuf([P, 4, N], F32, "n_raw%d" % w, over="tab_g0", shift=16 * J + 8 * J * w) for w in range(2)]
        for w, src in enumerate((nr, ni)):
            for t in range(4):
                nc.sync.dma_start(n_raw[w][:, t, :], src.rearrange("(g t i) n -> t g i n", t=4, i=8)[t])

        held_sums, rests = {}, {}
        spare = {("x", 0): ("tab_w",), ("x", 1): ("tab_w", 4096), ("x", 5): ("tab2_sw",), ("y", 0): ("tab_w", 8192), ("y", 1): ("tab_w", 12288),
                 ("x", 4, 1): ("wri_raw", 2048), ("x", 2): ("wri_g", 4672), ("x", 6): ("wrr_raw",), ("y", 6): ("wrr_raw", 4096),
                 ("arr", 2): ("wri_raw", 64), ("arr", 3): ("wri_g", 2624), ("ab6", 0): ("wri_g", -1984), ("ab6", 1): ("wri_g", 64), ("ab", 3): ("wri_raw", 4096),
                 ("x", 7): ("tab2_w",), ("y", 7): ("tab2_w", 4096), ("x", 4, 0): ("tab2_w", 8192), ("y", 4): ("tab2_w", 12288),
                 "rest": ("wri_raw", -960), "nr": ("ab6_1",), "pair0": ("ab6_1", 512), "ni": ("ab6_1", 1024), "pair1": ("ab6_1", 1536), "pair2": ("ab6_1", 2048)}
        ent, ab, rel, xs, ys, hs, hq, wr_g, wr_q, n_q = {}, {}, {}, {}, {}, {}, {}, {}, {}, {}

        def first_stage(dst, c, table, table_s, weight, weight_s, step, dtype, first, last):
            if c in TURNED:
                nc.tensor.matmul_mx(
                    out=dst[:], lhsT=table.bitcast(dtype), lhsT_scale=table_s, rhs=weight.bitcast(dtype), rhs_scale=weight_s,
                    start=first, stop=last,
                )
                return dst[:].rearrange("p (j t) -> p j t", t=4)
            for t in range(4):
                nc.tensor.matmul_mx(
                    out=dst[:, CH * t : CH * (t + 1)],
                    lhsT=weight[:, step * t : step * (t + 1)].bitcast(dtype), lhsT_scale=weight_s[:, P * t : P * (t + 1)],
                    rhs=table.bitcast(dtype), rhs_scale=table_s,
                    start=(first and t == 0), stop=(last and t == 3),
                )
            return dst[:].rearrange("p (t j) -> p j t", t=4)

        def entity_pass(c, w, a, first, ring="Scalar", pick=0):
            if first:
                ent[c, w] = bank([P, R], "e%d_%d" % (c, w), ring, pick)
            return first_stage(
                ent[c, w], c, tab_p[c][:, a, :], planes8[a][:, CH * c : CH * (c + 1)],
                w_p[w][:, a, :].bitcast(U8), planes8[a][:, J + R * w : J + R * (w + 1)], 2 * P, FP4X4, first, not first,
            )

        def entity_half(c, w, copy=nc.scalar.copy, begun=False, ring="Scalar"):
            if w == 0:
                ab[c] = sbuf([P, 2, CH, 4], F32, "ab%d" % c, *spare.get(("ab", c), ()))
            if not begun:
                entity_pass(c, w, 1, True, ring)
            copy(ab[c][:, w], entity_pass(c, w, int(begun), False))
            release("e%d_%d" % (c, w))

        def entity_sums(c, w, ring, pick=-1):
            entity_pass(c, w, 1, True, ring, pick)
            held_sums[c, w] = entity_pass(c, w, 0, False)

        def copy_held(c, copy=nc.scalar.copy):
            ab[c] = sbuf([P, 2, CH, 4], F32, "ab%d" % c, *spare.get(("ab", c), ()))
            for w in range(2):
                copy(ab[c][:, w], held_sums[c, w])
                release("e%d_%d" % (c, w))

        def entity(c, copy=nc.scalar.copy, begun=False):
            for w in range(2):
                entity_half(c, w, copy, begun)

        def relation(part, c, reader=None):
            codes, scales = wr_q[part]
            reader = reader or ("Scalar" if part == "r" and c in TIMES_ON_GPSIMD else "Vector")
            rel[part, c] = first_stage(
                bank([P, R], "%s%d" % (part, c), reader), c, tab2_g[c],
                plane2[:].bitcast(U8)[:, CH * c : CH * (c + 1)], codes[:], scales[:], P, FP8X4, True, True,
            )

        def quantise(codes, scales, rounded):
            nc.vector.quantize_mx(out=codes.bitcast(FP8X4), scales=scales, in_=rounded)

        def quantised(name, rounded):
            words = rounded.shape[1] // 4
            codes = sbuf([P, words], U32, name + "_c")
            scales = sbuf([P, words], U8, name + "_s", *spare.get(name, ()))
            quantise(codes[:], scales[:], rounded)
            return codes, scales

        def round_weight(part, engine, slots):
            if part not in wr_g:
                place["free"] = place["free"] + 4 * R
                wr_g[part] = sbuf([P, 5 * R], BF16, "wr%s_g" % part, room=18 * R)[:, 0 : 4 * R]
            for t in slots:
                if engine is nc.gpsimd:
                    dst = wr_g[part].rearrange("p (t g i j) -> p t g i j", g=16, i=8, j=4)[:, t]
                    src = wr_raw[part][:].rearrange("p j (g t i) -> p t g i j", t=4, i=8)[:, t]
                    nc.gpsimd.tensor_scalar(dst, src, 1.0, 0.0, MULT, ADD)
                    continue
                dst = wr_g[part].rearrange("p (t g u i j) -> p t g u j i", g=16, u=2, i=4, j=4)[:, t]
                src = wr_raw[part][:].rearrange("p j (g t u i) -> p t g u j i", t=4, u=2, i=4)[:, t]
                (nc.vector.tensor_copy if engine is nc.vector else nc.scalar.copy)(dst, src)

        def quantise_weight(part):
            wr_q[part] = quantised("wr" + part, wr_g[part])

        def times_arr(c):
            x = sbuf([P, 2, CH, 4], F32, "x%d" % c, *spare.get(("x", c), ()))[:]
            engine, arr = nc.vector, rel["r", c]
            if c in TIMES_ON_GPSIMD:
                engine, arr = nc.gpsimd, sbuf([P, CH, 4], F32, "arr%d" % c, *spare.get(("arr", c), ()))[:]
                nc.scalar.copy(arr, rel["r", c])
            engine.tensor_tensor(x, ab[c][:], arr.unsqueeze(1).to_broadcast([P, 2, CH, 4]), MULT)
            xs[c], xs[c, 0], xs[c, 1] = x, x[:, 0], x[:, 1]
            release("r%d" % c)

        def times_arr_half(c, w):
            xs[c, w] = sbuf([P, CH, 4], F32, "x%d_%d" % (c, w), *spare["x", c, w])[:]
            nc.vector.tensor_tensor(xs[c, w], ab[c][:, w], rel["r", c], MULT)

        def times_ari(c):
            ys[c] = sbuf([P, 2, CH, 4], F32, "y%d" % c, *spare.get(("y", c), ()))[:]
            nc.vector.scalar_tensor_tensor(ys[c][:, 0], ab[c][:, 1], -1.0, rel["i", c], MULT, MULT)
            nc.vector.tensor_tensor(ys[c][:, 1], ab[c][:, 0], rel["i", c], MULT)
            release("i%d" % c)

        def add_gpsimd(c):
            x, y = (z[c].rearrange("p w j t -> p w (j t)") for z in (xs, ys))
            nc.gpsimd.tensor_tensor(hs[c], x, y, ADD)

        def add_turned(c, w, pick=0):
            x, y = (z.rearrange("p j t -> p (j t)") for z in (xs[c, w], ys[c][:, w]))
            blocks = {"x": [x[:, P * t : P * (t + 1)] for t in range(x.shape[1] // P)] + rests.get((c, w), []),
                      "y": [y[:, P * t : P * (t + 1)] for t in range(4)]}
            dst = bank([P, 4, CH], "t%d_%d" % (c, w), pick=pick)
            for k, term in enumerate("xy" if c in TIMES_ON_GPSIMD else "yx"):
                for t in range(4):
                    nc.tensor.matmul(
                        dst[:, t, :], blocks[term][t], ident[:], is_transpose=True,
                        start=((k, t) == (0, 0)), stop=((k, t) == (1, 3)),
                    )
            nc.scalar.copy(hs[c][:, w].rearrange("p (j t) -> p j t", t=4), dst[:].rearrange("p t j -> p j t"))
            release("t%d_%d" % (c, w))

        def round_candidates(w, half):
            n0 = 2 * P * half
            nc.scalar.copy(
                n_g[:, w, n0 : n0 + 2 * P].rearrange("p (c i) t -> p c t i", i=4),
                n_raw[w][:, :, n0 : n0 + 2 * P].rearrange("p t (c i) -> p c t i", i=4),
            )

        def score_pass(dst, m, w, codes, scales, start, stop):
            cols = slice(P * m, P * (m + 1))
            nc.tensor.matmul_mx(
                out=dst, lhsT=n_q[w][0][:, cols].bitcast(FP8X4), lhsT_scale=n_q[w][1][:, cols],
                rhs=codes.bitcast(FP8X4), rhs_scale=scales, start=start, stop=stop,
            )

        def finish(sums, first, count, m0, rows):
            res = ring.tile([P, rows, count], F32, name="res")
            nc.scalar.activation(res[:], sums[:], SIGMOID)
            dst = out[P * m0 : P * (m0 + rows), first : first + count]
            nc.sync.dma_start(dst.rearrange("(m p) j -> p m j", p=P), res[:])

        def score(codes, scales, first, count):
            rows = R // count
            for m0 in range(0, 4, rows):
                sums = bank([P, rows, count], "s%d_%d" % (first, m0))
                for w in range(2):
                    for m in range(rows):
                        cols = slice(count * w, count * (w + 1))
                        start, stop = (w, m) == (0, 0), (w, m) == (1, rows - 1)
                        score_pass(sums[:, m, :], m0 + m, w, codes[:, cols], scales[:, cols], start, stop)
                finish(sums, first, count, m0, rows)
                release("s%d_%d" % (first, m0))

        for w in range(2):
            for c in range(2):
                entity_pass(c, w, 0, True)
        for c in range(2):
            entity(c, begun=True)
        round_weight("r", nc.vector, range(4))
        quantise_weight("r")
        for c in AHEAD:
            entity(c)
        entity_sums(3, 0, "Scalar", 0)
        tab2_g = {}
        tab2_words_g = sbuf([P, J], U32, "tab2_g", over="tab_p640")
        for first, size in ((0, LEAD), (LEAD, J - LEAD)):
            words = tab2_words_g[:, first : first + size]
            nc.vector.tensor_copy(words, tab2_w[:].bitcast(U32).indirect(idx2[:, first // 16 : (first + size) // 16]))
            for c in range(size // CH):
                tab2_g[first // CH + c] = words[:, CH * c : CH * (c + 1)]

        n_g = sbuf([P, 2, N, 4], BF16, "n_g")
        pair_h = [sbuf([P, 2, 2 * R], BF16, "h%d" % pair[0], *spare.get(("h", pair[0]), ())) for pair in PAIRS]
        for k, pair in enumerate(PAIRS):
            for place_in_pair, c in enumerate(pair):
                hs[c] = pair_h[k][:, :, R * place_in_pair : R * (place_in_pair + 1)]
        for c in (0, 1, 4, 5):
            hs[c] = sbuf([P, 2, R], BF16, "h%d" % c)[:]

        relation("r", 0)
        relation("r", 1)
        times_arr(0)
        relation("r", 5)
        relation("r", 4)
        entity_sums(3, 1, "Scalar")
        relation("r", 2)
        relation("r", 3)
        round_weight("i", nc.scalar, range(4))
        times_arr(1)
        entity_sums(6, 0, "Vector")
        times_arr(5)
        times_arr_half(4, 0)
        quantise_weight("i")
        most = 3 * CH // 4
        arr = sbuf([P, most, 4], F32, "arr2", *spare["arr", 2])[:]
        nc.scalar.copy(arr, rel["r", 2][:, 0:most])
        x = sbuf([P, 2, most, 4], F32, "x2", *spare["x", 2])[:]
        nc.gpsimd.tensor_tensor(x, ab[2][:, :, 0:most], arr.unsqueeze(1).to_broadcast([P, 2, most, 4]), MULT)
        xs[2, 0], xs[2, 1] = x[:, 0], x[:, 1]
        rest = sbuf([P, 2, CH - most, 4], F32, "x2_rest", *spare["rest"])[:]
        sums = rel["r", 2][:, most:CH].unsqueeze(1).to_broadcast([P, 2, CH - most, 4])
        nc.vector.tensor_tensor(rest, ab[2][:, :, most:CH], sums, MULT)
        release("r2")
        for w in range(2):
            rests[2, w] = [rest[:, w].rearrange("p j t -> p (j t)")]
        relation("i", 0)
        relation("i", 1)
        entity_sums(6, 1, "Scalar")
        copy_held(3)
        times_arr(3)
        times_arr_half(4, 1)
        release("r4")
        relation("i", 4)
        parts6 = [sbuf([P, CH + 32 * w, 4], F32, "ab6_%d" % w, *spare["ab6", w])[:, 0:CH] for w in range(2)]
        for w in range(2):
            nc.scalar.copy(parts6[w], held_sums[6, w])
            release("e6_%d" % w)
        relation("i", 5)
        round_candidates(0, 0)
        round_candidates(0, 1)
        times_ari(0)
        relation("i", 2)
        add_turned(0, 0)
        add_turned(0, 1)
        times_ari(1)
        add_gpsimd(1)
        relation("i", 3)
        round_candidates(1, 0)
        times_ari(4)
        add_turned(4, 0)
        add_turned(4, 1)
        relation("r", 6)
        round_candidates(1, 1)
        times_ari(2)
        relation("i", 6)
        add_turned(2, 0)
        add_turned(2, 1)
        times_ari(5)
        add_gpsimd(5)
        relation("r", 7)
        times_ari(3)
        relation("i", 7)
        add_turned(3, 0)
        add_turned(3, 1)
        xs[6] = sbuf([P, 2, CH, 4], F32, "x6", *spare["x", 6])[:]
        ys[6] = sbuf([P, 2, CH, 4], F32, "y6", *spare["y", 6])[:]
        for w in range(2):
            nc.vector.tensor_tensor(xs[6][:, w], parts6[w], rel["r", 6], MULT)
        release("r6")
        nc.vector.scalar_tensor_tensor(ys[6][:, 0], parts6[1], -1.0, rel["i", 6], MULT, MULT)
        nc.vector.tensor_tensor(ys[6][:, 1], parts6[0], rel["i", 6], MULT)
        release("i6")
        entity_half(7, 0, ring="Vector")
        entity_half(7, 1, ring="Vector")

        def quantised_pair(first):
            name = "pair%d" % (first // 2)
            codes, scales = sbuf([P, R], U32, name + "_c"), sbuf([P, R], U8, name + "_s", *spare[name])
            for c in range(2):
                for w in range(2):
                    cols = slice(CH * (2 * w + c), CH * (2 * w + c + 1))
                    quantise(codes[:, cols], scales[:, cols], hs[first + c][:, w])
            return codes, scales

        n_q[0] = quantised("nr", n_g[:, 0].rearrange("p n t -> p (n t)"))
        hq[0] = quantised_pair(0)
        n_q[1] = quantised("ni", n_g[:, 1].rearrange("p n t -> p (n t)"))
        hq[2] = quantised_pair(4)
        hq[1] = quantised("pair1", pair_h[0][:].rearrange("p w e -> p (w e)"))
        h6 = sbuf([P, 2 * R], BF16, "h6", over="h2")[:]
        hs[6] = h6.rearrange("p (w e) -> p w e", w=2)
        add_gpsimd(6)
        times_arr(7)
        times_ari(7)
        for k in (0, 2, 1):
            score(*hq[k], 2 * CH * k, 2 * CH)
        codes, scales = quantised("h6", h6)
        score(codes, scales, CH * 6, CH)
        halves = [sbuf([P, CH, 4], BF16, "h7_%d" % w) for w in range(2)]
        for w in range(2):
            nc.vector.tensor_tensor(halves[w][:], xs[7][:, w], ys[7][:, w], ADD)
        sums = [bank([P, 2, CH], "last%d" % half, "Vector") for half in range(2)]
        for w in range(2):
            codes, scales = quantised("last%d" % w, halves[w][:].rearrange("p j t -> p (j t)"))
            for m in range(4):
                start, stop = (w, m % 2) == (0, 0), (w, m % 2) == (1, 1)
                score_pass(sums[m // 2][:, m % 2, :], m, w, codes[:], scales[:], start, stop)
        for half in range(2):
            finish(sums[half], CH * 7, CH, 2 * half, 2)
